import numpy as np
import ml_dtypes


def mxq(x, axis, fmt="e4m3"):
    dtype, down = {"e4m3": (ml_dtypes.float8_e4m3fn, 7), "e5m2": (ml_dtypes.float8_e5m2, 14)}[fmt]
    v = np.moveaxis(np.asarray(x, np.float32).astype(ml_dtypes.bfloat16).astype(np.float64), axis, -1)
    blocks = v.reshape(v.shape[:-1] + (-1, 32))
    amax = np.abs(blocks).max(-1, keepdims=True)
    byte = np.maximum(np.where(amax > 0, np.frexp(amax)[1] - 1 + 127, 0) - down, 1)
    scale = np.exp2(byte - 127.0)
    codes = (blocks / scale).astype(np.float32).astype(dtype).astype(np.float64)
    return np.moveaxis((codes * scale).reshape(v.shape), -1, axis)


WIDE = False


def mx_kscale(k):
    if not WIDE:
        return np.ones(k)
    levels = np.array([10, -10, 5, -5, 0])
    if k % 512:
        return np.exp2(np.random.permutation(np.resize(levels, k // 32))).repeat(32)
    a = np.empty((k // 512, 16))
    for p in range(k // 512):
        a[p, :8] = np.random.permutation(np.resize(levels, 8))
        for g in range(8):
            far = levels[np.abs(levels - a[p, g]) >= 10]
            a[p, g + 8] = far[np.random.randint(len(far))]
    return np.exp2(a.ravel()).repeat(32)


def f64(x):
    return np.asarray(x).astype(np.float64)


def striped(idx):
    return np.tile(idx.reshape(-1, 16).T, (8, 1)).astype(np.uint16)


def unstriped(offs):
    return offs[:16].T.reshape(-1).astype(np.int64)


def striped8(idx):
    return np.concatenate([x.reshape(-1, 16).T for x in idx]).astype(np.uint16)


def runs(offs, k):
    lists = np.stack([offs[16 * r : 16 * r + 16].T.reshape(-1) for r in range(8)]).astype(np.int64)
    return lists[np.arange(k) % 512 // 64]


def pack_weight(w):
    k, n = w.shape
    w = f64(np.asarray(w, np.float32).astype(ml_dtypes.bfloat16)).reshape(k // 32, 32, n)
    amax = np.abs(w).max(1)
    byte = np.clip(np.where(amax > 0, np.frexp(amax)[1] - 1 + 127 - 7, 1), 1, 254)
    scaled = (w * np.exp2(127.0 - byte)[:, None, :]).reshape(k, n).astype(np.float32)
    words = np.ascontiguousarray(scaled.reshape(k // 512, 128, 4, n).transpose(0, 1, 3, 2)).astype(ml_dtypes.float8_e4m3fn).view(np.uint8)
    return words, np.ascontiguousarray(byte.astype(np.uint8).reshape(k // 512, 16, n))


def unpack_weight(words, scales):
    g, p, n, _ = words.shape
    vals = np.ascontiguousarray(words).view(ml_dtypes.float8_e4m3fn).astype(np.float64) * np.repeat(np.exp2(scales.astype(np.float64) - 127.0), 8, axis=1)[..., None]
    return vals.transpose(0, 1, 3, 2).reshape(g * 512, n)


E2M1 = np.array([0.0, 0.5, 1.0, 1.5, 2.0, 3.0, 4.0, 6.0, -0.0, -0.5, -1.0, -1.5, -2.0, -3.0, -4.0, -6.0])


def pack_fp4(w):
    k, n = w.shape
    w = f64(np.asarray(w, np.float32).astype(ml_dtypes.bfloat16)).reshape(k // 32, 32, n)
    amax = np.abs(w).max(1)
    mant, ex = np.frexp(amax / 6.0)
    byte = np.clip(np.where(amax > 0, np.where(mant > 0.5, ex, ex - 1) + 127, 1), 1, 254)
    scaled = (w * np.exp2(127.0 - byte)[:, None, :]).reshape(k, n).astype(np.float32)
    c = np.ascontiguousarray(scaled.reshape(k // 512, 128, 4, n).transpose(0, 1, 3, 2)).astype(ml_dtypes.float4_e2m1fn).view(np.uint8) & 0xF
    words = (c[..., 0::2] | (c[..., 1::2] << 4)).reshape(k // 512, 128, 2 * n)
    return np.ascontiguousarray(words), np.ascontiguousarray(byte.astype(np.uint8).reshape(k // 512, 16, n))


def unpack_fp4(words, scales):
    g, _, n = scales.shape
    words = np.ascontiguousarray(words).reshape(g, 128, n, 2)
    nib = np.empty((g, 128, n, 4), np.uint8)
    nib[..., 0::2] = words & 0xF
    nib[..., 1::2] = words >> 4
    vals = E2M1[nib] * np.repeat(np.exp2(scales.astype(np.float64) - 127.0), 8, axis=1)[..., None]
    return vals.transpose(0, 1, 3, 2).reshape(g * 512, n)


def relu(v):
    return np.maximum(v, 0.0)

def planes(y):
    n, m = y.shape
    v = y.astype(np.float32).astype(ml_dtypes.bfloat16).astype(np.float64).reshape(n // 32, 32, m)
    top = np.abs(v).max(1)
    byte = np.clip(np.where(top > 0, np.frexp(top)[1] - 1 + 127 - 7, 1), 1, 254)
    codes = (v * np.exp2(127.0 - byte)[:, None, :]).reshape(n, m).astype(np.float32).astype(ml_dtypes.float8_e4m3fn).view(np.uint8)
    words = codes.reshape(n // 512, 128, 4, m).transpose(0, 1, 3, 2)
    return np.ascontiguousarray(words), np.ascontiguousarray(byte.astype(np.uint8).reshape(n // 512, 16, m))


K, T, S, N, H = 1024, 2048, 512, 512, 512


def setup_inputs():
    n = np.random.standard_normal
    s = mx_kscale(K)[:, None]
    u = mx_kscale(H)
    packed_xT = pack_weight(n((K, T)) * s)
    packed_w1 = pack_fp4(n((K, H)) / np.sqrt(K) / s)
    packed_w2 = pack_fp4(n((H, N)) / np.sqrt(H) / u[:, None])
    return {
        "x_words": packed_xT[0],
        "x_scales": packed_xT[1],
        "w1_words": packed_w1[0],
        "w1_scales": packed_w1[1],
        "gn": (np.random.uniform(0.5, 1.5, (H, 1)) * u[:, None]).astype(np.float32),
        "w2_words": packed_w2[0],
        "w2_scales": packed_w2[1],
        "offs": striped(np.random.permutation(T)[:S]),
        "p1": striped8(np.stack([np.random.permutation(S) for _ in range(8)])),
        "p2": striped8(np.stack([np.random.permutation(S) for _ in range(8)])),
    }


def reference(x_words, x_scales, w1_words, w1_scales, gn, w2_words, w2_scales, offs, p1, p2):
    xq = unpack_weight(x_words, x_scales)[:, unstriped(offs)]
    y = relu(unpack_fp4(w1_words, w1_scales).T @ xq)
    q = (y) ** 2
    z = f64(gn) * (y / (np.sqrt(0.5 * (q + q[np.arange(H)[:, None], runs(p1, H)] + q[np.arange(H)[:, None], runs(p2, H)]) + 1)))
    out_0 = unpack_fp4(w2_words, w2_scales).T @ mxq(z, 0, "e4m3")
    return (out_0,) + planes(out_0)

@@ -1,0 +1,249 @@
+from contextlib import ExitStack
+
+import concourse.mybir as mybir
+from concourse.masks import make_identity
+
+K, T, S, N, H = 1024, 2048, 512, 512, 512
+FLOPS = 2 * K * H * S + 2 * H * N * S
+
+F32 = mybir.dt.float32
+BF16 = mybir.dt.bfloat16
+I32 = mybir.dt.int32
+U32 = mybir.dt.uint32
+U16 = mybir.dt.uint16
+U8 = mybir.dt.uint8
+FP8X4 = mybir.dt.float8_e4m3fn_x4
+FP4X4 = mybir.dt.float4_e2m1fn_x4
+ACT = mybir.ActivationFunctionType
+ALU = mybir.AluOpType
+
+P = 128
+PACK = 4
+PASSES = K // 512
+CHUNKS = [256,256]
+PIECES = [256,128]
+PE_SUM = False
+G_ON_VECTOR = [1]
+O_ON_VECTOR = [3]
+
+
+def deal_words(nc, dealt, raw):
+    nc.vector.tensor_copy(
+        out=dealt[:].rearrange("p (t c m b) -> p c t m b", t=PACK, m=8, b=2),
+        in_=raw[:].rearrange("p (c m t b) -> p c t m b", t=PACK, m=8, b=2),
+    )
+
+
+def deal_scales(nc, dealt, raw):
+    nc.vector.tensor_copy(
+        out=dealt[:].rearrange("p (t c m) -> p c t m", t=PACK, m=16),
+        in_=raw[:].rearrange("p (c m t) -> p c t m", t=PACK, m=16),
+    )
+
+
+def tile_picked_lrn8_relu_po_kernel(tc, x_words, x_scales, w1_words, w1_scales, gn, w2_words, w2_scales, offs, p1, p2, out_0, out_1, out_2):
+    nc = tc.nc
+    with ExitStack() as ctx:
+        keep = ctx.enter_context(tc.tile_pool(name="keep", bufs=1))
+        psum = ctx.enter_context(tc.psum_pool(name="psum", bufs=8))
+
+        offs_sb = keep.tile([P, S // 16], U16, name="offs_sb")
+        p1_sb = keep.tile([P, S // 16], U16, name="p1_sb")
+        p2_sb = keep.tile([P, S // 16], U16, name="p2_sb")
+
+        xs_raw = keep.tile([P, T], U8, name="xs_raw", align_bytes=64)
+        xs_got = keep.tile([P, S], U8, name="xs_got", tag="small", align_bytes=64)
+        xs_moved = keep.tile([P, PASSES * S], U8, name="xs_moved", align_bytes=64)
+        w1s_raw = keep.tile([P, PASSES * H], U8, name="w1s_raw", tag="late", align_bytes=64)
+        w1w_raw = keep.tile([P, PASSES * 2 * H], U8, name="w1w_raw", tag="words", align_bytes=64)
+        w1s = keep.tile([P, PASSES * H], U8, name="w1s", align_bytes=64)
+        w2s = keep.tile([P, N], U8, name="w2s", align_bytes=64)
+        w1w = keep.tile([P, PASSES * 2 * H], U8, name="w1w", align_bytes=64)
+        w2w = keep.tile([P, 2 * N], U8, name="w2w", align_bytes=64)
+        xw_raw = [keep.tile([P, T], U32, name=f"xw_raw{z}", align_bytes=64) for z in range(PASSES)]
+        xw = [keep.tile([P, S], U32, name=f"xw{z}", align_bytes=64) for z in range(PASSES)]
+        ones = keep.tile([P, 1], F32, name="ones")
+        bias = keep.tile([P, 1], F32, name="bias")
+
+        nc.vector.memset(xs_raw[32:64, :].bitcast(I32), 0)
+        nc.vector.memset(xs_raw[64:128, :].bitcast(I32), 0)
+        nc.gpsimd.memset(w1s_raw[:].bitcast(I32), 0)
+        nc.vector.memset(ones[:], 1.0)
+        nc.vector.memset(xs_moved[:].bitcast(I32), 0)
+        nc.scalar.activation(bias[:], ones[:], ACT.Abs_reciprocal_sqrt)
+
+        nc.sync.dma_start(offs_sb[:], offs)
+        nc.sync.dma_start(xs_raw[0:32, :].bitcast(I32), x_scales.bitcast(I32).rearrange("z r c -> r z c"))
+        nc.sync.dma_start(
+            w1w_raw[:].bitcast(I32).rearrange("p (z c) -> p z c", z=PASSES),
+            w1_words.bitcast(I32).rearrange("z p c -> p z c"),
+        )
+        nc.sync.dma_start(p1_sb[:], p1)
+        nc.sync.dma_start(p2_sb[:], p2)
+        for z in range(PASSES):
+            nc.sync.dma_start(xw_raw[z][:].bitcast(I32), x_words[z].rearrange("p n t -> p (n t)").bitcast(I32))
+        for q in range(4):
+            queue = nc.gpsimd if q < 2 else nc.scalar
+            queue.dma_start(
+                w1s_raw[32 * q : 32 * q + 4, :].bitcast(I32).rearrange("r (z c) -> r z c", z=PASSES),
+                w1_scales[:, 4 * q : 4 * q + 4, :].bitcast(I32).rearrange("z r c -> r z c"),
+            )
+        if PE_SUM:
+            ident = keep.tile([P, P], F32, name="ident")
+            make_identity(nc, ident[:])
+
+        nc.vector.tensor_copy(xs_got[:], xs_raw[:].indirect(offs_sb[:]))
+        for q in range(4):
+            nc.scalar.dma_start(
+                xs_moved[32 * q : 32 * q + 4, :].bitcast(I32).rearrange("r (z c) -> r z c", z=PASSES),
+                xs_got[8 * q : 8 * q + 8, :].bitcast(I32),
+            )
+        deal_words(nc, w1w, w1w_raw)
+        nc.vector.tensor_copy(xw[0][:], xw_raw[0][:].indirect(offs_sb[:]))
+        deal_scales(nc, w1s, w1s_raw)
+        gn_sb = keep.tile([P, PACK], F32, name="gn_sb", tag="late", align_bytes=64)
+        nc.sync.dma_start(gn_sb[:], gn.rearrange("(p t) o -> p (t o)", t=PACK))
+        nc.vector.tensor_copy(xw[1][:], xw_raw[1][:].indirect(offs_sb[:]))
+        w2w_raw = keep.tile([P, 2 * N], U8, name="w2w_raw", tag="words", align_bytes=64)
+        nc.sync.dma_start(w2w_raw[:].bitcast(I32), w2_words[0].bitcast(I32))
+        w2s_raw = keep.tile([P, N], U8, name="w2s_raw", tag="small", align_bytes=64)
+        nc.gpsimd.memset(w2s_raw[:].bitcast(I32), 0)
+        for q in range(4):
+            nc.sync.dma_start(w2s_raw[32 * q : 32 * q + 4, :].bitcast(I32), w2_scales[0, 4 * q : 4 * q + 4, :].bitcast(I32))
+        deal_words(nc, w2w, w2w_raw)
+        deal_scales(nc, w2s, w2s_raw)
+
+        acc = [psum.tile([P, S], F32, name=f"acc{t}", tag="bank") for t in range(PACK)]
+        for t in range(PACK):
+            for z in range(PASSES):
+                col = (t * PASSES + z) * P
+                nc.tensor.matmul_mx(
+                    out=acc[t][:],
+                    lhsT=w1w[:, 2 * col : 2 * col + 2 * P].bitcast(FP4X4),
+                    lhsT_scale=w1s[:, col : col + P],
+                    rhs=xw[z][:].bitcast(FP8X4),
+                    rhs_scale=xs_moved[:, z * S : (z + 1) * S],
+                    start=(z == 0),
+                    stop=(z == PASSES - 1),
+                )
+
+        y = [keep.tile([P, S], F32, name=f"y{t}") for t in range(PACK)]
+        sq = [keep.tile([P, S], F32, name=f"sq{t}") for t in range(PACK)]
+        own = [keep.tile([P, S], F32, name=f"own{t}") for t in range(PACK)]
+        widest = max(CHUNKS)
+        near1 = keep.tile([P, 8 * widest], F32, name="near1")
+        near2 = keep.tile([P, 8 * widest], F32, name="near2")
+        out_words = keep.tile([P, S], U32, name="out_words", align_bytes=64)
+        out_scales = keep.tile([P, S], U8, name="out_scales", align_bytes=64)
+        out_rows = out_0.rearrange("(p t) j -> p t j", t=PACK)
+        out_w = out_1[0].rearrange("p n t -> p (n t)").bitcast(I32)
+
+        def square(t):
+            nc.scalar.activation(y[t][:], acc[t][:], ACT.Relu)
+            nc.scalar.activation(sq[t][:], y[t][:], ACT.Square)
+            if not PE_SUM:
+                first = CHUNKS[0]
+                nc.scalar.activation(own[t][:, :first], y[t][:, :first], ACT.Square)
+                nc.sync.dma_start(own[t][:, first:], sq[t][:, first:])
+
+        def fetch(u, c0, n, t):
+            lists = slice(c0 // 16, (c0 + n) // 16)
+            a = near1[:, (u % 8) * widest : (u % 8) * widest + n]
+            b = near2[:, (u % 8) * widest : (u % 8) * widest + n]
+            rs = keep.tile([P, n], F32, name=f"rs{u}")
+            if PE_SUM:
+                nc.vector.tensor_copy(a, sq[t][:].indirect(p1_sb[:, lists]))
+                nc.vector.tensor_copy(b, sq[t][:].indirect(p2_sb[:, lists]))
+                total = psum.tile([P, S], F32, name=f"total{u}", tag="bank")
+                blocks = n // P
+                terms = [sq[t][:, c0 : c0 + n], a, b]
+                for i, term in enumerate(terms):
+                    for k in range(blocks):
+                        nc.tensor.matmul(
+                            total[:, k * P : (k + 1) * P],
+                            term[:, k * P : (k + 1) * P],
+                            ident[:],
+                            start=(i == 0 and k == 0),
+                            stop=(i == 2 and k == blocks - 1),
+                            is_transpose=True,
+                        )
+                nc.scalar.activation(rs[:], total[:, :n], ACT.Abs_reciprocal_sqrt, bias=bias[:], scale=0.5)
+                back = psum.tile([P, S], F32, name=f"back{u}", tag="bank")
+                for k in range(blocks):
+                    nc.tensor.transpose(back[:, k * P : (k + 1) * P], rs[:, k * P : (k + 1) * P], ident[:])
+                return back[:, :n]
+            nc.vector.tensor_tensor(a, sq[t][:].indirect(p1_sb[:, lists]), own[t][:, c0 : c0 + n], ALU.add)
+            nc.vector.tensor_tensor(b, sq[t][:].indirect(p2_sb[:, lists]), a, ALU.add)
+            nc.scalar.activation(rs[:], b, ACT.Abs_reciprocal_sqrt, bias=bias[:], scale=0.5)
+            return rs[:]
+
+        def second(ci, c0, n, z_rows, lo, width):
+            name = f"{ci}_{lo}"
+            z_in = keep.tile([P, width * PACK], BF16, name=f"z_in{name}", align_bytes=64)
+            dst = z_in[:].rearrange("p (c i t) -> p c t i", i=4, t=PACK)
+            src = z_rows[:].rearrange("p (t c i) -> p c t i", i=4, t=PACK)[:, lo // 4 : (lo + width) // 4]
+            if ci in G_ON_VECTOR:
+                nc.vector.tensor_copy(dst, src)
+            else:
+                nc.scalar.copy(dst, src)
+            z_words = keep.tile([P, width], U32, name=f"z_words{name}", align_bytes=64)
+            z_scales = keep.tile([P, width], U8, name=f"z_scales{name}", align_bytes=64)
+            nc.vector.quantize_mx(z_words[:].bitcast(FP8X4), z_scales[:], z_in[:])
+            res = keep.tile([P, PACK, width], F32, name=f"res{name}")
+            res_in = keep.tile([P, width * PACK], BF16, name=f"res_in{name}", align_bytes=64)
+            for k in range(width // P):
+                cols = slice(k * P, (k + 1) * P)
+                bank = psum.tile([P, PACK, P], F32, name=f"out{name}_{k}", tag="bank")
+                for t in range(PACK):
+                    nc.tensor.matmul_mx(
+                        out=bank[:, t, :],
+                        lhsT=w2w[:, 2 * t * P : 2 * (t + 1) * P].bitcast(FP4X4),
+                        lhsT_scale=w2s[:, t * P : (t + 1) * P],
+                        rhs=z_words[:, cols].bitcast(FP8X4),
+                        rhs_scale=z_scales[:, cols],
+                        start=True,
+                        stop=True,
+                    )
+                dst = res_in[:, k * P * PACK : (k + 1) * P * PACK].rearrange("p (j t) -> p j t", t=PACK)
+                if (c0 + lo) // P + k in O_ON_VECTOR:
+                    nc.vector.tensor_copy(dst, bank[:].rearrange("p t j -> p j t"))
+                else:
+                    nc.scalar.copy(dst, bank[:].rearrange("p t j -> p j t"))
+                nc.scalar.copy(res[:, :, cols], bank[:])
+            first = c0 + lo
+            nc.vector.quantize_mx(out_words[:, first : first + width].bitcast(FP8X4), out_scales[:, first : first + width], res_in[:])
+            nc.sync.dma_start(out_rows[:, :, first : first + width], res[:])
+            nc.sync.dma_start(out_w[:, first : first + width], out_words[:, first : first + width].bitcast(I32))
+
+        units = []
+        c0 = 0
+        for ci, n in enumerate(CHUNKS):
+            z_rows = keep.tile([P, PACK * n], BF16, name=f"z_rows{ci}")
+            for t in range(PACK):
+                units.append((ci, c0, n, t, z_rows))
+            c0 = c0 + n
+
+        square(0)
+        square(1)
+        pending = None
+        for u in range(len(units) + 1):
+            got = None
+            if u < len(units):
+                ci, c0, n, t, z_rows = units[u]
+                if u + 2 < PACK:
+                    square(u + 2)
+                got = fetch(u, c0, n, t)
+            if pending is not None:
+                ci, c0, n, t, z_rows = units[u - 1]
+                nc.vector.scalar_tensor_tensor(
+                    z_rows[:, t * n : (t + 1) * n], y[t][:, c0 : c0 + n], gn_sb[:, t : t + 1], pending, ALU.mult, ALU.mult
+                )
+                if t == PACK - 1:
+                    piece = PIECES[ci]
+                    for lo in range(0, n, piece):
+                        second(ci, c0, n, z_rows, lo, piece)
+            pending = got
+
+        for q in range(4):
+            queue = nc.sync if q % 2 == 0 else nc.scalar
+            queue.dma_start(out_2[0, 4 * q : 4 * q + 4, :].bitcast(I32), out_scales[32 * q : 32 * q + 4, :].bitcast(I32))

@@ -24,7 +24,7 @@ CHUNKS = [256,256]
 PIECES = [256,128]
 PE_SUM = False
 G_ON_VECTOR = [1]
-O_ON_VECTOR = [3]
+O_ON_VECTOR = [2,3]
 
 
 def deal_words(nc, dealt, raw):
@@ -45,6 +45,7 @@ def tile_picked_lrn8_relu_po_kernel(tc, x_words, x_scales, w1_words, w1_scales, 
     nc = tc.nc
     with ExitStack() as ctx:
         keep = ctx.enter_context(tc.tile_pool(name="keep", bufs=1))
+        reuse = ctx.enter_context(tc.tile_pool(name="reuse", bufs=1))
         psum = ctx.enter_context(tc.psum_pool(name="psum", bufs=8))
 
         offs_sb = keep.tile([P, S // 16], U16, name="offs_sb")
@@ -54,26 +55,31 @@ def tile_picked_lrn8_relu_po_kernel(tc, x_words, x_scales, w1_words, w1_scales, 
         xs_raw = keep.tile([P, T], U8, name="xs_raw", align_bytes=64)
         xs_got = keep.tile([P, S], U8, name="xs_got", tag="small", align_bytes=64)
         xs_moved = keep.tile([P, PASSES * S], U8, name="xs_moved", align_bytes=64)
-        w1s_raw = keep.tile([P, PASSES * H], U8, name="w1s_raw", tag="late", align_bytes=64)
+        w1s_raw = keep.tile([P, H], U8, name="w1s_raw", align_bytes=64)
+        w1s_flat = keep.tile([P, H], U8, name="w1s_flat", align_bytes=64)
         w1w_raw = keep.tile([P, PASSES * 2 * H], U8, name="w1w_raw", tag="words", align_bytes=64)
         w1s = keep.tile([P, PASSES * H], U8, name="w1s", align_bytes=64)
-        w2s = keep.tile([P, N], U8, name="w2s", align_bytes=64)
         w1w = keep.tile([P, PASSES * 2 * H], U8, name="w1w", align_bytes=64)
-        w2w = keep.tile([P, 2 * N], U8, name="w2w", align_bytes=64)
-        xw_raw = [keep.tile([P, T], U32, name=f"xw_raw{z}", align_bytes=64) for z in range(PASSES)]
+        xw_raw = [
+            keep.tile([P, T], U32, name="xw_raw0", tag="late", align_bytes=64),
+            reuse.tile([P, T], U32, name="xw_raw1", align_bytes=64, offset=0),
+        ]
         xw = [keep.tile([P, S], U32, name=f"xw{z}", align_bytes=64) for z in range(PASSES)]
         ones = keep.tile([P, 1], F32, name="ones")
         bias = keep.tile([P, 1], F32, name="bias")
 
         nc.vector.memset(xs_raw[32:64, :].bitcast(I32), 0)
         nc.vector.memset(xs_raw[64:128, :].bitcast(I32), 0)
-        nc.gpsimd.memset(w1s_raw[:].bitcast(I32), 0)
+        nc.gpsimd.memset(w1s_raw[32:64, :].bitcast(I32), 0)
+        nc.gpsimd.memset(w1s_raw[64:128, :].bitcast(I32), 0)
+        nc.gpsimd.memset(w1s[:].bitcast(I32), 0)
         nc.vector.memset(ones[:], 1.0)
         nc.vector.memset(xs_moved[:].bitcast(I32), 0)
         nc.scalar.activation(bias[:], ones[:], ACT.Abs_reciprocal_sqrt)
 
         nc.sync.dma_start(offs_sb[:], offs)
         nc.sync.dma_start(xs_raw[0:32, :].bitcast(I32), x_scales.bitcast(I32).rearrange("z r c -> r z c"))
+        nc.sync.dma_start(w1s_raw[0:32, :].bitcast(I32), w1_scales.bitcast(I32).rearrange("z r c -> r z c"))
         nc.sync.dma_start(
             w1w_raw[:].bitcast(I32).rearrange("p (z c) -> p z c", z=PASSES),
             w1_words.bitcast(I32).rearrange("z p c -> p z c"),
@@ -82,16 +88,17 @@ def tile_picked_lrn8_relu_po_kernel(tc, x_words, x_scales, w1_words, w1_scales, 
         nc.sync.dma_start(p2_sb[:], p2)
         for z in range(PASSES):
             nc.sync.dma_start(xw_raw[z][:].bitcast(I32), x_words[z].rearrange("p n t -> p (n t)").bitcast(I32))
-        for q in range(4):
-            queue = nc.gpsimd if q < 2 else nc.scalar
-            queue.dma_start(
-                w1s_raw[32 * q : 32 * q + 4, :].bitcast(I32).rearrange("r (z c) -> r z c", z=PASSES),
-                w1_scales[:, 4 * q : 4 * q + 4, :].bitcast(I32).rearrange("z r c -> r z c"),
-            )
         if PE_SUM:
             ident = keep.tile([P, P], F32, name="ident")
             make_identity(nc, ident[:])
 
+        deal_scales(nc, w1s_flat, w1s_raw)
+        for q in range(4):
+            queue = nc.gpsimd if q < 2 else nc.scalar
+            queue.dma_start(
+                w1s[32 * q : 32 * q + 4, :].bitcast(I32).rearrange("r (z c) -> r z c", z=PASSES),
+                w1s_flat[8 * q : 8 * q + 8, :].bitcast(I32),
+            )
         nc.vector.tensor_copy(xs_got[:], xs_raw[:].indirect(offs_sb[:]))
         for q in range(4):
             nc.scalar.dma_start(
@@ -100,38 +107,46 @@ def tile_picked_lrn8_relu_po_kernel(tc, x_words, x_scales, w1_words, w1_scales, 
             )
         deal_words(nc, w1w, w1w_raw)
         nc.vector.tensor_copy(xw[0][:], xw_raw[0][:].indirect(offs_sb[:]))
-        deal_scales(nc, w1s, w1s_raw)
         gn_sb = keep.tile([P, PACK], F32, name="gn_sb", tag="late", align_bytes=64)
         nc.sync.dma_start(gn_sb[:], gn.rearrange("(p t) o -> p (t o)", t=PACK))
-        nc.vector.tensor_copy(xw[1][:], xw_raw[1][:].indirect(offs_sb[:]))
+        for h in range(2):
+            nc.vector.tensor_copy(xw[1][:, h * 256 : (h + 1) * 256], xw_raw[1][:].indirect(offs_sb[:, h * 16 : (h + 1) * 16]))
         w2w_raw = keep.tile([P, 2 * N], U8, name="w2w_raw", tag="words", align_bytes=64)
         nc.sync.dma_start(w2w_raw[:].bitcast(I32), w2_words[0].bitcast(I32))
         w2s_raw = keep.tile([P, N], U8, name="w2s_raw", tag="small", align_bytes=64)
         nc.gpsimd.memset(w2s_raw[:].bitcast(I32), 0)
         for q in range(4):
             nc.sync.dma_start(w2s_raw[32 * q : 32 * q + 4, :].bitcast(I32), w2_scales[0, 4 * q : 4 * q + 4, :].bitcast(I32))
+        w2w = reuse.tile([P, 2 * N], U8, name="w2w", align_bytes=64, offset=0)
+        w2s = reuse.tile([P, N], U8, name="w2s", align_bytes=64, offset=2 * N)
         deal_words(nc, w2w, w2w_raw)
         deal_scales(nc, w2s, w2s_raw)
 
-        acc = [psum.tile([P, S], F32, name=f"acc{t}", tag="bank") for t in range(PACK)]
-        for t in range(PACK):
+        def first(bank, t, lo, width):
             for z in range(PASSES):
                 col = (t * PASSES + z) * P
                 nc.tensor.matmul_mx(
-                    out=acc[t][:],
+                    out=bank,
                     lhsT=w1w[:, 2 * col : 2 * col + 2 * P].bitcast(FP4X4),
-                    lhsT_scale=w1s[:, col : col + P],
-                    rhs=xw[z][:].bitcast(FP8X4),
-                    rhs_scale=xs_moved[:, z * S : (z + 1) * S],
+                    lhsT_scale=w1s[:, z * H + t * P : z * H + (t + 1) * P],
+                    rhs=xw[z][:, lo : lo + width].bitcast(FP8X4),
+                    rhs_scale=xs_moved[:, z * S + lo : z * S + lo + width],
                     start=(z == 0),
                     stop=(z == PASSES - 1),
                 )
+
+        halves = [psum.tile([P, S], F32, name=f"half{h}", tag="bank") for h in range(2)]
+        for k in range(S // P):
+            first(halves[k // 2][:, (k % 2) * P : (k % 2 + 1) * P], 0, k * P, P)
+        acc = [None] + [psum.tile([P, S], F32, name=f"acc{t}", tag="bank") for t in range(1, PACK)]
+        for t in range(1, PACK):
+            first(acc[t][:], t, 0, S)
 
         y = [keep.tile([P, S], F32, name=f"y{t}") for t in range(PACK)]
         sq = [keep.tile([P, S], F32, name=f"sq{t}") for t in range(PACK)]
         own = [keep.tile([P, S], F32, name=f"own{t}") for t in range(PACK)]
         widest = max(CHUNKS)
-        near1 = keep.tile([P, 8 * widest], F32, name="near1")
+        near1 = keep.tile([P, 2 * widest], F32, name="near1")
         near2 = keep.tile([P, 8 * widest], F32, name="near2")
         out_words = keep.tile([P, S], U32, name="out_words", align_bytes=64)
         out_scales = keep.tile([P, S], U8, name="out_scales", align_bytes=64)
@@ -139,6 +154,14 @@ def tile_picked_lrn8_relu_po_kernel(tc, x_words, x_scales, w1_words, w1_scales, 
         out_w = out_1[0].rearrange("p n t -> p (n t)").bitcast(I32)
 
         def square(t):
+            if t == 0:
+                for h in range(2):
+                    cols = slice(h * 256, (h + 1) * 256)
+                    nc.scalar.activation(y[0][:, cols], halves[h][:, :256], ACT.Relu)
+                    nc.scalar.activation(sq[0][:, cols], y[0][:, cols], ACT.Square)
+                nc.vector.tensor_tensor(own[0][:, :256], y[0][:, :256], y[0][:, :256], ALU.mult)
+                nc.sync.dma_start(own[0][:, 256:], sq[0][:, 256:])
+                return
             nc.scalar.activation(y[t][:], acc[t][:], ACT.Relu)
             nc.scalar.activation(sq[t][:], y[t][:], ACT.Square)
             if not PE_SUM:
@@ -148,7 +171,7 @@ def tile_picked_lrn8_relu_po_kernel(tc, x_words, x_scales, w1_words, w1_scales, 
 
         def fetch(u, c0, n, t):
             lists = slice(c0 // 16, (c0 + n) // 16)
-            a = near1[:, (u % 8) * widest : (u % 8) * widest + n]
+            a = near1[:, (u % 2) * widest : (u % 2) * widest + n]
             b = near2[:, (u % 8) * widest : (u % 8) * widest + n]
             rs = keep.tile([P, n], F32, name=f"rs{u}")
             if PE_SUM:
@@ -205,11 +228,14 @@ def tile_picked_lrn8_relu_po_kernel(tc, x_words, x_scales, w1_words, w1_scales, 
                         stop=True,
                     )
                 dst = res_in[:, k * P * PACK : (k + 1) * P * PACK].rearrange("p (j t) -> p j t", t=PACK)
+                nc.scalar.copy(res[:, :, cols], bank[:])
                 if (c0 + lo) // P + k in O_ON_VECTOR:
-                    nc.vector.tensor_copy(dst, bank[:].rearrange("p t j -> p j t"))
+                    nc.vector.tensor_copy(
+                        res_in[:, k * P * PACK : (k + 1) * P * PACK].rearrange("p (c i t) -> p c t i", i=4, t=PACK),
+                        res[:, :, cols].rearrange("p t (c i) -> p c t i", i=4),
+                    )
                 else:
                     nc.scalar.copy(dst, bank[:].rearrange("p t j -> p j t"))
-                nc.scalar.copy(res[:, :, cols], bank[:])
             first = c0 + lo
             nc.vector.quantize_mx(out_words[:, first : first + width].bitcast(FP8X4), out_scales[:, first : first + width], res_in[:])
             nc.sync.dma_start(out_rows[:, :, first : first + width], res[:])

@@ -46,6 +46,7 @@ def tile_picked_lrn8_relu_po_kernel(tc, x_words, x_scales, w1_words, w1_scales, 
     with ExitStack() as ctx:
         keep = ctx.enter_context(tc.tile_pool(name="keep", bufs=1))
         reuse = ctx.enter_context(tc.tile_pool(name="reuse", bufs=1))
+        later = ctx.enter_context(tc.tile_pool(name="later", bufs=1))
         psum = ctx.enter_context(tc.psum_pool(name="psum", bufs=8))
 
         offs_sb = keep.tile([P, S // 16], U16, name="offs_sb")
@@ -53,27 +54,27 @@ def tile_picked_lrn8_relu_po_kernel(tc, x_words, x_scales, w1_words, w1_scales, 
         p2_sb = keep.tile([P, S // 16], U16, name="p2_sb")
 
         xs_raw = keep.tile([P, T], U8, name="xs_raw", align_bytes=64)
-        xs_got = keep.tile([P, S], U8, name="xs_got", tag="small", align_bytes=64)
+        xs_got = keep.tile([P, S], U8, name="xs_got", align_bytes=64)
         xs_moved = keep.tile([P, PASSES * S], U8, name="xs_moved", align_bytes=64)
         w1s_raw = keep.tile([P, H], U8, name="w1s_raw", align_bytes=64)
         w1s_flat = keep.tile([P, H], U8, name="w1s_flat", align_bytes=64)
-        w1w_raw = keep.tile([P, PASSES * 2 * H], U8, name="w1w_raw", tag="words", align_bytes=64)
+        w1w_raw = keep.tile([P, PASSES * 2 * H], U8, name="w1w_raw", align_bytes=64)
         w1s = keep.tile([P, PASSES * H], U8, name="w1s", align_bytes=64)
         w1w = keep.tile([P, PASSES * 2 * H], U8, name="w1w", align_bytes=64)
         xw_raw = [
-            keep.tile([P, T], U32, name="xw_raw0", tag="late", align_bytes=64),
+            later.tile([P, T], U32, name="xw_raw0", align_bytes=64, offset=0),
             reuse.tile([P, T], U32, name="xw_raw1", align_bytes=64, offset=0),
         ]
         xw = [keep.tile([P, S], U32, name=f"xw{z}", align_bytes=64) for z in range(PASSES)]
-        ones = keep.tile([P, 1], F32, name="ones")
+        ones = reuse.tile([P, 1], F32, name="ones", align_bytes=64, offset=4096)
         bias = keep.tile([P, 1], F32, name="bias")
 
+        nc.vector.memset(ones[:], 1.0)
         nc.vector.memset(xs_raw[32:64, :].bitcast(I32), 0)
         nc.vector.memset(xs_raw[64:128, :].bitcast(I32), 0)
         nc.gpsimd.memset(w1s_raw[32:64, :].bitcast(I32), 0)
         nc.gpsimd.memset(w1s_raw[64:128, :].bitcast(I32), 0)
         nc.gpsimd.memset(w1s[:].bitcast(I32), 0)
-        nc.vector.memset(ones[:], 1.0)
         nc.vector.memset(xs_moved[:].bitcast(I32), 0)
         nc.scalar.activation(bias[:], ones[:], ACT.Abs_reciprocal_sqrt)
 
@@ -86,34 +87,34 @@ def tile_picked_lrn8_relu_po_kernel(tc, x_words, x_scales, w1_words, w1_scales, 
         )
         nc.sync.dma_start(p1_sb[:], p1)
         nc.sync.dma_start(p2_sb[:], p2)
-        for z in range(PASSES):
-            nc.sync.dma_start(xw_raw[z][:].bitcast(I32), x_words[z].rearrange("p n t -> p (n t)").bitcast(I32))
+        nc.sync.dma_start(xw_raw[0][:].bitcast(I32), x_words[0].rearrange("p n t -> p (n t)").bitcast(I32))
         if PE_SUM:
             ident = keep.tile([P, P], F32, name="ident")
             make_identity(nc, ident[:])
 
         deal_scales(nc, w1s_flat, w1s_raw)
         for q in range(4):
-            queue = nc.gpsimd if q < 2 else nc.scalar
+            queue = nc.gpsimd if q == 0 else nc.scalar
             queue.dma_start(
                 w1s[32 * q : 32 * q + 4, :].bitcast(I32).rearrange("r (z c) -> r z c", z=PASSES),
                 w1s_flat[8 * q : 8 * q + 8, :].bitcast(I32),
             )
+        nc.sync.dma_start(xw_raw[1][:].bitcast(I32), x_words[1].rearrange("p n t -> p (n t)").bitcast(I32))
         nc.vector.tensor_copy(xs_got[:], xs_raw[:].indirect(offs_sb[:]))
         for q in range(4):
-            nc.scalar.dma_start(
+            nc.sync.dma_start(
                 xs_moved[32 * q : 32 * q + 4, :].bitcast(I32).rearrange("r (z c) -> r z c", z=PASSES),
                 xs_got[8 * q : 8 * q + 8, :].bitcast(I32),
             )
         deal_words(nc, w1w, w1w_raw)
         nc.vector.tensor_copy(xw[0][:], xw_raw[0][:].indirect(offs_sb[:]))
-        gn_sb = keep.tile([P, PACK], F32, name="gn_sb", tag="late", align_bytes=64)
+        gn_sb = later.tile([P, PACK], F32, name="gn_sb", align_bytes=64, offset=1088)
         nc.sync.dma_start(gn_sb[:], gn.rearrange("(p t) o -> p (t o)", t=PACK))
         for h in range(2):
             nc.vector.tensor_copy(xw[1][:, h * 256 : (h + 1) * 256], xw_raw[1][:].indirect(offs_sb[:, h * 16 : (h + 1) * 16]))
-        w2w_raw = keep.tile([P, 2 * N], U8, name="w2w_raw", tag="words", align_bytes=64)
+        w2w_raw = later.tile([P, 2 * N], U8, name="w2w_raw", align_bytes=64, offset=64)
         nc.sync.dma_start(w2w_raw[:].bitcast(I32), w2_words[0].bitcast(I32))
-        w2s_raw = keep.tile([P, N], U8, name="w2s_raw", tag="small", align_bytes=64)
+        w2s_raw = later.tile([P, N], U8, name="w2s_raw", align_bytes=64, offset=1152)
         nc.gpsimd.memset(w2s_raw[:].bitcast(I32), 0)
         for q in range(4):
             nc.sync.dma_start(w2s_raw[32 * q : 32 * q + 4, :].bitcast(I32), w2_scales[0, 4 * q : 4 * q + 4, :].bitcast(I32))
@@ -123,7 +124,7 @@ def tile_picked_lrn8_relu_po_kernel(tc, x_words, x_scales, w1_words, w1_scales, 
         deal_scales(nc, w2s, w2s_raw)
 
         def first(bank, t, lo, width):
-            for z in range(PASSES):
+            for z in reversed(range(PASSES)):
                 col = (t * PASSES + z) * P
                 nc.tensor.matmul_mx(
                     out=bank,
@@ -131,8 +132,8 @@ def tile_picked_lrn8_relu_po_kernel(tc, x_words, x_scales, w1_words, w1_scales, 
                     lhsT_scale=w1s[:, z * H + t * P : z * H + (t + 1) * P],
                     rhs=xw[z][:, lo : lo + width].bitcast(FP8X4),
                     rhs_scale=xs_moved[:, z * S + lo : z * S + lo + width],
-                    start=(z == 0),
-                    stop=(z == PASSES - 1),
+                    start=(z == PASSES - 1),
+                    stop=(z == 0),
                 )
 
         halves = [psum.tile([P, S], F32, name=f"half{h}", tag="bank") for h in range(2)]

@@ -1,7 +1,6 @@
 from contextlib import ExitStack
 
 import concourse.mybir as mybir
-from concourse.masks import make_identity
 
 K, T, S, N, H = 1024, 2048, 512, 512, 512
 FLOPS = 2 * K * H * S + 2 * H * N * S
@@ -20,24 +19,20 @@ ALU = mybir.AluOpType
 P = 128
 PACK = 4
 PASSES = K // 512
-CHUNKS = [256,256]
-PIECES = [256,128]
-PE_SUM = False
-G_ON_VECTOR = [1]
-O_ON_VECTOR = [2,3]
+HALF = S // 2
 
 
 def deal_words(nc, dealt, raw):
     nc.vector.tensor_copy(
-        out=dealt[:].rearrange("p (t c m b) -> p c t m b", t=PACK, m=8, b=2),
-        in_=raw[:].rearrange("p (c m t b) -> p c t m b", t=PACK, m=8, b=2),
+        out=dealt.rearrange("p (t c m b) -> p c t m b", t=PACK, m=8, b=2),
+        in_=raw.rearrange("p (c m t b) -> p c t m b", t=PACK, m=8, b=2),
     )
 
 
 def deal_scales(nc, dealt, raw):
     nc.vector.tensor_copy(
-        out=dealt[:].rearrange("p (t c m) -> p c t m", t=PACK, m=16),
-        in_=raw[:].rearrange("p (c m t) -> p c t m", t=PACK, m=16),
+        out=dealt.rearrange("p (t c m) -> p c t m", t=PACK, m=16),
+        in_=raw.rearrange("p (c m t) -> p c t m", t=PACK, m=16),
     )
 
 
@@ -45,8 +40,10 @@ def tile_picked_lrn8_relu_po_kernel(tc, x_words, x_scales, w1_words, w1_scales, 
     nc = tc.nc
     with ExitStack() as ctx:
         keep = ctx.enter_context(tc.tile_pool(name="keep", bufs=1))
-        reuse = ctx.enter_context(tc.tile_pool(name="reuse", bufs=1))
         later = ctx.enter_context(tc.tile_pool(name="later", bufs=1))
+        owns = ctx.enter_context(tc.tile_pool(name="owns", bufs=1))
+        roots = ctx.enter_context(tc.tile_pool(name="roots", bufs=1))
+        ring = ctx.enter_context(tc.tile_pool(name="ring", bufs=3))
         psum = ctx.enter_context(tc.psum_pool(name="psum", bufs=8))
 
         offs_sb = keep.tile([P, S // 16], U16, name="offs_sb")
@@ -55,221 +52,273 @@ def tile_picked_lrn8_relu_po_kernel(tc, x_words, x_scales, w1_words, w1_scales, 
 
         xs_raw = keep.tile([P, T], U8, name="xs_raw", align_bytes=64)
         xs_got = keep.tile([P, S], U8, name="xs_got", align_bytes=64)
-        xs_moved = keep.tile([P, PASSES * S], U8, name="xs_moved", align_bytes=64)
         w1s_raw = keep.tile([P, H], U8, name="w1s_raw", align_bytes=64)
-        w1s_flat = keep.tile([P, H], U8, name="w1s_flat", align_bytes=64)
+        flat = keep.tile([P, S + H], U8, name="flat", align_bytes=64)
+        planes1 = keep.tile([P, PASSES * (S + H)], U8, name="planes1", align_bytes=64)
         w1w_raw = keep.tile([P, PASSES * 2 * H], U8, name="w1w_raw", align_bytes=64)
-        w1s = keep.tile([P, PASSES * H], U8, name="w1s", align_bytes=64)
         w1w = keep.tile([P, PASSES * 2 * H], U8, name="w1w", align_bytes=64)
         xw_raw = [
             later.tile([P, T], U32, name="xw_raw0", align_bytes=64, offset=0),
-            reuse.tile([P, T], U32, name="xw_raw1", align_bytes=64, offset=0),
+            keep.tile([P, T], U32, name="xw_raw1", align_bytes=64),
         ]
         xw = [keep.tile([P, S], U32, name=f"xw{z}", align_bytes=64) for z in range(PASSES)]
-        ones = reuse.tile([P, 1], F32, name="ones", align_bytes=64, offset=4096)
+        ones = keep.tile([P, 1], F32, name="ones")
         bias = keep.tile([P, 1], F32, name="bias")
 
         nc.vector.memset(ones[:], 1.0)
+        nc.vector.memset(w1s_raw[32:64, :].bitcast(I32), 0)
+        nc.vector.memset(w1s_raw[64:128, :].bitcast(I32), 0)
         nc.vector.memset(xs_raw[32:64, :].bitcast(I32), 0)
-        nc.vector.memset(xs_raw[64:128, :].bitcast(I32), 0)
-        nc.gpsimd.memset(w1s_raw[32:64, :].bitcast(I32), 0)
-        nc.gpsimd.memset(w1s_raw[64:128, :].bitcast(I32), 0)
-        nc.gpsimd.memset(w1s[:].bitcast(I32), 0)
-        nc.vector.memset(xs_moved[:].bitcast(I32), 0)
-        nc.scalar.activation(bias[:], ones[:], ACT.Abs_reciprocal_sqrt)
+        nc.gpsimd.memset(xs_raw[64:128, :].bitcast(I32), 0)
+        nc.gpsimd.memset(planes1[:].bitcast(I32), 0)
 
         nc.sync.dma_start(offs_sb[:], offs)
         nc.sync.dma_start(xs_raw[0:32, :].bitcast(I32), x_scales.bitcast(I32).rearrange("z r c -> r z c"))
         nc.sync.dma_start(w1s_raw[0:32, :].bitcast(I32), w1_scales.bitcast(I32).rearrange("z r c -> r z c"))
+        nc.sync.dma_start(p1_sb[:], p1)
+        nc.sync.dma_start(p2_sb[:], p2)
         nc.sync.dma_start(
             w1w_raw[:].bitcast(I32).rearrange("p (z c) -> p z c", z=PASSES),
             w1_words.bitcast(I32).rearrange("z p c -> p z c"),
         )
-        nc.sync.dma_start(p1_sb[:], p1)
-        nc.sync.dma_start(p2_sb[:], p2)
-        nc.sync.dma_start(xw_raw[0][:].bitcast(I32), x_words[0].rearrange("p n t -> p (n t)").bitcast(I32))
-        if PE_SUM:
-            ident = keep.tile([P, P], F32, name="ident")
-            make_identity(nc, ident[:])
+        for z in range(PASSES):
+            nc.sync.dma_start(xw_raw[z][:].bitcast(I32), x_words[z].rearrange("p n t -> p (n t)").bitcast(I32))
+        nc.scalar.activation(bias[:], ones[:], ACT.Abs_reciprocal_sqrt)
 
-        deal_scales(nc, w1s_flat, w1s_raw)
-        for q in range(4):
-            queue = nc.gpsimd if q == 0 else nc.scalar
-            queue.dma_start(
-                w1s[32 * q : 32 * q + 4, :].bitcast(I32).rearrange("r (z c) -> r z c", z=PASSES),
-                w1s_flat[8 * q : 8 * q + 8, :].bitcast(I32),
-            )
-        nc.sync.dma_start(xw_raw[1][:].bitcast(I32), x_words[1].rearrange("p n t -> p (n t)").bitcast(I32))
+        deal_scales(nc, flat[:, S:], w1s_raw[:])
         nc.vector.tensor_copy(xs_got[:], xs_raw[:].indirect(offs_sb[:]))
+        nc.vector.tensor_copy(flat[:, :S].bitcast(I32), xs_got[:].bitcast(I32))
         for q in range(4):
-            nc.sync.dma_start(
-                xs_moved[32 * q : 32 * q + 4, :].bitcast(I32).rearrange("r (z c) -> r z c", z=PASSES),
-                xs_got[8 * q : 8 * q + 8, :].bitcast(I32),
+            nc.scalar.dma_start(
+                planes1[32 * q : 32 * q + 4, :].bitcast(I32).rearrange("r (z c) -> r z c", z=PASSES),
+                flat[8 * q : 8 * q + 8, :].bitcast(I32),
             )
-        deal_words(nc, w1w, w1w_raw)
+        deal_words(nc, w1w[:], w1w_raw[:])
         nc.vector.tensor_copy(xw[0][:], xw_raw[0][:].indirect(offs_sb[:]))
-        gn_sb = later.tile([P, PACK], F32, name="gn_sb", align_bytes=64, offset=1088)
-        nc.sync.dma_start(gn_sb[:], gn.rearrange("(p t) o -> p (t o)", t=PACK))
         for h in range(2):
-            nc.vector.tensor_copy(xw[1][:, h * 256 : (h + 1) * 256], xw_raw[1][:].indirect(offs_sb[:, h * 16 : (h + 1) * 16]))
-        w2w_raw = later.tile([P, 2 * N], U8, name="w2w_raw", align_bytes=64, offset=64)
+            nc.vector.tensor_copy(xw[1][:, h * HALF : (h + 1) * HALF], xw_raw[1][:].indirect(offs_sb[:, h * 16 : (h + 1) * 16]))
+
+        w2w_raw = later.tile([P, 2 * N], U8, name="w2w_raw", align_bytes=64, offset=0)
+        w2s_raw = later.tile([P, N], U8, name="w2s_raw", align_bytes=64, offset=2 * N)
+        gn_sb = later.tile([P, PACK], F32, name="gn_sb", align_bytes=64, offset=3 * N)
         nc.sync.dma_start(w2w_raw[:].bitcast(I32), w2_words[0].bitcast(I32))
-        w2s_raw = later.tile([P, N], U8, name="w2s_raw", align_bytes=64, offset=1152)
+        nc.sync.dma_start(gn_sb[:], gn.rearrange("(p t) o -> p (t o)", t=PACK))
         nc.gpsimd.memset(w2s_raw[:].bitcast(I32), 0)
         for q in range(4):
             nc.sync.dma_start(w2s_raw[32 * q : 32 * q + 4, :].bitcast(I32), w2_scales[0, 4 * q : 4 * q + 4, :].bitcast(I32))
-        w2w = reuse.tile([P, 2 * N], U8, name="w2w", align_bytes=64, offset=0)
-        w2s = reuse.tile([P, N], U8, name="w2s", align_bytes=64, offset=2 * N)
-        deal_words(nc, w2w, w2w_raw)
-        deal_scales(nc, w2s, w2s_raw)
 
-        def first(bank, t, lo, width):
-            for z in reversed(range(PASSES)):
+        def first(bank, t, lo, width, order):
+            for z in order:
                 col = (t * PASSES + z) * P
                 nc.tensor.matmul_mx(
                     out=bank,
                     lhsT=w1w[:, 2 * col : 2 * col + 2 * P].bitcast(FP4X4),
-                    lhsT_scale=w1s[:, z * H + t * P : z * H + (t + 1) * P],
+                    lhsT_scale=planes1[:, z * (S + H) + S + t * P : z * (S + H) + S + (t + 1) * P],
                     rhs=xw[z][:, lo : lo + width].bitcast(FP8X4),
-                    rhs_scale=xs_moved[:, z * S + lo : z * S + lo + width],
-                    start=(z == PASSES - 1),
-                    stop=(z == 0),
+                    rhs_scale=planes1[:, z * (S + H) + lo : z * (S + H) + lo + width],
+                    start=(z == order[0]),
+                    stop=(z == order[-1]),
                 )
-
-        halves = [psum.tile([P, S], F32, name=f"half{h}", tag="bank") for h in range(2)]
-        for k in range(S // P):
-            first(halves[k // 2][:, (k % 2) * P : (k % 2 + 1) * P], 0, k * P, P)
-        acc = [None] + [psum.tile([P, S], F32, name=f"acc{t}", tag="bank") for t in range(1, PACK)]
-        for t in range(1, PACK):
-            first(acc[t][:], t, 0, S)
 
         y = [keep.tile([P, S], F32, name=f"y{t}") for t in range(PACK)]
         sq = [keep.tile([P, S], F32, name=f"sq{t}") for t in range(PACK)]
-        own = [keep.tile([P, S], F32, name=f"own{t}") for t in range(PACK)]
-        widest = max(CHUNKS)
-        near1 = keep.tile([P, 2 * widest], F32, name="near1")
-        near2 = keep.tile([P, 8 * widest], F32, name="near2")
+        own_a = [owns.tile([P, HALF], F32, name=f"own_a{t}", align_bytes=64, offset=1024 * t) for t in range(PACK)]
+        own_b = [keep.tile([P, HALF], F32, name=f"own_b{t}") for t in range(PACK)]
+
+        for k in range(S // P):
+            cols = slice(k * P, (k + 1) * P)
+            bank = psum.tile([P, P], F32, name=f"acc0_{k}", tag="bank")
+            first(bank[:], 0, k * P, P, [0, 1])
+            if k < 2:
+                nc.scalar.activation(y[0][:, cols], bank[:], ACT.Relu)
+            else:
+                nc.vector.tensor_scalar_max(y[0][:, cols], bank[:], 0.0)
+        nc.scalar.activation(sq[0][:, :HALF], y[0][:, :HALF], ACT.Square)
+        nc.scalar.activation(own_a[0][:], y[0][:, :HALF], ACT.Square)
+        nc.vector.tensor_tensor(sq[0][:, HALF:], y[0][:, HALF:], y[0][:, HALF:], ALU.mult)
+        nc.sync.dma_start(own_b[0][:], sq[0][:, HALF:])
+        for t in range(1, PACK):
+            bank = psum.tile([P, S], F32, name=f"acc{t}", tag="bank")
+            first(bank[:], t, 0, S, [1, 0])
+            nc.scalar.activation(y[t][:], bank[:], ACT.Relu)
+            nc.scalar.activation(sq[t][:], y[t][:], ACT.Square)
+            nc.scalar.activation(own_a[t][:], y[t][:, :HALF], ACT.Square)
+            nc.sync.dma_start(own_b[t][:], sq[t][:, HALF:])
+
+        w2w = {}
+        w2_cols = w2w_raw[:].rearrange("p (m t b) -> p t m b", t=PACK, b=2)
+
+        def deal_w2(t, pool, **place):
+            w2w[t] = pool.tile([P, 2 * P], U8, name=f"w2w{t}", align_bytes=64, **place)
+            nc.vector.tensor_copy(w2w[t][:].rearrange("p (m b) -> p m b", b=2), w2_cols[:, t])
+
+        deal_w2(0, keep)
+        deal_w2(1, keep)
+
+        root_a = roots.tile([P, PACK, HALF], F32, name="root_a", align_bytes=64, offset=0)
+        root_2 = roots.tile([P, PACK, P], F32, name="root_2", align_bytes=64, offset=4096)
+        root_3 = keep.tile([P, PACK, P], F32, name="root_3")
+        root = [root_a[:, :, :P], root_a[:, :, P:], root_2[:], root_3[:]]
+        gained = [keep.tile([P, PACK, HALF], F32, name=f"gained{h}") for h in range(2)]
+        total_a = [keep.tile([P, HALF], F32, name=f"total_a{t}") for t in range(PACK)]
+        near = {}
+        total = {}
+
+        def fetch1(c, t):
+            near[c, t] = ring.tile([P, P], F32, name=f"near{c}_{t}", tag="near")
+            own = own_a[t] if c < 2 else own_b[t]
+            nc.vector.tensor_tensor(near[c, t][:], sq[t][:].indirect(p1_sb[:, 8 * c : 8 * c + 8]), own[:, (c % 2) * P : (c % 2 + 1) * P], ALU.add)
+
+        def fetch2(c, t):
+            if c < 2:
+                total[c, t] = total_a[t][:, c * P : (c + 1) * P]
+            elif c == 2:
+                total[c, t] = keep.tile([P, P], F32, name=f"total{c}_{t}")[:]
+            else:
+                total[c, t] = roots.tile([P, P], F32, name=f"total{c}_{t}", align_bytes=64, offset=4096 * (t // 2) + 512 * (t % 2))[:]
+            nc.vector.tensor_tensor(total[c, t], sq[t][:].indirect(p2_sb[:, 8 * c : 8 * c + 8]), near[c, t][:], ALU.add)
+
+        def take_root_a(t):
+            nc.scalar.activation(root_a[:, t, :], total_a[t][:], ACT.Abs_reciprocal_sqrt, bias=bias[:], scale=0.5)
+
+        def take_root(c, t):
+            nc.scalar.activation(root[c][:, t, :], total[c, t], ACT.Abs_reciprocal_sqrt, bias=bias[:], scale=0.5)
+
+        def gain(h, t):
+            nc.scalar.activation(gained[h][:, t, :], y[t][:, h * HALF : (h + 1) * HALF], ACT.Copy, scale=gn_sb[:, t : t + 1])
+
+        z_in = {}
+        z_words = {}
+        z_scales = {}
+
+        def normalise(c):
+            z_in[c] = keep.tile([P, P * PACK], BF16, name=f"z_in{c}", align_bytes=64)
+            lo = (c % 2) * P
+            nc.vector.tensor_tensor(
+                z_in[c][:].rearrange("p (c i t) -> p c t i", i=2, t=PACK),
+                gained[c // 2][:, :, lo : lo + P].rearrange("p t (c i) -> p c t i", i=2),
+                root[c].rearrange("p t (c i) -> p c t i", i=2),
+                ALU.mult,
+            )
+
         out_words = keep.tile([P, S], U32, name="out_words", align_bytes=64)
         out_scales = keep.tile([P, S], U8, name="out_scales", align_bytes=64)
+        res_in = [keep.tile([P, P * PACK], BF16, name=f"res_in{c}", align_bytes=64) for c in range(4)]
         out_rows = out_0.rearrange("(p t) j -> p t j", t=PACK)
         out_w = out_1[0].rearrange("p n t -> p (n t)").bitcast(I32)
+        banks = {}
+        res = {}
 
-        def square(t):
-            if t == 0:
-                for h in range(2):
-                    cols = slice(h * 256, (h + 1) * 256)
-                    nc.scalar.activation(y[0][:, cols], halves[h][:, :256], ACT.Relu)
-                    nc.scalar.activation(sq[0][:, cols], y[0][:, cols], ACT.Square)
-                nc.vector.tensor_tensor(own[0][:, :256], y[0][:, :256], y[0][:, :256], ALU.mult)
-                nc.sync.dma_start(own[0][:, 256:], sq[0][:, 256:])
-                return
-            nc.scalar.activation(y[t][:], acc[t][:], ACT.Relu)
-            nc.scalar.activation(sq[t][:], y[t][:], ACT.Square)
-            if not PE_SUM:
-                first = CHUNKS[0]
-                nc.scalar.activation(own[t][:, :first], y[t][:, :first], ACT.Square)
-                nc.sync.dma_start(own[t][:, first:], sq[t][:, first:])
-
-        def fetch(u, c0, n, t):
-            lists = slice(c0 // 16, (c0 + n) // 16)
-            a = near1[:, (u % 2) * widest : (u % 2) * widest + n]
-            b = near2[:, (u % 8) * widest : (u % 8) * widest + n]
-            rs = keep.tile([P, n], F32, name=f"rs{u}")
-            if PE_SUM:
-                nc.vector.tensor_copy(a, sq[t][:].indirect(p1_sb[:, lists]))
-                nc.vector.tensor_copy(b, sq[t][:].indirect(p2_sb[:, lists]))
-                total = psum.tile([P, S], F32, name=f"total{u}", tag="bank")
-                blocks = n // P
-                terms = [sq[t][:, c0 : c0 + n], a, b]
-                for i, term in enumerate(terms):
-                    for k in range(blocks):
-                        nc.tensor.matmul(
-                            total[:, k * P : (k + 1) * P],
-                            term[:, k * P : (k + 1) * P],
-                            ident[:],
-                            start=(i == 0 and k == 0),
-                            stop=(i == 2 and k == blocks - 1),
-                            is_transpose=True,
-                        )
-                nc.scalar.activation(rs[:], total[:, :n], ACT.Abs_reciprocal_sqrt, bias=bias[:], scale=0.5)
-                back = psum.tile([P, S], F32, name=f"back{u}", tag="bank")
-                for k in range(blocks):
-                    nc.tensor.transpose(back[:, k * P : (k + 1) * P], rs[:, k * P : (k + 1) * P], ident[:])
-                return back[:, :n]
-            nc.vector.tensor_tensor(a, sq[t][:].indirect(p1_sb[:, lists]), own[t][:, c0 : c0 + n], ALU.add)
-            nc.vector.tensor_tensor(b, sq[t][:].indirect(p2_sb[:, lists]), a, ALU.add)
-            nc.scalar.activation(rs[:], b, ACT.Abs_reciprocal_sqrt, bias=bias[:], scale=0.5)
-            return rs[:]
-
-        def second(ci, c0, n, z_rows, lo, width):
-            name = f"{ci}_{lo}"
-            z_in = keep.tile([P, width * PACK], BF16, name=f"z_in{name}", align_bytes=64)
-            dst = z_in[:].rearrange("p (c i t) -> p c t i", i=4, t=PACK)
-            src = z_rows[:].rearrange("p (t c i) -> p c t i", i=4, t=PACK)[:, lo // 4 : (lo + width) // 4]
-            if ci in G_ON_VECTOR:
-                nc.vector.tensor_copy(dst, src)
+        def second(c):
+            z_words[c] = keep.tile([P, P], U32, name=f"z_words{c}", align_bytes=64)
+            z_scales[c] = keep.tile([P, P], U8, name=f"z_scales{c}", align_bytes=64)
+            nc.vector.quantize_mx(z_words[c][:].bitcast(FP8X4), z_scales[c][:], z_in[c][:])
+            if c < 3:
+                banks[c] = psum.tile([P, PACK, P], F32, name=f"out{c}", tag="bank")
+                outs = [banks[c][:, t, :] for t in range(PACK)]
             else:
-                nc.scalar.copy(dst, src)
-            z_words = keep.tile([P, width], U32, name=f"z_words{name}", align_bytes=64)
-            z_scales = keep.tile([P, width], U8, name=f"z_scales{name}", align_bytes=64)
-            nc.vector.quantize_mx(z_words[:].bitcast(FP8X4), z_scales[:], z_in[:])
-            res = keep.tile([P, PACK, width], F32, name=f"res{name}")
-            res_in = keep.tile([P, width * PACK], BF16, name=f"res_in{name}", align_bytes=64)
-            for k in range(width // P):
-                cols = slice(k * P, (k + 1) * P)
-                bank = psum.tile([P, PACK, P], F32, name=f"out{name}_{k}", tag="bank")
-                for t in range(PACK):
-                    nc.tensor.matmul_mx(
-                        out=bank[:, t, :],
-                        lhsT=w2w[:, 2 * t * P : 2 * (t + 1) * P].bitcast(FP4X4),
-                        lhsT_scale=w2s[:, t * P : (t + 1) * P],
-                        rhs=z_words[:, cols].bitcast(FP8X4),
-                        rhs_scale=z_scales[:, cols],
-                        start=True,
-                        stop=True,
-                    )
-                dst = res_in[:, k * P * PACK : (k + 1) * P * PACK].rearrange("p (j t) -> p j t", t=PACK)
-                nc.scalar.copy(res[:, :, cols], bank[:])
-                if (c0 + lo) // P + k in O_ON_VECTOR:
-                    nc.vector.tensor_copy(
-                        res_in[:, k * P * PACK : (k + 1) * P * PACK].rearrange("p (c i t) -> p c t i", i=4, t=PACK),
-                        res[:, :, cols].rearrange("p t (c i) -> p c t i", i=4),
-                    )
-                else:
-                    nc.scalar.copy(dst, bank[:].rearrange("p t j -> p j t"))
-            first = c0 + lo
-            nc.vector.quantize_mx(out_words[:, first : first + width].bitcast(FP8X4), out_scales[:, first : first + width], res_in[:])
-            nc.sync.dma_start(out_rows[:, :, first : first + width], res[:])
-            nc.sync.dma_start(out_w[:, first : first + width], out_words[:, first : first + width].bitcast(I32))
-
-        units = []
-        c0 = 0
-        for ci, n in enumerate(CHUNKS):
-            z_rows = keep.tile([P, PACK * n], BF16, name=f"z_rows{ci}")
+                banks[c] = [psum.tile([P, 2, P], F32, name=f"out{c}_{u}", tag="bank") for u in range(2)]
+                outs = [banks[c][t // 2][:, t % 2, :] for t in range(PACK)]
             for t in range(PACK):
-                units.append((ci, c0, n, t, z_rows))
-            c0 = c0 + n
-
-        square(0)
-        square(1)
-        pending = None
-        for u in range(len(units) + 1):
-            got = None
-            if u < len(units):
-                ci, c0, n, t, z_rows = units[u]
-                if u + 2 < PACK:
-                    square(u + 2)
-                got = fetch(u, c0, n, t)
-            if pending is not None:
-                ci, c0, n, t, z_rows = units[u - 1]
-                nc.vector.scalar_tensor_tensor(
-                    z_rows[:, t * n : (t + 1) * n], y[t][:, c0 : c0 + n], gn_sb[:, t : t + 1], pending, ALU.mult, ALU.mult
+                nc.tensor.matmul_mx(
+                    out=outs[t],
+                    lhsT=w2w[t][:].bitcast(FP4X4),
+                    lhsT_scale=w2s[:, t * P : (t + 1) * P],
+                    rhs=z_words[c][:].bitcast(FP8X4),
+                    rhs_scale=z_scales[c][:],
+                    start=True,
+                    stop=True,
                 )
-                if t == PACK - 1:
-                    piece = PIECES[ci]
-                    for lo in range(0, n, piece):
-                        second(ci, c0, n, z_rows, lo, piece)
-            pending = got
+
+        def empty(c):
+            res[c] = keep.tile([P, PACK, P], F32, name=f"res{c}")
+            if c < 3:
+                nc.scalar.copy(res[c][:], banks[c][:])
+            else:
+                for u in range(2):
+                    nc.scalar.copy(res[c][:, 2 * u : 2 * u + 2, :], banks[c][u][:])
+            nc.sync.dma_start(out_rows[:, :, c * P : (c + 1) * P], res[c][:])
+
+        def round_scalar(c):
+            nc.scalar.copy(res_in[c][:].rearrange("p (j t) -> p j t", t=PACK), banks[c][:].rearrange("p t j -> p j t"))
+
+        def round_vector(c, lo, n):
+            nc.vector.tensor_copy(
+                res_in[c][:, lo * PACK : (lo + n) * PACK].rearrange("p (c i t) -> p c t i", i=2, t=PACK),
+                res[c][:, :, lo : lo + n].rearrange("p t (c i) -> p c t i", i=2),
+            )
+
+        def planes(c):
+            cols = slice(c * P, (c + 1) * P)
+            nc.vector.quantize_mx(out_words[:, cols].bitcast(FP8X4), out_scales[:, cols], res_in[c][:])
+
+        def store_words(queue, lo, n):
+            queue.dma_start(out_w[:, lo : lo + n], out_words[:, lo : lo + n].bitcast(I32))
+
+        for t in range(PACK):
+            fetch1(0, t)
+            fetch1(1, t)
+            if t < 2:
+                deal_w2(2 + t, owns, offset=1024 * t)
+            if t == 2:
+                w2s = owns.tile([P, N], U8, name="w2s", align_bytes=64, offset=1024 * t)
+                deal_scales(nc, w2s[:], w2s_raw[:])
+            fetch2(0, t)
+            fetch2(1, t)
+        for t in range(PACK - 1):
+            take_root_a(t)
+        for t in range(PACK):
+            gain(0, t)
+        take_root_a(PACK - 1)
+        for t in range(PACK):
+            gain(1, t)
+
+        fetch1(2, 0)
+        fetch1(2, 1)
+        fetch2(2, 0)
+        take_root(2, 0)
+        fetch1(2, 2)
+        fetch2(2, 1)
+        take_root(2, 1)
+        normalise(0)
+        fetch2(2, 2)
+        take_root(2, 2)
+        second(0)
+        fetch1(2, 3)
+        normalise(1)
+        fetch2(2, 3)
+        take_root(2, 3)
+        second(1)
+        fetch1(3, 0)
+        fetch1(3, 1)
+        empty(0)
+        round_scalar(0)
+        fetch2(3, 0)
+        normalise(2)
+        fetch2(3, 1)
+        second(2)
+        take_root(3, 0)
+        take_root(3, 1)
+        empty(1)
+        round_scalar(1)
+        fetch1(3, 2)
+        fetch1(3, 3)
+        fetch2(3, 2)
+        take_root(3, 2)
+        fetch2(3, 3)
+        take_root(3, 3)
+        planes(0)
+        normalise(3)
+        empty(2)
+        round_scalar(2)
+        planes(1)
+        second(3)
+        planes(2)
+        store_words(nc.sync, 0, 3 * P)
+        empty(3)
+        round_vector(3, 0, P)
+        planes(3)
+        store_words(nc.scalar, 3 * P, P)
 
         for q in range(4):
             queue = nc.sync if q % 2 == 0 else nc.scalar

@@ -42,8 +42,8 @@ def tile_picked_lrn8_relu_po_kernel(tc, x_words, x_scales, w1_words, w1_scales, 
         keep = ctx.enter_context(tc.tile_pool(name="keep", bufs=1))
         later = ctx.enter_context(tc.tile_pool(name="later", bufs=1))
         owns = ctx.enter_context(tc.tile_pool(name="owns", bufs=1))
+        spent = ctx.enter_context(tc.tile_pool(name="spent", bufs=1))
         roots = ctx.enter_context(tc.tile_pool(name="roots", bufs=1))
-        ring = ctx.enter_context(tc.tile_pool(name="ring", bufs=3))
         psum = ctx.enter_context(tc.psum_pool(name="psum", bufs=8))
 
         offs_sb = keep.tile([P, S // 16], U16, name="offs_sb")
@@ -51,17 +51,19 @@ def tile_picked_lrn8_relu_po_kernel(tc, x_words, x_scales, w1_words, w1_scales, 
         p2_sb = keep.tile([P, S // 16], U16, name="p2_sb")
 
         xs_raw = keep.tile([P, T], U8, name="xs_raw", align_bytes=64)
+        w2w_raw = keep.tile([P, 2 * N], U8, name="w2w_raw", align_bytes=64)
+        w2w = keep.tile([P, 2 * N], U8, name="w2w", align_bytes=64)
         xs_got = keep.tile([P, S], U8, name="xs_got", align_bytes=64)
         w1s_raw = keep.tile([P, H], U8, name="w1s_raw", align_bytes=64)
         flat = keep.tile([P, S + H], U8, name="flat", align_bytes=64)
-        planes1 = keep.tile([P, PASSES * (S + H)], U8, name="planes1", align_bytes=64)
-        w1w_raw = keep.tile([P, PASSES * 2 * H], U8, name="w1w_raw", align_bytes=64)
-        w1w = keep.tile([P, PASSES * 2 * H], U8, name="w1w", align_bytes=64)
+        planes1 = spent.tile([P, PASSES * (S + H)], U8, name="planes1", align_bytes=64, offset=8192)
+        w1w_raw = spent.tile([P, PASSES * 2 * H], U8, name="w1w_raw", align_bytes=64, offset=4096)
+        w1w = spent.tile([P, PASSES * 2 * H], U8, name="w1w", align_bytes=64, offset=6144)
         xw_raw = [
             later.tile([P, T], U32, name="xw_raw0", align_bytes=64, offset=0),
             keep.tile([P, T], U32, name="xw_raw1", align_bytes=64),
         ]
-        xw = [keep.tile([P, S], U32, name=f"xw{z}", align_bytes=64) for z in range(PASSES)]
+        xw = [spent.tile([P, S], U32, name=f"xw{z}", align_bytes=64, offset=2048 * z) for z in range(PASSES)]
         ones = keep.tile([P, 1], F32, name="ones")
         bias = keep.tile([P, 1], F32, name="bias")
 
@@ -81,12 +83,13 @@ def tile_picked_lrn8_relu_po_kernel(tc, x_words, x_scales, w1_words, w1_scales, 
             w1w_raw[:].bitcast(I32).rearrange("p (z c) -> p z c", z=PASSES),
             w1_words.bitcast(I32).rearrange("z p c -> p z c"),
         )
+        nc.sync.dma_start(w2w_raw[:].bitcast(I32), w2_words[0].bitcast(I32))
         for z in range(PASSES):
             nc.sync.dma_start(xw_raw[z][:].bitcast(I32), x_words[z].rearrange("p n t -> p (n t)").bitcast(I32))
         nc.scalar.activation(bias[:], ones[:], ACT.Abs_reciprocal_sqrt)
 
-        deal_scales(nc, flat[:, S:], w1s_raw[:])
         nc.vector.tensor_copy(xs_got[:], xs_raw[:].indirect(offs_sb[:]))
+        deal_scales(nc, flat[:, S:], w1s_raw[:])
         nc.vector.tensor_copy(flat[:, :S].bitcast(I32), xs_got[:].bitcast(I32))
         for q in range(4):
             nc.scalar.dma_start(
@@ -98,10 +101,9 @@ def tile_picked_lrn8_relu_po_kernel(tc, x_words, x_scales, w1_words, w1_scales, 
         for h in range(2):
             nc.vector.tensor_copy(xw[1][:, h * HALF : (h + 1) * HALF], xw_raw[1][:].indirect(offs_sb[:, h * 16 : (h + 1) * 16]))
 
-        w2w_raw = later.tile([P, 2 * N], U8, name="w2w_raw", align_bytes=64, offset=0)
+        deal_words(nc, w2w[:], w2w_raw[:])
         w2s_raw = later.tile([P, N], U8, name="w2s_raw", align_bytes=64, offset=2 * N)
         gn_sb = later.tile([P, PACK], F32, name="gn_sb", align_bytes=64, offset=3 * N)
-        nc.sync.dma_start(w2w_raw[:].bitcast(I32), w2_words[0].bitcast(I32))
         nc.sync.dma_start(gn_sb[:], gn.rearrange("(p t) o -> p (t o)", t=PACK))
         nc.gpsimd.memset(w2s_raw[:].bitcast(I32), 0)
         for q in range(4):
@@ -123,66 +125,70 @@ def tile_picked_lrn8_relu_po_kernel(tc, x_words, x_scales, w1_words, w1_scales, 
         y = [keep.tile([P, S], F32, name=f"y{t}") for t in range(PACK)]
         sq = [keep.tile([P, S], F32, name=f"sq{t}") for t in range(PACK)]
         own_a = [owns.tile([P, HALF], F32, name=f"own_a{t}", align_bytes=64, offset=1024 * t) for t in range(PACK)]
-        own_b = [keep.tile([P, HALF], F32, name=f"own_b{t}") for t in range(PACK)]
+        own_b = [owns.tile([P, HALF], F32, name=f"own_b{t}", align_bytes=64, offset=1024 * (PACK + t)) for t in range(PACK)]
 
         for k in range(S // P):
             cols = slice(k * P, (k + 1) * P)
             bank = psum.tile([P, P], F32, name=f"acc0_{k}", tag="bank")
             first(bank[:], 0, k * P, P, [0, 1])
-            if k < 2:
+            if k < 3:
                 nc.scalar.activation(y[0][:, cols], bank[:], ACT.Relu)
             else:
                 nc.vector.tensor_scalar_max(y[0][:, cols], bank[:], 0.0)
-        nc.scalar.activation(sq[0][:, :HALF], y[0][:, :HALF], ACT.Square)
-        nc.scalar.activation(own_a[0][:], y[0][:, :HALF], ACT.Square)
-        nc.vector.tensor_tensor(sq[0][:, HALF:], y[0][:, HALF:], y[0][:, HALF:], ALU.mult)
+        for k in range(S // P):
+            cols = slice(k * P, (k + 1) * P)
+            if k < 2:
+                nc.vector.tensor_tensor(sq[0][:, cols], y[0][:, cols], y[0][:, cols], ALU.mult)
+            else:
+                nc.scalar.activation(sq[0][:, cols], y[0][:, cols], ACT.Square)
+        for k in range(2):
+            cols = slice(k * P, (k + 1) * P)
+            nc.vector.tensor_copy(own_a[0][:, cols], sq[0][:, cols])
         nc.sync.dma_start(own_b[0][:], sq[0][:, HALF:])
         for t in range(1, PACK):
             bank = psum.tile([P, S], F32, name=f"acc{t}", tag="bank")
-            first(bank[:], t, 0, S, [1, 0])
+            first(bank[:], t, 0, S, [0, 1] if t == 1 else [1, 0])
             nc.scalar.activation(y[t][:], bank[:], ACT.Relu)
             nc.scalar.activation(sq[t][:], y[t][:], ACT.Square)
             nc.scalar.activation(own_a[t][:], y[t][:, :HALF], ACT.Square)
             nc.sync.dma_start(own_b[t][:], sq[t][:, HALF:])
 
-        w2w = {}
-        w2_cols = w2w_raw[:].rearrange("p (m t b) -> p t m b", t=PACK, b=2)
-
-        def deal_w2(t, pool, **place):
-            w2w[t] = pool.tile([P, 2 * P], U8, name=f"w2w{t}", align_bytes=64, **place)
-            nc.vector.tensor_copy(w2w[t][:].rearrange("p (m b) -> p m b", b=2), w2_cols[:, t])
-
-        deal_w2(0, keep)
-        deal_w2(1, keep)
-
-        root_a = roots.tile([P, PACK, HALF], F32, name="root_a", align_bytes=64, offset=0)
-        root_2 = roots.tile([P, PACK, P], F32, name="root_2", align_bytes=64, offset=4096)
+        root_a = spent.tile([P, PACK, HALF], F32, name="root_a", align_bytes=64, offset=0)
+        root_2 = roots.tile([P, PACK, P], F32, name="root_2", align_bytes=64, offset=0)
         root_3 = keep.tile([P, PACK, P], F32, name="root_3")
         root = [root_a[:, :, :P], root_a[:, :, P:], root_2[:], root_3[:]]
-        gained = [keep.tile([P, PACK, HALF], F32, name=f"gained{h}") for h in range(2)]
+        gained = [spent.tile([P, PACK, HALF], F32, name=f"gained{h}", align_bytes=64, offset=4096 * (h + 1)) for h in range(2)]
         total_a = [keep.tile([P, HALF], F32, name=f"total_a{t}") for t in range(PACK)]
         near = {}
         total = {}
 
         def fetch1(c, t):
-            near[c, t] = ring.tile([P, P], F32, name=f"near{c}_{t}", tag="near")
-            own = own_a[t] if c < 2 else own_b[t]
-            nc.vector.tensor_tensor(near[c, t][:], sq[t][:].indirect(p1_sb[:, 8 * c : 8 * c + 8]), own[:, (c % 2) * P : (c % 2 + 1) * P], ALU.add)
+            near[c, t] = owns.tile([P, P], F32, name=f"near{c}_{t}", align_bytes=64, offset=1024 * (8 + t % 2) + 512 * c)[:]
+            nc.vector.tensor_tensor(near[c, t], sq[t][:].indirect(p1_sb[:, 8 * c : 8 * c + 8]), own_a[t][:, c * P : (c + 1) * P], ALU.add)
+
+        def fetch1_b(t, pool, place):
+            both = pool.tile([P, HALF], F32, name=f"near_b{t}", align_bytes=64, offset=place)
+            near[2, t] = both[:, :P]
+            near[3, t] = both[:, P:]
+            nc.vector.tensor_tensor(both[:], sq[t][:].indirect(p1_sb[:, 16:32]), own_b[t][:], ALU.add)
 
         def fetch2(c, t):
             if c < 2:
                 total[c, t] = total_a[t][:, c * P : (c + 1) * P]
             elif c == 2:
-                total[c, t] = keep.tile([P, P], F32, name=f"total{c}_{t}")[:]
+                if t < 2:
+                    total[c, t] = owns.tile([P, P], F32, name=f"total{c}_{t}", align_bytes=64, offset=1024 * 10 + 1536 * t)[:]
+                else:
+                    total[c, t] = keep.tile([P, P], F32, name=f"total{c}_{t}")[:]
             else:
-                total[c, t] = roots.tile([P, P], F32, name=f"total{c}_{t}", align_bytes=64, offset=4096 * (t // 2) + 512 * (t % 2))[:]
-            nc.vector.tensor_tensor(total[c, t], sq[t][:].indirect(p2_sb[:, 8 * c : 8 * c + 8]), near[c, t][:], ALU.add)
+                total[c, t] = spent.tile([P, P], F32, name=f"total{c}_{t}", align_bytes=64, offset=512 * t)[:]
+            nc.vector.tensor_tensor(total[c, t], sq[t][:].indirect(p2_sb[:, 8 * c : 8 * c + 8]), near[c, t], ALU.add)
 
         def take_root_a(t):
-            nc.scalar.activation(root_a[:, t, :], total_a[t][:], ACT.Abs_reciprocal_sqrt, bias=bias[:], scale=0.5)
+            nc.scalar.activation(root_a[:, t, :], total_a[t][:], ACT.Abs_reciprocal_sqrt, bias=bias[:] if t == 0 else 1.0, scale=0.5)
 
         def take_root(c, t):
-            nc.scalar.activation(root[c][:, t, :], total[c, t], ACT.Abs_reciprocal_sqrt, bias=bias[:], scale=0.5)
+            nc.scalar.activation(root[c][:, t, :], total[c, t], ACT.Abs_reciprocal_sqrt, bias=1.0, scale=0.5)
 
         def gain(h, t):
             nc.scalar.activation(gained[h][:, t, :], y[t][:, h * HALF : (h + 1) * HALF], ACT.Copy, scale=gn_sb[:, t : t + 1])
@@ -192,7 +198,7 @@ def tile_picked_lrn8_relu_po_kernel(tc, x_words, x_scales, w1_words, w1_scales, 
         z_scales = {}
 
         def normalise(c):
-            z_in[c] = keep.tile([P, P * PACK], BF16, name=f"z_in{c}", align_bytes=64)
+            z_in[c] = owns.tile([P, P * PACK], BF16, name=f"z_in{c}", align_bytes=64, offset=1024 * (10 + c))
             lo = (c % 2) * P
             nc.vector.tensor_tensor(
                 z_in[c][:].rearrange("p (c i t) -> p c t i", i=2, t=PACK),
@@ -203,7 +209,8 @@ def tile_picked_lrn8_relu_po_kernel(tc, x_words, x_scales, w1_words, w1_scales, 
 
         out_words = keep.tile([P, S], U32, name="out_words", align_bytes=64)
         out_scales = keep.tile([P, S], U8, name="out_scales", align_bytes=64)
-        res_in = [keep.tile([P, P * PACK], BF16, name=f"res_in{c}", align_bytes=64) for c in range(4)]
+        res_ab = [keep.tile([P, HALF * PACK], BF16, name=f"res_in{h}", align_bytes=64) for h in range(2)]
+        res_in = [res_ab[c // 2][:, (c % 2) * P * PACK : (c % 2 + 1) * P * PACK] for c in range(4)]
         out_rows = out_0.rearrange("(p t) j -> p t j", t=PACK)
         out_w = out_1[0].rearrange("p n t -> p (n t)").bitcast(I32)
         banks = {}
@@ -222,7 +229,7 @@ def tile_picked_lrn8_relu_po_kernel(tc, x_words, x_scales, w1_words, w1_scales, 
             for t in range(PACK):
                 nc.tensor.matmul_mx(
                     out=outs[t],
-                    lhsT=w2w[t][:].bitcast(FP4X4),
+                    lhsT=w2w[:, 2 * t * P : 2 * (t + 1) * P].bitcast(FP4X4),
                     lhsT_scale=w2s[:, t * P : (t + 1) * P],
                     rhs=z_words[c][:].bitcast(FP8X4),
                     rhs_scale=z_scales[c][:],
@@ -232,15 +239,20 @@ def tile_picked_lrn8_relu_po_kernel(tc, x_words, x_scales, w1_words, w1_scales, 
 
         def empty(c):
             res[c] = keep.tile([P, PACK, P], F32, name=f"res{c}")
-            if c < 3:
-                nc.scalar.copy(res[c][:], banks[c][:])
-            else:
-                for u in range(2):
-                    nc.scalar.copy(res[c][:, 2 * u : 2 * u + 2, :], banks[c][u][:])
+            nc.scalar.copy(res[c][:], banks[c][:])
             nc.sync.dma_start(out_rows[:, :, c * P : (c + 1) * P], res[c][:])
 
+        def empty_last(u):
+            pair = keep.tile([P, 2, P], F32, name=f"pair{u}")
+            nc.vector.tensor_copy(
+                res_in[3].rearrange("p (j u e) -> p u j e", u=2, e=2)[:, u],
+                banks[3][u][:].rearrange("p e j -> p j e"),
+            )
+            nc.scalar.copy(pair[:], banks[3][u][:])
+            nc.sync.dma_start(out_rows[:, 2 * u : 2 * u + 2, 3 * P :], pair[:])
+
         def round_scalar(c):
-            nc.scalar.copy(res_in[c][:].rearrange("p (j t) -> p j t", t=PACK), banks[c][:].rearrange("p t j -> p j t"))
+            nc.scalar.copy(res_in[c].rearrange("p (j t) -> p j t", t=PACK), banks[c][:].rearrange("p t j -> p j t"))
 
         def round_vector(c, lo, n):
             nc.vector.tensor_copy(
@@ -248,9 +260,9 @@ def tile_picked_lrn8_relu_po_kernel(tc, x_words, x_scales, w1_words, w1_scales, 
                 res[c][:, :, lo : lo + n].rearrange("p t (c i) -> p c t i", i=2),
             )
 
-        def planes(c):
-            cols = slice(c * P, (c + 1) * P)
-            nc.vector.quantize_mx(out_words[:, cols].bitcast(FP8X4), out_scales[:, cols], res_in[c][:])
+        def planes(h):
+            cols = slice(h * HALF, (h + 1) * HALF)
+            nc.vector.quantize_mx(out_words[:, cols].bitcast(FP8X4), out_scales[:, cols], res_ab[h][:])
 
         def store_words(queue, lo, n):
             queue.dma_start(out_w[:, lo : lo + n], out_words[:, lo : lo + n].bitcast(I32))
@@ -258,13 +270,11 @@ def tile_picked_lrn8_relu_po_kernel(tc, x_words, x_scales, w1_words, w1_scales, 
         for t in range(PACK):
             fetch1(0, t)
             fetch1(1, t)
-            if t < 2:
-                deal_w2(2 + t, owns, offset=1024 * t)
-            if t == 2:
-                w2s = owns.tile([P, N], U8, name="w2s", align_bytes=64, offset=1024 * t)
-                deal_scales(nc, w2s[:], w2s_raw[:])
             fetch2(0, t)
             fetch2(1, t)
+            if t == 0:
+                w2s = owns.tile([P, N], U8, name="w2s", align_bytes=64, offset=1024 * t)
+                deal_scales(nc, w2s[:], w2s_raw[:])
         for t in range(PACK - 1):
             take_root_a(t)
         for t in range(PACK):
@@ -273,52 +283,41 @@ def tile_picked_lrn8_relu_po_kernel(tc, x_words, x_scales, w1_words, w1_scales, 
         for t in range(PACK):
             gain(1, t)
 
-        fetch1(2, 0)
-        fetch1(2, 1)
-        fetch2(2, 0)
-        take_root(2, 0)
-        fetch1(2, 2)
-        fetch2(2, 1)
-        take_root(2, 1)
+        fetch1_b(0, owns, 1024 * 3)
+        fetch1_b(1, owns, 1024 * 9 - 512)
         normalise(0)
-        fetch2(2, 2)
-        take_root(2, 2)
-        second(0)
-        fetch1(2, 3)
         normalise(1)
-        fetch2(2, 3)
-        take_root(2, 3)
+        second(0)
         second(1)
-        fetch1(3, 0)
-        fetch1(3, 1)
+        fetch2(2, 0)
+        fetch2(2, 1)
+        fetch1_b(2, owns, 1024 * 10 + 512)
+        fetch1_b(3, spent, 2048)
         empty(0)
         round_scalar(0)
-        fetch2(3, 0)
-        normalise(2)
-        fetch2(3, 1)
-        second(2)
-        take_root(3, 0)
-        take_root(3, 1)
+        take_root(2, 0)
+        take_root(2, 1)
         empty(1)
+        fetch2(2, 2)
+        take_root(2, 2)
+        fetch2(2, 3)
+        take_root(2, 3)
         round_scalar(1)
-        fetch1(3, 2)
-        fetch1(3, 3)
-        fetch2(3, 2)
-        take_root(3, 2)
-        fetch2(3, 3)
-        take_root(3, 3)
+        for t in range(PACK):
+            fetch2(3, t)
+            take_root(3, t)
+        normalise(2)
         planes(0)
+        store_words(nc.sync, 0, HALF)
+        second(2)
         normalise(3)
-        empty(2)
-        round_scalar(2)
-        planes(1)
         second(3)
-        planes(2)
-        store_words(nc.sync, 0, 3 * P)
-        empty(3)
-        round_vector(3, 0, P)
-        planes(3)
-        store_words(nc.scalar, 3 * P, P)
+        round_scalar(2)
+        empty(2)
+        empty_last(0)
+        empty_last(1)
+        planes(1)
+        store_words(nc.scalar, HALF, HALF)
 
         for q in range(4):
             queue = nc.sync if q % 2 == 0 else nc.scalar

@@ -68,10 +68,10 @@ def tile_picked_lrn8_relu_po_kernel(tc, x_words, x_scales, w1_words, w1_scales, 
         bias = keep.tile([P, 1], F32, name="bias")
 
         nc.vector.memset(ones[:], 1.0)
+        nc.vector.memset(xs_raw[32:64, :].bitcast(I32), 0)
+        nc.vector.memset(xs_raw[64:128, :].bitcast(I32), 0)
         nc.vector.memset(w1s_raw[32:64, :].bitcast(I32), 0)
         nc.vector.memset(w1s_raw[64:128, :].bitcast(I32), 0)
-        nc.vector.memset(xs_raw[32:64, :].bitcast(I32), 0)
-        nc.gpsimd.memset(xs_raw[64:128, :].bitcast(I32), 0)
         nc.gpsimd.memset(planes1[:].bitcast(I32), 0)
 
         nc.sync.dma_start(offs_sb[:], offs)
@@ -201,9 +201,9 @@ def tile_picked_lrn8_relu_po_kernel(tc, x_words, x_scales, w1_words, w1_scales, 
             z_in[c] = owns.tile([P, P * PACK], BF16, name=f"z_in{c}", align_bytes=64, offset=1024 * (10 + c))
             lo = (c % 2) * P
             nc.vector.tensor_tensor(
-                z_in[c][:].rearrange("p (c i t) -> p c t i", i=2, t=PACK),
-                gained[c // 2][:, :, lo : lo + P].rearrange("p t (c i) -> p c t i", i=2),
-                root[c].rearrange("p t (c i) -> p c t i", i=2),
+                z_in[c][:].rearrange("p (c i t) -> p c t i", i=4, t=PACK),
+                gained[c // 2][:, :, lo : lo + P].rearrange("p t (c i) -> p c t i", i=4),
+                root[c].rearrange("p t (c i) -> p c t i", i=4),
                 ALU.mult,
             )
 
@@ -256,8 +256,8 @@ def tile_picked_lrn8_relu_po_kernel(tc, x_words, x_scales, w1_words, w1_scales, 
 
         def round_vector(c, lo, n):
             nc.vector.tensor_copy(
-                res_in[c][:, lo * PACK : (lo + n) * PACK].rearrange("p (c i t) -> p c t i", i=2, t=PACK),
-                res[c][:, :, lo : lo + n].rearrange("p t (c i) -> p c t i", i=2),
+                res_in[c][:, lo * PACK : (lo + n) * PACK].rearrange("p (c i t) -> p c t i", i=4, t=PACK),
+                res[c][:, :, lo : lo + n].rearrange("p t (c i) -> p c t i", i=4),
             )
 
         def planes(h):

@@ -24,8 +24,8 @@ HALF = S // 2
 
 def deal_words(nc, dealt, raw):
     nc.vector.tensor_copy(
-        out=dealt.rearrange("p (t c m b) -> p c t m b", t=PACK, m=8, b=2),
-        in_=raw.rearrange("p (c m t b) -> p c t m b", t=PACK, m=8, b=2),
+        out=dealt.bitcast(U16).rearrange("p (t c m) -> p c t m", t=PACK, m=8),
+        in_=raw.bitcast(U16).rearrange("p (c m t) -> p c t m", t=PACK, m=8),
     )
 
 
@@ -55,6 +55,9 @@ def tile_picked_lrn8_relu_po_kernel(tc, x_words, x_scales, w1_words, w1_scales, 
         w2w = keep.tile([P, 2 * N], U8, name="w2w", align_bytes=64)
         xs_got = keep.tile([P, S], U8, name="xs_got", align_bytes=64)
         w1s_raw = keep.tile([P, H], U8, name="w1s_raw", align_bytes=64)
+        w2s_raw = keep.tile([P, N], U8, name="w2s_raw", align_bytes=64)
+        w2s_flat = keep.tile([P, N], U8, name="w2s_flat", align_bytes=64)
+        w2s = keep.tile([P, N], U8, name="w2s", align_bytes=64)
         flat = keep.tile([P, S + H], U8, name="flat", align_bytes=64)
         planes1 = spent.tile([P, PASSES * (S + H)], U8, name="planes1", align_bytes=64, offset=8192)
         w1w_raw = spent.tile([P, PASSES * 2 * H], U8, name="w1w_raw", align_bytes=64, offset=4096)
@@ -72,13 +75,15 @@ def tile_picked_lrn8_relu_po_kernel(tc, x_words, x_scales, w1_words, w1_scales, 
         nc.vector.memset(xs_raw[64:128, :].bitcast(I32), 0)
         nc.vector.memset(w1s_raw[32:64, :].bitcast(I32), 0)
         nc.vector.memset(w1s_raw[64:128, :].bitcast(I32), 0)
+        nc.vector.memset(w2s_raw[32:64, :].bitcast(I32), 0)
+        nc.vector.memset(w2s_raw[64:128, :].bitcast(I32), 0)
         nc.gpsimd.memset(planes1[:].bitcast(I32), 0)
+        nc.gpsimd.memset(w2s[:].bitcast(I32), 0)
 
         nc.sync.dma_start(offs_sb[:], offs)
         nc.sync.dma_start(xs_raw[0:32, :].bitcast(I32), x_scales.bitcast(I32).rearrange("z r c -> r z c"))
         nc.sync.dma_start(w1s_raw[0:32, :].bitcast(I32), w1_scales.bitcast(I32).rearrange("z r c -> r z c"))
-        nc.sync.dma_start(p1_sb[:], p1)
-        nc.sync.dma_start(p2_sb[:], p2)
+        nc.sync.dma_start(w2s_raw[0:32, :].bitcast(I32), w2_scales.bitcast(I32).rearrange("z r c -> r z c").to_broadcast([16, 2, N // 4]))
         nc.sync.dma_start(
             w1w_raw[:].bitcast(I32).rearrange("p (z c) -> p z c", z=PASSES),
             w1_words.bitcast(I32).rearrange("z p c -> p z c"),
@@ -86,6 +91,8 @@ def tile_picked_lrn8_relu_po_kernel(tc, x_words, x_scales, w1_words, w1_scales, 
         nc.sync.dma_start(w2w_raw[:].bitcast(I32), w2_words[0].bitcast(I32))
         for z in range(PASSES):
             nc.sync.dma_start(xw_raw[z][:].bitcast(I32), x_words[z].rearrange("p n t -> p (n t)").bitcast(I32))
+        nc.sync.dma_start(p1_sb[:], p1)
+        nc.sync.dma_start(p2_sb[:], p2)
         nc.scalar.activation(bias[:], ones[:], ACT.Abs_reciprocal_sqrt)
 
         nc.vector.tensor_copy(xs_got[:], xs_raw[:].indirect(offs_sb[:]))
@@ -98,16 +105,15 @@ def tile_picked_lrn8_relu_po_kernel(tc, x_words, x_scales, w1_words, w1_scales, 
             )
         deal_words(nc, w1w[:], w1w_raw[:])
         nc.vector.tensor_copy(xw[0][:], xw_raw[0][:].indirect(offs_sb[:]))
+        deal_scales(nc, w2s_flat[:], w2s_raw[:])
         for h in range(2):
             nc.vector.tensor_copy(xw[1][:, h * HALF : (h + 1) * HALF], xw_raw[1][:].indirect(offs_sb[:, h * 16 : (h + 1) * 16]))
 
         deal_words(nc, w2w[:], w2w_raw[:])
-        w2s_raw = later.tile([P, N], U8, name="w2s_raw", align_bytes=64, offset=2 * N)
         gn_sb = later.tile([P, PACK], F32, name="gn_sb", align_bytes=64, offset=3 * N)
         nc.sync.dma_start(gn_sb[:], gn.rearrange("(p t) o -> p (t o)", t=PACK))
-        nc.gpsimd.memset(w2s_raw[:].bitcast(I32), 0)
         for q in range(4):
-            nc.sync.dma_start(w2s_raw[32 * q : 32 * q + 4, :].bitcast(I32), w2_scales[0, 4 * q : 4 * q + 4, :].bitcast(I32))
+            nc.sync.dma_start(w2s[32 * q : 32 * q + 4, :].bitcast(I32), w2s_flat[8 * q : 8 * q + 8 : 2, :].bitcast(I32))
 
         def first(bank, t, lo, width, order):
             for z in order:
@@ -124,103 +130,76 @@ def tile_picked_lrn8_relu_po_kernel(tc, x_words, x_scales, w1_words, w1_scales, 
 
         y = [keep.tile([P, S], F32, name=f"y{t}") for t in range(PACK)]
         sq = [keep.tile([P, S], F32, name=f"sq{t}") for t in range(PACK)]
-        own_a = [owns.tile([P, HALF], F32, name=f"own_a{t}", align_bytes=64, offset=1024 * t) for t in range(PACK)]
-        own_b = [owns.tile([P, HALF], F32, name=f"own_b{t}", align_bytes=64, offset=1024 * (PACK + t)) for t in range(PACK)]
+        own = [owns.tile([P, S], F32, name=f"own{t}", align_bytes=64, offset=2048 * t) for t in range(PACK)]
 
         for k in range(S // P):
             cols = slice(k * P, (k + 1) * P)
             bank = psum.tile([P, P], F32, name=f"acc0_{k}", tag="bank")
             first(bank[:], 0, k * P, P, [0, 1])
-            if k < 3:
+            if k < 2:
                 nc.scalar.activation(y[0][:, cols], bank[:], ACT.Relu)
             else:
                 nc.vector.tensor_scalar_max(y[0][:, cols], bank[:], 0.0)
-        for k in range(S // P):
-            cols = slice(k * P, (k + 1) * P)
-            if k < 2:
-                nc.vector.tensor_tensor(sq[0][:, cols], y[0][:, cols], y[0][:, cols], ALU.mult)
-            else:
+            if k == 1:
+                nc.scalar.activation(sq[0][:, :HALF], y[0][:, :HALF], ACT.Square)
+            if k > 1:
                 nc.scalar.activation(sq[0][:, cols], y[0][:, cols], ACT.Square)
-        for k in range(2):
-            cols = slice(k * P, (k + 1) * P)
-            nc.vector.tensor_copy(own_a[0][:, cols], sq[0][:, cols])
-        nc.sync.dma_start(own_b[0][:], sq[0][:, HALF:])
+        nc.vector.tensor_copy(own[0][:, :HALF], sq[0][:, :HALF])
+        nc.vector.tensor_tensor(own[0][:, HALF:], y[0][:, HALF:], y[0][:, HALF:], ALU.mult)
         for t in range(1, PACK):
             bank = psum.tile([P, S], F32, name=f"acc{t}", tag="bank")
-            first(bank[:], t, 0, S, [0, 1] if t == 1 else [1, 0])
+            first(bank[:], t, 0, S, [1, 0])
             nc.scalar.activation(y[t][:], bank[:], ACT.Relu)
+            if t < PACK - 1:
+                nc.scalar.activation(own[t][:], y[t][:], ACT.Square)
             nc.scalar.activation(sq[t][:], y[t][:], ACT.Square)
-            nc.scalar.activation(own_a[t][:], y[t][:, :HALF], ACT.Square)
-            nc.sync.dma_start(own_b[t][:], sq[t][:, HALF:])
+        nc.sync.dma_start(own[PACK - 1][:], sq[PACK - 1][:])
 
-        root_a = spent.tile([P, PACK, HALF], F32, name="root_a", align_bytes=64, offset=0)
-        root_2 = roots.tile([P, PACK, P], F32, name="root_2", align_bytes=64, offset=0)
-        root_3 = keep.tile([P, PACK, P], F32, name="root_3")
-        root = [root_a[:, :, :P], root_a[:, :, P:], root_2[:], root_3[:]]
-        gained = [spent.tile([P, PACK, HALF], F32, name=f"gained{h}", align_bytes=64, offset=4096 * (h + 1)) for h in range(2)]
-        total_a = [keep.tile([P, HALF], F32, name=f"total_a{t}") for t in range(PACK)]
-        near = {}
-        total = {}
+        gained = spent.tile([P, PACK, S], F32, name="gained", align_bytes=64, offset=0)
+        root_a = spent.tile([P, PACK, HALF], F32, name="root_a", align_bytes=64, offset=8192)
+        total = keep.tile([P, PACK - 1, S], F32, name="total")
+        near = [keep.tile([P, S], F32, name=f"near{t}") for t in range(PACK - 1)]
+        last = PACK - 1
 
-        def fetch1(c, t):
-            near[c, t] = owns.tile([P, P], F32, name=f"near{c}_{t}", align_bytes=64, offset=1024 * (8 + t % 2) + 512 * c)[:]
-            nc.vector.tensor_tensor(near[c, t], sq[t][:].indirect(p1_sb[:, 8 * c : 8 * c + 8]), own_a[t][:, c * P : (c + 1) * P], ALU.add)
+        def offsets(table, lo, n):
+            return table[:, lo // 16 : (lo + n) // 16]
 
-        def fetch1_b(t, pool, place):
-            both = pool.tile([P, HALF], F32, name=f"near_b{t}", align_bytes=64, offset=place)
-            near[2, t] = both[:, :P]
-            near[3, t] = both[:, P:]
-            nc.vector.tensor_tensor(both[:], sq[t][:].indirect(p1_sb[:, 16:32]), own_b[t][:], ALU.add)
+        def fetch1(out, t, lo, n):
+            nc.vector.tensor_tensor(out, sq[t][:].indirect(offsets(p1_sb, lo, n)), own[t][:, lo : lo + n], ALU.add)
 
-        def fetch2(c, t):
-            if c < 2:
-                total[c, t] = total_a[t][:, c * P : (c + 1) * P]
-            elif c == 2:
-                if t < 2:
-                    total[c, t] = owns.tile([P, P], F32, name=f"total{c}_{t}", align_bytes=64, offset=1024 * 10 + 1536 * t)[:]
-                else:
-                    total[c, t] = keep.tile([P, P], F32, name=f"total{c}_{t}")[:]
-            else:
-                total[c, t] = spent.tile([P, P], F32, name=f"total{c}_{t}", align_bytes=64, offset=512 * t)[:]
-            nc.vector.tensor_tensor(total[c, t], sq[t][:].indirect(p2_sb[:, 8 * c : 8 * c + 8]), near[c, t], ALU.add)
+        def fetch2(out, t, lo, n, partial):
+            nc.vector.tensor_tensor(out, sq[t][:].indirect(offsets(p2_sb, lo, n)), partial, ALU.add)
 
-        def take_root_a(t):
-            nc.scalar.activation(root_a[:, t, :], total_a[t][:], ACT.Abs_reciprocal_sqrt, bias=bias[:] if t == 0 else 1.0, scale=0.5)
+        def take_root(out, sums, one=1.0):
+            nc.scalar.activation(out, sums, ACT.Abs_reciprocal_sqrt, bias=one, scale=0.5)
 
-        def take_root(c, t):
-            nc.scalar.activation(root[c][:, t, :], total[c, t], ACT.Abs_reciprocal_sqrt, bias=1.0, scale=0.5)
+        def gain(t, lo, n):
+            nc.scalar.activation(gained[:, t, lo : lo + n], y[t][:, lo : lo + n], ACT.Copy, scale=gn_sb[:, t : t + 1])
 
-        def gain(h, t):
-            nc.scalar.activation(gained[h][:, t, :], y[t][:, h * HALF : (h + 1) * HALF], ACT.Copy, scale=gn_sb[:, t : t + 1])
-
-        z_in = {}
-        z_words = {}
-        z_scales = {}
+        z_in = [keep.tile([P, P * PACK], BF16, name=f"z_in{c}", align_bytes=64) for c in range(4)]
+        z_words = [keep.tile([P, P], U32, name=f"z_words{c}", align_bytes=64) for c in range(4)]
+        z_scales = [keep.tile([P, P], U8, name=f"z_scales{c}", align_bytes=64) for c in range(4)]
 
         def normalise(c):
-            z_in[c] = owns.tile([P, P * PACK], BF16, name=f"z_in{c}", align_bytes=64, offset=1024 * (10 + c))
-            lo = (c % 2) * P
+            cols = slice(c * P, (c + 1) * P)
             nc.vector.tensor_tensor(
                 z_in[c][:].rearrange("p (c i t) -> p c t i", i=4, t=PACK),
-                gained[c // 2][:, :, lo : lo + P].rearrange("p t (c i) -> p c t i", i=4),
-                root[c].rearrange("p t (c i) -> p c t i", i=4),
+                gained[:, :, cols].rearrange("p t (c i) -> p c t i", i=4),
+                root[c // 2][:, :, (c % 2) * P : (c % 2 + 1) * P].rearrange("p t (c i) -> p c t i", i=4),
                 ALU.mult,
             )
 
         out_words = keep.tile([P, S], U32, name="out_words", align_bytes=64)
         out_scales = keep.tile([P, S], U8, name="out_scales", align_bytes=64)
-        res_ab = [keep.tile([P, HALF * PACK], BF16, name=f"res_in{h}", align_bytes=64) for h in range(2)]
-        res_in = [res_ab[c // 2][:, (c % 2) * P * PACK : (c % 2 + 1) * P * PACK] for c in range(4)]
+        res_in = keep.tile([P, S * PACK], BF16, name="res_in", align_bytes=64)
+        res = [keep.tile([P, PACK, P], F32, name=f"res{c}") for c in range(4)]
         out_rows = out_0.rearrange("(p t) j -> p t j", t=PACK)
         out_w = out_1[0].rearrange("p n t -> p (n t)").bitcast(I32)
         banks = {}
-        res = {}
 
         def second(c):
-            z_words[c] = keep.tile([P, P], U32, name=f"z_words{c}", align_bytes=64)
-            z_scales[c] = keep.tile([P, P], U8, name=f"z_scales{c}", align_bytes=64)
             nc.vector.quantize_mx(z_words[c][:].bitcast(FP8X4), z_scales[c][:], z_in[c][:])
-            if c < 3:
+            if c < 4:
                 banks[c] = psum.tile([P, PACK, P], F32, name=f"out{c}", tag="bank")
                 outs = [banks[c][:, t, :] for t in range(PACK)]
             else:
@@ -237,86 +216,105 @@ def tile_picked_lrn8_relu_po_kernel(tc, x_words, x_scales, w1_words, w1_scales, 
                     stop=True,
                 )
 
+        def rounded(c):
+            return res_in[:, c * P * PACK : (c + 1) * P * PACK]
+
         def empty(c):
-            res[c] = keep.tile([P, PACK, P], F32, name=f"res{c}")
             nc.scalar.copy(res[c][:], banks[c][:])
             nc.sync.dma_start(out_rows[:, :, c * P : (c + 1) * P], res[c][:])
 
-        def empty_last(u):
-            pair = keep.tile([P, 2, P], F32, name=f"pair{u}")
+        def round_pair(u):
             nc.vector.tensor_copy(
-                res_in[3].rearrange("p (j u e) -> p u j e", u=2, e=2)[:, u],
+                rounded(3).rearrange("p (j u e) -> p u j e", u=2, e=2)[:, u],
                 banks[3][u][:].rearrange("p e j -> p j e"),
             )
-            nc.scalar.copy(pair[:], banks[3][u][:])
-            nc.sync.dma_start(out_rows[:, 2 * u : 2 * u + 2, 3 * P :], pair[:])
+
+        def empty_pair(u):
+            nc.scalar.copy(res[3][:, 2 * u : 2 * u + 2, :], banks[3][u][:])
+            nc.sync.dma_start(out_rows[:, 2 * u : 2 * u + 2, 3 * P :], res[3][:, 2 * u : 2 * u + 2, :])
 
         def round_scalar(c):
-            nc.scalar.copy(res_in[c].rearrange("p (j t) -> p j t", t=PACK), banks[c][:].rearrange("p t j -> p j t"))
+            nc.scalar.copy(rounded(c).rearrange("p (j t) -> p j t", t=PACK), banks[c][:].rearrange("p t j -> p j t"))
 
-        def round_vector(c, lo, n):
+        def round_bank(c):
+            nc.vector.tensor_copy(rounded(c).rearrange("p (j t) -> p j t", t=PACK), banks[c][:].rearrange("p t j -> p j t"))
+
+        def round_copy(c):
             nc.vector.tensor_copy(
-                res_in[c][:, lo * PACK : (lo + n) * PACK].rearrange("p (c i t) -> p c t i", i=4, t=PACK),
-                res[c][:, :, lo : lo + n].rearrange("p t (c i) -> p c t i", i=4),
+                rounded(c).rearrange("p (c i t) -> p c t i", i=4, t=PACK),
+                res[c][:].rearrange("p t (c i) -> p c t i", i=4),
             )
 
-        def planes(h):
-            cols = slice(h * HALF, (h + 1) * HALF)
-            nc.vector.quantize_mx(out_words[:, cols].bitcast(FP8X4), out_scales[:, cols], res_ab[h][:])
+        def planes(lo, n):
+            nc.vector.quantize_mx(out_words[:, lo : lo + n].bitcast(FP8X4), out_scales[:, lo : lo + n], res_in[:, lo * PACK : (lo + n) * PACK])
 
         def store_words(queue, lo, n):
             queue.dma_start(out_w[:, lo : lo + n], out_words[:, lo : lo + n].bitcast(I32))
 
+        for t in range(last):
+            for lo in (0, HALF):
+                fetch1(near[t][:, lo : lo + HALF], t, lo, HALF)
+            for lo in (0, HALF):
+                fetch2(total[:, t, lo : lo + HALF], t, lo, HALF, near[t][:, lo : lo + HALF])
         for t in range(PACK):
-            fetch1(0, t)
-            fetch1(1, t)
-            fetch2(0, t)
-            fetch2(1, t)
-            if t == 0:
-                w2s = owns.tile([P, N], U8, name="w2s", align_bytes=64, offset=1024 * t)
-                deal_scales(nc, w2s[:], w2s_raw[:])
-        for t in range(PACK - 1):
-            take_root_a(t)
-        for t in range(PACK):
-            gain(0, t)
-        take_root_a(PACK - 1)
-        for t in range(PACK):
-            gain(1, t)
+            gain(t, 0, S)
+        take_root(root_a[:, 0:2, :], total[:, 0:2, :HALF], bias[:])
+        take_root(root_a[:, 2, :], total[:, 2, :HALF])
 
-        fetch1_b(0, owns, 1024 * 3)
-        fetch1_b(1, owns, 1024 * 9 - 512)
+        partial = {}
+        sums = {}
+
+        def begin(c):
+            partial[c] = roots.tile([P, P], F32, name=f"partial{c}", align_bytes=64, offset=[512, 2048][c])[:]
+            fetch1(partial[c], last, c * P, P)
+
+        def begin_late():
+            both = roots.tile([P, HALF], F32, name="partial_late", align_bytes=64, offset=0)
+            partial[2] = both[:, :P]
+            partial[3] = both[:, P:]
+            fetch1(both[:], last, HALF, HALF)
+
+        def finish(c):
+            sums[c] = roots.tile([P, P], F32, name=f"sums{c}", align_bytes=64, offset=1024 + 512 * (c % 2))
+            fetch2(sums[c][:], last, c * P, P, partial[c])
+
+        def last_root(c):
+            take_root(root[c // 2][:, last, (c % 2) * P : (c % 2 + 1) * P], sums[c][:])
+
+        root_b = roots.tile([P, PACK, HALF], F32, name="root_b", align_bytes=64, offset=2048)
+        root = [root_a, root_b]
+        begin(0)
+        begin(1)
+        finish(0)
+        last_root(0)
+        finish(1)
+        last_root(1)
+        take_root(root_b[:, 0:last, :], total[:, :, HALF:])
+        begin_late()
         normalise(0)
-        normalise(1)
+        finish(2)
+        last_root(2)
         second(0)
+        normalise(1)
+        finish(3)
+        last_root(3)
         second(1)
-        fetch2(2, 0)
-        fetch2(2, 1)
-        fetch1_b(2, owns, 1024 * 10 + 512)
-        fetch1_b(3, spent, 2048)
         empty(0)
         round_scalar(0)
-        take_root(2, 0)
-        take_root(2, 1)
-        empty(1)
-        fetch2(2, 2)
-        take_root(2, 2)
-        fetch2(2, 3)
-        take_root(2, 3)
-        round_scalar(1)
-        for t in range(PACK):
-            fetch2(3, t)
-            take_root(3, t)
         normalise(2)
-        planes(0)
-        store_words(nc.sync, 0, HALF)
-        second(2)
         normalise(3)
+        second(2)
         second(3)
-        round_scalar(2)
+        empty(1)
+        round_scalar(1)
+        planes(0, P)
         empty(2)
-        empty_last(0)
-        empty_last(1)
-        planes(1)
+        round_bank(3)
+        empty(3)
+        planes(P, P)
+        store_words(nc.sync, 0, HALF)
+        round_copy(2)
+        planes(HALF, HALF)
         store_words(nc.scalar, HALF, HALF)
 
         for q in range(4):

@@ -20,6 +20,7 @@ P = 128
 PACK = 4
 PASSES = K // 512
 HALF = S // 2
+BANK = 2048
 
 
 def deal_words(nc, dealt, raw):
@@ -44,7 +45,7 @@ def tile_picked_lrn8_relu_po_kernel(tc, x_words, x_scales, w1_words, w1_scales, 
         owns = ctx.enter_context(tc.tile_pool(name="owns", bufs=1))
         spent = ctx.enter_context(tc.tile_pool(name="spent", bufs=1))
         roots = ctx.enter_context(tc.tile_pool(name="roots", bufs=1))
-        psum = ctx.enter_context(tc.psum_pool(name="psum", bufs=8))
+        psum = ctx.enter_context(tc.psum_pool(name="psum", bufs=1))
 
         offs_sb = keep.tile([P, S // 16], U16, name="offs_sb")
         p1_sb = keep.tile([P, S // 16], U16, name="p1_sb")
@@ -77,20 +78,20 @@ def tile_picked_lrn8_relu_po_kernel(tc, x_words, x_scales, w1_words, w1_scales, 
         nc.vector.memset(w1s_raw[64:128, :].bitcast(I32), 0)
         nc.vector.memset(w2s_raw[32:64, :].bitcast(I32), 0)
         nc.vector.memset(w2s_raw[64:128, :].bitcast(I32), 0)
-        nc.gpsimd.memset(planes1[:].bitcast(I32), 0)
-        nc.gpsimd.memset(w2s[:].bitcast(I32), 0)
+        nc.vector.memset(planes1[:].bitcast(I32), 0)
+        nc.vector.memset(w2s[:].bitcast(I32), 0)
 
         nc.sync.dma_start(offs_sb[:], offs)
-        nc.sync.dma_start(xs_raw[0:32, :].bitcast(I32), x_scales.bitcast(I32).rearrange("z r c -> r z c"))
-        nc.sync.dma_start(w1s_raw[0:32, :].bitcast(I32), w1_scales.bitcast(I32).rearrange("z r c -> r z c"))
-        nc.sync.dma_start(w2s_raw[0:32, :].bitcast(I32), w2_scales.bitcast(I32).rearrange("z r c -> r z c").to_broadcast([16, 2, N // 4]))
+        nc.scalar.dma_start(xs_raw[0:32, :].bitcast(I32), x_scales.bitcast(I32).rearrange("z r c -> r z c"))
+        nc.scalar.dma_start(w1s_raw[0:32, :].bitcast(I32), w1_scales.bitcast(I32).rearrange("z r c -> r z c"))
+        nc.scalar.dma_start(w2s_raw[0:32, :].bitcast(I32), w2_scales.bitcast(I32).rearrange("z r c -> r z c").to_broadcast([16, 2, N // 4]))
         nc.sync.dma_start(
             w1w_raw[:].bitcast(I32).rearrange("p (z c) -> p z c", z=PASSES),
             w1_words.bitcast(I32).rearrange("z p c -> p z c"),
         )
-        nc.sync.dma_start(w2w_raw[:].bitcast(I32), w2_words[0].bitcast(I32))
         for z in range(PASSES):
             nc.sync.dma_start(xw_raw[z][:].bitcast(I32), x_words[z].rearrange("p n t -> p (n t)").bitcast(I32))
+        nc.sync.dma_start(w2w_raw[:].bitcast(I32), w2_words[0].bitcast(I32))
         nc.sync.dma_start(p1_sb[:], p1)
         nc.sync.dma_start(p2_sb[:], p2)
         nc.scalar.activation(bias[:], ones[:], ACT.Abs_reciprocal_sqrt)
@@ -134,7 +135,7 @@ def tile_picked_lrn8_relu_po_kernel(tc, x_words, x_scales, w1_words, w1_scales, 
 
         for k in range(S // P):
             cols = slice(k * P, (k + 1) * P)
-            bank = psum.tile([P, P], F32, name=f"acc0_{k}", tag="bank")
+            bank = psum.tile([P, P], F32, name=f"acc0_{k}", offset=BANK * k)
             first(bank[:], 0, k * P, P, [0, 1])
             if k < 2:
                 nc.scalar.activation(y[0][:, cols], bank[:], ACT.Relu)
@@ -147,7 +148,7 @@ def tile_picked_lrn8_relu_po_kernel(tc, x_words, x_scales, w1_words, w1_scales, 
         nc.vector.tensor_copy(own[0][:, :HALF], sq[0][:, :HALF])
         nc.vector.tensor_tensor(own[0][:, HALF:], y[0][:, HALF:], y[0][:, HALF:], ALU.mult)
         for t in range(1, PACK):
-            bank = psum.tile([P, S], F32, name=f"acc{t}", tag="bank")
+            bank = psum.tile([P, S], F32, name=f"acc{t}", offset=BANK * (3 + t))
             first(bank[:], t, 0, S, [1, 0])
             nc.scalar.activation(y[t][:], bank[:], ACT.Relu)
             if t < PACK - 1:
@@ -199,11 +200,11 @@ def tile_picked_lrn8_relu_po_kernel(tc, x_words, x_scales, w1_words, w1_scales, 
 
         def second(c):
             nc.vector.quantize_mx(z_words[c][:].bitcast(FP8X4), z_scales[c][:], z_in[c][:])
-            if c < 4:
-                banks[c] = psum.tile([P, PACK, P], F32, name=f"out{c}", tag="bank")
+            if c < 3:
+                banks[c] = psum.tile([P, PACK, P], F32, name=f"out{c}", offset=BANK * c)
                 outs = [banks[c][:, t, :] for t in range(PACK)]
             else:
-                banks[c] = [psum.tile([P, 2, P], F32, name=f"out{c}_{u}", tag="bank") for u in range(2)]
+                banks[c] = [psum.tile([P, 2, P], F32, name=f"out{c}_{u}", offset=BANK * (c + u)) for u in range(2)]
                 outs = [banks[c][t // 2][:, t % 2, :] for t in range(PACK)]
             for t in range(PACK):
                 nc.tensor.matmul_mx(
@@ -223,15 +224,14 @@ def tile_picked_lrn8_relu_po_kernel(tc, x_words, x_scales, w1_words, w1_scales, 
             nc.scalar.copy(res[c][:], banks[c][:])
             nc.sync.dma_start(out_rows[:, :, c * P : (c + 1) * P], res[c][:])
 
-        def round_pair(u):
-            nc.vector.tensor_copy(
+        def round_pair(copy, u):
+            copy(
                 rounded(3).rearrange("p (j u e) -> p u j e", u=2, e=2)[:, u],
                 banks[3][u][:].rearrange("p e j -> p j e"),
             )
 
-        def empty_pair(u):
-            nc.scalar.copy(res[3][:, 2 * u : 2 * u + 2, :], banks[3][u][:])
-            nc.sync.dma_start(out_rows[:, 2 * u : 2 * u + 2, 3 * P :], res[3][:, 2 * u : 2 * u + 2, :])
+        def empty_pair(copy, u):
+            copy(res[3][:, 2 * u : 2 * u + 2, :], banks[3][u][:])
 
         def round_scalar(c):
             nc.scalar.copy(rounded(c).rearrange("p (j t) -> p j t", t=PACK), banks[c][:].rearrange("p t j -> p j t"))
@@ -295,27 +295,30 @@ def tile_picked_lrn8_relu_po_kernel(tc, x_words, x_scales, w1_words, w1_scales, 
         finish(2)
         last_root(2)
         second(0)
-        normalise(1)
         finish(3)
         last_root(3)
+        normalise(1)
+        normalise(2)
         second(1)
+        second(2)
         empty(0)
         round_scalar(0)
-        normalise(2)
         normalise(3)
-        second(2)
+        planes(0, P)
         second(3)
         empty(1)
-        round_scalar(1)
-        planes(0, P)
         empty(2)
-        round_bank(3)
-        empty(3)
-        planes(P, P)
-        store_words(nc.sync, 0, HALF)
+        round_scalar(1)
         round_copy(2)
-        planes(HALF, HALF)
-        store_words(nc.scalar, HALF, HALF)
+        planes(P, P)
+        planes(HALF, P)
+        store_words(nc.sync, 0, 3 * P)
+        empty_pair(nc.vector.tensor_copy, 0)
+        empty_pair(nc.scalar.copy, 1)
+        nc.sync.dma_start(out_rows[:, :, 3 * P :], res[3][:])
+        round_copy(3)
+        planes(3 * P, P)
+        store_words(nc.scalar, 3 * P, P)
 
         for q in range(4):
             queue = nc.sync if q % 2 == 0 else nc.scalar

@@ -147,14 +147,23 @@ def tile_picked_lrn8_relu_po_kernel(tc, x_words, x_scales, w1_words, w1_scales, 
                 nc.scalar.activation(sq[0][:, cols], y[0][:, cols], ACT.Square)
         nc.vector.tensor_copy(own[0][:, :HALF], sq[0][:, :HALF])
         nc.vector.tensor_tensor(own[0][:, HALF:], y[0][:, HALF:], y[0][:, HALF:], ALU.mult)
-        for t in range(1, PACK):
-            bank = psum.tile([P, S], F32, name=f"acc{t}", offset=BANK * (3 + t))
+        for h in range(2):
+            cols = slice(h * HALF, (h + 1) * HALF)
+            bank = psum.tile([P, HALF], F32, name=f"acc1_{h}", offset=BANK * (4 + h))
+            for k in range(2):
+                first(bank[:, k * P : (k + 1) * P], 1, h * HALF + k * P, P, [1, 0])
+            nc.scalar.activation(y[1][:, cols], bank[:], ACT.Relu)
+            if h == 0:
+                nc.scalar.activation(own[1][:, cols], y[1][:, cols], ACT.Square)
+        nc.scalar.activation(sq[1][:, :HALF], y[1][:, :HALF], ACT.Square)
+        nc.scalar.activation(own[1][:, HALF:], y[1][:, HALF:], ACT.Square)
+        nc.scalar.activation(sq[1][:, HALF:], y[1][:, HALF:], ACT.Square)
+        for t in range(2, PACK):
+            bank = psum.tile([P, S], F32, name=f"acc{t}", offset=BANK * (4 + t))
             first(bank[:], t, 0, S, [1, 0])
             nc.scalar.activation(y[t][:], bank[:], ACT.Relu)
-            if t < PACK - 1:
-                nc.scalar.activation(own[t][:], y[t][:], ACT.Square)
+            nc.scalar.activation(own[t][:], y[t][:], ACT.Square)
             nc.scalar.activation(sq[t][:], y[t][:], ACT.Square)
-        nc.sync.dma_start(own[PACK - 1][:], sq[PACK - 1][:])
 
         gained = spent.tile([P, PACK, S], F32, name="gained", align_bytes=64, offset=0)
         root_a = spent.tile([P, PACK, HALF], F32, name="root_a", align_bytes=64, offset=8192)

@@ -162,6 +162,7 @@ def tile_picked_lrn8_relu_po_kernel(tc, x_words, x_scales, w1_words, w1_scales, 
             bank = psum.tile([P, S], F32, name=f"acc{t}", offset=BANK * (4 + t))
             first(bank[:], t, 0, S, [1, 0])
             nc.scalar.activation(y[t][:], bank[:], ACT.Relu)
+        for t in range(2, PACK):
             nc.scalar.activation(own[t][:], y[t][:], ACT.Square)
             nc.scalar.activation(sq[t][:], y[t][:], ACT.Square)
 
@@ -190,12 +191,12 @@ def tile_picked_lrn8_relu_po_kernel(tc, x_words, x_scales, w1_words, w1_scales, 
         z_words = [keep.tile([P, P], U32, name=f"z_words{c}", align_bytes=64) for c in range(4)]
         z_scales = [keep.tile([P, P], U8, name=f"z_scales{c}", align_bytes=64) for c in range(4)]
 
-        def normalise(c):
-            cols = slice(c * P, (c + 1) * P)
+        def normalise(c, lo=0, n=P):
+            cols = slice(c * P + lo, c * P + lo + n)
             nc.vector.tensor_tensor(
-                z_in[c][:].rearrange("p (c i t) -> p c t i", i=4, t=PACK),
+                z_in[c][:, lo * PACK : (lo + n) * PACK].rearrange("p (c i t) -> p c t i", i=4, t=PACK),
                 gained[:, :, cols].rearrange("p t (c i) -> p c t i", i=4),
-                root[c // 2][:, :, (c % 2) * P : (c % 2 + 1) * P].rearrange("p t (c i) -> p c t i", i=4),
+                root[c // 2][:, :, (c % 2) * P + lo : (c % 2) * P + lo + n].rearrange("p t (c i) -> p c t i", i=4),
                 ALU.mult,
             )
 
@@ -248,11 +249,14 @@ def tile_picked_lrn8_relu_po_kernel(tc, x_words, x_scales, w1_words, w1_scales, 
         def round_bank(c):
             nc.vector.tensor_copy(rounded(c).rearrange("p (j t) -> p j t", t=PACK), banks[c][:].rearrange("p t j -> p j t"))
 
-        def round_copy(c):
+        def round_copy(c, n=P):
             nc.vector.tensor_copy(
-                rounded(c).rearrange("p (c i t) -> p c t i", i=4, t=PACK),
-                res[c][:].rearrange("p t (c i) -> p c t i", i=4),
+                rounded(c)[:, : n * PACK].rearrange("p (c i t) -> p c t i", i=4, t=PACK),
+                res[c][:, :, :n].rearrange("p t (c i) -> p c t i", i=4),
             )
+
+        def round_rest(c, lo):
+            nc.scalar.copy(rounded(c)[:, lo * PACK :].rearrange("p (j t) -> p j t", t=PACK), res[c][:, :, lo:].rearrange("p t j -> p j t"))
 
         def planes(lo, n):
             nc.vector.quantize_mx(out_words[:, lo : lo + n].bitcast(FP8X4), out_scales[:, lo : lo + n], res_in[:, lo * PACK : (lo + n) * PACK])
@@ -266,7 +270,7 @@ def tile_picked_lrn8_relu_po_kernel(tc, x_words, x_scales, w1_words, w1_scales, 
             for lo in (0, HALF):
                 fetch2(total[:, t, lo : lo + HALF], t, lo, HALF, near[t][:, lo : lo + HALF])
         for t in range(PACK):
-            gain(t, 0, S)
+            gain(t, 0, S if t < 2 else HALF)
         take_root(root_a[:, 0:2, :], total[:, 0:2, :HALF], bias[:])
         take_root(root_a[:, 2, :], total[:, 2, :HALF])
 
@@ -299,35 +303,39 @@ def tile_picked_lrn8_relu_po_kernel(tc, x_words, x_scales, w1_words, w1_scales, 
         finish(1)
         last_root(1)
         take_root(root_b[:, 0:last, :], total[:, :, HALF:])
+        for t in range(2, PACK):
+            gain(t, HALF, HALF)
         begin_late()
         normalise(0)
         finish(2)
         last_root(2)
         second(0)
+        normalise(1)
         finish(3)
         last_root(3)
-        normalise(1)
-        normalise(2)
         second(1)
-        second(2)
         empty(0)
         round_scalar(0)
-        normalise(3)
+        normalise(2)
+        normalise(3, 0, P // 2)
+        second(2)
+        normalise(3, P // 2, P // 2)
         planes(0, P)
         second(3)
         empty(1)
         empty(2)
-        round_scalar(1)
-        round_copy(2)
-        planes(P, P)
-        planes(HALF, P)
-        store_words(nc.sync, 0, 3 * P)
+        round_copy(1)
         empty_pair(nc.vector.tensor_copy, 0)
         empty_pair(nc.scalar.copy, 1)
         nc.sync.dma_start(out_rows[:, :, 3 * P :], res[3][:])
-        round_copy(3)
+        round_copy(2)
+        round_copy(3, P // 2)
+        round_rest(3, P // 2)
+        planes(P, P)
+        store_words(nc.sync, 0, HALF)
+        planes(HALF, P)
         planes(3 * P, P)
-        store_words(nc.scalar, 3 * P, P)
+        store_words(nc.scalar, HALF, HALF)
 
         for q in range(4):
             queue = nc.sync if q % 2 == 0 else nc.scalar

@@ -19,8 +19,13 @@ ALU = mybir.AluOpType
 P = 128
 PACK = 4
 PASSES = K // 512
+BLOCKS = S // P
 HALF = S // 2
+LAST = PACK - 1
 BANK = 2048
+QUADRANTS = 4
+ROWS = S + H
+BLOCK_BYTES = 4 * P
 
 
 def deal_words(nc, dealt, raw):
@@ -42,9 +47,8 @@ def tile_picked_lrn8_relu_po_kernel(tc, x_words, x_scales, w1_words, w1_scales, 
     with ExitStack() as ctx:
         keep = ctx.enter_context(tc.tile_pool(name="keep", bufs=1))
         later = ctx.enter_context(tc.tile_pool(name="later", bufs=1))
-        owns = ctx.enter_context(tc.tile_pool(name="owns", bufs=1))
         spent = ctx.enter_context(tc.tile_pool(name="spent", bufs=1))
-        roots = ctx.enter_context(tc.tile_pool(name="roots", bufs=1))
+        chain = ctx.enter_context(tc.tile_pool(name="chain", bufs=1))
         psum = ctx.enter_context(tc.psum_pool(name="psum", bufs=1))
 
         offs_sb = keep.tile([P, S // 16], U16, name="offs_sb")
@@ -52,173 +56,187 @@ def tile_picked_lrn8_relu_po_kernel(tc, x_words, x_scales, w1_words, w1_scales, 
         p2_sb = keep.tile([P, S // 16], U16, name="p2_sb")
 
         xs_raw = keep.tile([P, T], U8, name="xs_raw", align_bytes=64)
-        w2w_raw = keep.tile([P, 2 * N], U8, name="w2w_raw", align_bytes=64)
-        w2w = keep.tile([P, 2 * N], U8, name="w2w", align_bytes=64)
         xs_got = keep.tile([P, S], U8, name="xs_got", align_bytes=64)
         w1s_raw = keep.tile([P, H], U8, name="w1s_raw", align_bytes=64)
         w2s_raw = keep.tile([P, N], U8, name="w2s_raw", align_bytes=64)
         w2s_flat = keep.tile([P, N], U8, name="w2s_flat", align_bytes=64)
         w2s = keep.tile([P, N], U8, name="w2s", align_bytes=64)
-        flat = keep.tile([P, S + H], U8, name="flat", align_bytes=64)
-        planes1 = spent.tile([P, PASSES * (S + H)], U8, name="planes1", align_bytes=64, offset=8192)
-        w1w_raw = spent.tile([P, PASSES * 2 * H], U8, name="w1w_raw", align_bytes=64, offset=4096)
-        w1w = spent.tile([P, PASSES * 2 * H], U8, name="w1w", align_bytes=64, offset=6144)
+        joined = keep.tile([P, ROWS], U8, name="joined", align_bytes=64)
+        w2w_raw = keep.tile([P, 2 * N], U8, name="w2w_raw", align_bytes=64)
+        w2w = keep.tile([P, 2 * N], U8, name="w2w", align_bytes=64)
         xw_raw = [
             later.tile([P, T], U32, name="xw_raw0", align_bytes=64, offset=0),
             keep.tile([P, T], U32, name="xw_raw1", align_bytes=64),
         ]
-        xw = [spent.tile([P, S], U32, name=f"xw{z}", align_bytes=64, offset=2048 * z) for z in range(PASSES)]
+        xw = [spent.tile([P, S], U32, name=f"xw{g}", align_bytes=64, offset=2048 * g) for g in range(PASSES)]
+        w1w_raw = spent.tile([P, PASSES * 2 * H], U8, name="w1w_raw", align_bytes=64, offset=2048 * 2)
+        w1w = spent.tile([P, PASSES * 2 * H], U8, name="w1w", align_bytes=64, offset=2048 * 3)
+        scales1 = spent.tile([P, PASSES * ROWS], U8, name="scales1", align_bytes=64, offset=2048 * 4)
         ones = keep.tile([P, 1], F32, name="ones")
         bias = keep.tile([P, 1], F32, name="bias")
 
+        nc.vector.memset(w2s_raw[:].bitcast(I32), 0)
         nc.vector.memset(ones[:], 1.0)
-        nc.vector.memset(xs_raw[32:64, :].bitcast(I32), 0)
-        nc.vector.memset(xs_raw[64:128, :].bitcast(I32), 0)
-        nc.vector.memset(w1s_raw[32:64, :].bitcast(I32), 0)
-        nc.vector.memset(w1s_raw[64:128, :].bitcast(I32), 0)
-        nc.vector.memset(w2s_raw[32:64, :].bitcast(I32), 0)
-        nc.vector.memset(w2s_raw[64:128, :].bitcast(I32), 0)
-        nc.vector.memset(planes1[:].bitcast(I32), 0)
+        for raw in (xs_raw, w1s_raw):
+            nc.vector.memset(raw[32:64, :].bitcast(I32), 0)
+            nc.vector.memset(raw[64:128, :].bitcast(I32), 0)
+        nc.vector.memset(scales1[:].bitcast(I32), 0)
         nc.vector.memset(w2s[:].bitcast(I32), 0)
 
         nc.sync.dma_start(offs_sb[:], offs)
-        nc.scalar.dma_start(xs_raw[0:32, :].bitcast(I32), x_scales.bitcast(I32).rearrange("z r c -> r z c"))
-        nc.scalar.dma_start(w1s_raw[0:32, :].bitcast(I32), w1_scales.bitcast(I32).rearrange("z r c -> r z c"))
-        nc.scalar.dma_start(w2s_raw[0:32, :].bitcast(I32), w2_scales.bitcast(I32).rearrange("z r c -> r z c").to_broadcast([16, 2, N // 4]))
+        nc.scalar.dma_start(xs_raw[0:32, :].bitcast(I32), x_scales.bitcast(I32).rearrange("g r c -> r g c"))
+        nc.scalar.dma_start(w1s_raw[0:32, :].bitcast(I32), w1_scales.bitcast(I32).rearrange("g r c -> r g c"))
+        nc.scalar.dma_start(w2s_raw[0:16, :].bitcast(I32), w2_scales[0].bitcast(I32))
         nc.sync.dma_start(
-            w1w_raw[:].bitcast(I32).rearrange("p (z c) -> p z c", z=PASSES),
-            w1_words.bitcast(I32).rearrange("z p c -> p z c"),
+            w1w_raw[:].bitcast(I32).rearrange("p (g c) -> p g c", g=PASSES),
+            w1_words.bitcast(I32).rearrange("g p c -> p g c"),
         )
-        for z in range(PASSES):
-            nc.sync.dma_start(xw_raw[z][:].bitcast(I32), x_words[z].rearrange("p n t -> p (n t)").bitcast(I32))
+        for g in range(PASSES):
+            nc.sync.dma_start(xw_raw[g][:].bitcast(I32), x_words[g].rearrange("p n t -> p (n t)").bitcast(I32))
         nc.sync.dma_start(w2w_raw[:].bitcast(I32), w2_words[0].bitcast(I32))
         nc.sync.dma_start(p1_sb[:], p1)
         nc.sync.dma_start(p2_sb[:], p2)
         nc.scalar.activation(bias[:], ones[:], ACT.Abs_reciprocal_sqrt)
 
         nc.vector.tensor_copy(xs_got[:], xs_raw[:].indirect(offs_sb[:]))
-        deal_scales(nc, flat[:, S:], w1s_raw[:])
-        nc.vector.tensor_copy(flat[:, :S].bitcast(I32), xs_got[:].bitcast(I32))
-        for q in range(4):
+        deal_scales(nc, joined[:, S:], w1s_raw[:])
+        nc.vector.tensor_copy(joined[:, :S].bitcast(I32), xs_got[:].bitcast(I32))
+        for q in range(QUADRANTS):
             nc.scalar.dma_start(
-                planes1[32 * q : 32 * q + 4, :].bitcast(I32).rearrange("r (z c) -> r z c", z=PASSES),
-                flat[8 * q : 8 * q + 8, :].bitcast(I32),
+                scales1[32 * q : 32 * q + 4, :].bitcast(I32).rearrange("r (g c) -> r g c", g=PASSES),
+                joined[8 * q : 8 * q + 8, :].bitcast(I32),
             )
         deal_words(nc, w1w[:], w1w_raw[:])
         nc.vector.tensor_copy(xw[0][:], xw_raw[0][:].indirect(offs_sb[:]))
         deal_scales(nc, w2s_flat[:], w2s_raw[:])
-        for h in range(2):
-            nc.vector.tensor_copy(xw[1][:, h * HALF : (h + 1) * HALF], xw_raw[1][:].indirect(offs_sb[:, h * 16 : (h + 1) * 16]))
 
+        def entries(lists, lo, n):
+            return lists[:, lo // 16 : (lo + n) // 16]
+
+        for lo in (0, HALF):
+            nc.vector.tensor_copy(xw[1][:, lo : lo + HALF], xw_raw[1][:].indirect(entries(offs_sb, lo, HALF)))
         deal_words(nc, w2w[:], w2w_raw[:])
-        gn_sb = later.tile([P, PACK], F32, name="gn_sb", align_bytes=64, offset=3 * N)
-        nc.sync.dma_start(gn_sb[:], gn.rearrange("(p t) o -> p (t o)", t=PACK))
-        for q in range(4):
-            nc.sync.dma_start(w2s[32 * q : 32 * q + 4, :].bitcast(I32), w2s_flat[8 * q : 8 * q + 8 : 2, :].bitcast(I32))
 
-        def first(bank, t, lo, width, order):
-            for z in order:
-                col = (t * PASSES + z) * P
+        gn_sb = later.tile([P, PACK], F32, name="gn_sb", align_bytes=64, offset=0)
+        nc.sync.dma_start(gn_sb[:], gn.rearrange("(p t) o -> p (t o)", t=PACK))
+        for q in range(QUADRANTS):
+            nc.sync.dma_start(w2s[32 * q : 32 * q + 4, :].bitcast(I32), w2s_flat[4 * q : 4 * q + 4, :].bitcast(I32))
+
+        def first_product(acc, t, lo, n, passes):
+            for g in passes:
+                column = (t * PASSES + g) * P
                 nc.tensor.matmul_mx(
-                    out=bank,
-                    lhsT=w1w[:, 2 * col : 2 * col + 2 * P].bitcast(FP4X4),
-                    lhsT_scale=planes1[:, z * (S + H) + S + t * P : z * (S + H) + S + (t + 1) * P],
-                    rhs=xw[z][:, lo : lo + width].bitcast(FP8X4),
-                    rhs_scale=planes1[:, z * (S + H) + lo : z * (S + H) + lo + width],
-                    start=(z == order[0]),
-                    stop=(z == order[-1]),
+                    out=acc,
+                    lhsT=w1w[:, 2 * column : 2 * column + 2 * P].bitcast(FP4X4),
+                    lhsT_scale=scales1[:, g * ROWS + S + t * P : g * ROWS + S + (t + 1) * P],
+                    rhs=xw[g][:, lo : lo + n].bitcast(FP8X4),
+                    rhs_scale=scales1[:, g * ROWS + lo : g * ROWS + lo + n],
+                    start=(g == passes[0]),
+                    stop=(g == passes[-1]),
                 )
 
         y = [keep.tile([P, S], F32, name=f"y{t}") for t in range(PACK)]
         sq = [keep.tile([P, S], F32, name=f"sq{t}") for t in range(PACK)]
-        own = [owns.tile([P, S], F32, name=f"own{t}", align_bytes=64, offset=2048 * t) for t in range(PACK)]
+        own = [keep.tile([P, S], F32, name=f"own{t}") for t in range(PACK)]
 
-        for k in range(S // P):
-            cols = slice(k * P, (k + 1) * P)
-            bank = psum.tile([P, P], F32, name=f"acc0_{k}", offset=BANK * k)
-            first(bank[:], 0, k * P, P, [0, 1])
-            if k < 2:
-                nc.scalar.activation(y[0][:, cols], bank[:], ACT.Relu)
+        def square(out, t, lo, n):
+            nc.scalar.activation(out[t][:, lo : lo + n], y[t][:, lo : lo + n], ACT.Square)
+
+        for c in range(BLOCKS):
+            columns = slice(c * P, (c + 1) * P)
+            acc = psum.tile([P, P], F32, name=f"acc0_{c}", offset=BANK * c)
+            first_product(acc[:], 0, c * P, P, [0, 1])
+            if c * P < HALF:
+                nc.scalar.activation(y[0][:, columns], acc[:], ACT.Relu)
+                if (c + 1) * P == HALF:
+                    square(sq, 0, 0, HALF)
             else:
-                nc.vector.tensor_scalar_max(y[0][:, cols], bank[:], 0.0)
-            if k == 1:
-                nc.scalar.activation(sq[0][:, :HALF], y[0][:, :HALF], ACT.Square)
-            if k > 1:
-                nc.scalar.activation(sq[0][:, cols], y[0][:, cols], ACT.Square)
+                nc.vector.tensor_scalar_max(y[0][:, columns], acc[:], 0.0)
+                square(sq, 0, c * P, P)
         nc.vector.tensor_copy(own[0][:, :HALF], sq[0][:, :HALF])
         nc.vector.tensor_tensor(own[0][:, HALF:], y[0][:, HALF:], y[0][:, HALF:], ALU.mult)
+
         for h in range(2):
-            cols = slice(h * HALF, (h + 1) * HALF)
-            bank = psum.tile([P, HALF], F32, name=f"acc1_{h}", offset=BANK * (4 + h))
-            for k in range(2):
-                first(bank[:, k * P : (k + 1) * P], 1, h * HALF + k * P, P, [1, 0])
-            nc.scalar.activation(y[1][:, cols], bank[:], ACT.Relu)
-            if h == 0:
-                nc.scalar.activation(own[1][:, cols], y[1][:, cols], ACT.Square)
-        nc.scalar.activation(sq[1][:, :HALF], y[1][:, :HALF], ACT.Square)
-        nc.scalar.activation(own[1][:, HALF:], y[1][:, HALF:], ACT.Square)
-        nc.scalar.activation(sq[1][:, HALF:], y[1][:, HALF:], ACT.Square)
+            acc = psum.tile([P, HALF], F32, name=f"acc1_{h}", offset=BANK * (BLOCKS + h))
+            for lo in (0, P):
+                first_product(acc[:, lo : lo + P], 1, h * HALF + lo, P, [1, 0])
+            nc.scalar.activation(y[1][:, h * HALF : (h + 1) * HALF], acc[:], ACT.Relu)
+            square(own if h == 0 else sq, 1, 0, HALF)
+        square(own, 1, HALF, HALF)
+        square(sq, 1, HALF, HALF)
         for t in range(2, PACK):
-            bank = psum.tile([P, S], F32, name=f"acc{t}", offset=BANK * (4 + t))
-            first(bank[:], t, 0, S, [1, 0])
-            nc.scalar.activation(y[t][:], bank[:], ACT.Relu)
+            acc = psum.tile([P, S], F32, name=f"acc{t}", offset=BANK * (BLOCKS + t))
+            first_product(acc[:], t, 0, S, [1, 0])
+            nc.scalar.activation(y[t][:], acc[:], ACT.Relu)
         for t in range(2, PACK):
-            nc.scalar.activation(own[t][:], y[t][:], ACT.Square)
-            nc.scalar.activation(sq[t][:], y[t][:], ACT.Square)
+            square(own, t, 0, S)
+            square(sq, t, 0, S)
+
+        def fetch_p1(out, t, lo, n):
+            nc.vector.tensor_tensor(out, sq[t][:].indirect(entries(p1_sb, lo, n)), own[t][:, lo : lo + n], ALU.add)
+
+        def fetch_p2(out, t, lo, n, so_far):
+            nc.vector.tensor_tensor(out, sq[t][:].indirect(entries(p2_sb, lo, n)), so_far, ALU.add)
+
+        near = [keep.tile([P, S], F32, name=f"near{t}") for t in range(LAST)]
+        total = keep.tile([P, LAST, S], F32, name="total")
+        for t in range(LAST):
+            for lo in (0, HALF):
+                fetch_p1(near[t][:, lo : lo + HALF], t, lo, HALF)
+            for lo in (0, HALF):
+                fetch_p2(total[:, t, lo : lo + HALF], t, lo, HALF, near[t][:, lo : lo + HALF])
 
         gained = spent.tile([P, PACK, S], F32, name="gained", align_bytes=64, offset=0)
-        root_a = spent.tile([P, PACK, HALF], F32, name="root_a", align_bytes=64, offset=8192)
-        total = keep.tile([P, PACK - 1, S], F32, name="total")
-        near = [keep.tile([P, S], F32, name=f"near{t}") for t in range(PACK - 1)]
-        last = PACK - 1
-
-        def offsets(table, lo, n):
-            return table[:, lo // 16 : (lo + n) // 16]
-
-        def fetch1(out, t, lo, n):
-            nc.vector.tensor_tensor(out, sq[t][:].indirect(offsets(p1_sb, lo, n)), own[t][:, lo : lo + n], ALU.add)
-
-        def fetch2(out, t, lo, n, partial):
-            nc.vector.tensor_tensor(out, sq[t][:].indirect(offsets(p2_sb, lo, n)), partial, ALU.add)
-
-        def take_root(out, sums, one=1.0):
-            nc.scalar.activation(out, sums, ACT.Abs_reciprocal_sqrt, bias=one, scale=0.5)
+        root_early = spent.tile([P, PACK, HALF], F32, name="root_early", align_bytes=64, offset=2048 * 4)
 
         def gain(t, lo, n):
             nc.scalar.activation(gained[:, t, lo : lo + n], y[t][:, lo : lo + n], ACT.Copy, scale=gn_sb[:, t : t + 1])
 
-        z_in = [keep.tile([P, P * PACK], BF16, name=f"z_in{c}", align_bytes=64) for c in range(4)]
-        z_words = [keep.tile([P, P], U32, name=f"z_words{c}", align_bytes=64) for c in range(4)]
-        z_scales = [keep.tile([P, P], U8, name=f"z_scales{c}", align_bytes=64) for c in range(4)]
+        def take_root(out, sums, one=1.0):
+            nc.scalar.activation(out, sums, ACT.Abs_reciprocal_sqrt, bias=one, scale=0.5)
+
+        for t in range(PACK):
+            gain(t, 0, S if t < 2 else HALF)
+        take_root(root_early[:, 0:2, :], total[:, 0:2, :HALF], bias[:])
+        take_root(root_early[:, 2, :], total[:, 2, :HALF])
+
+        near_early = [chain.tile([P, P], F32, name=f"near_early{c}", align_bytes=64, offset=BLOCK_BYTES * (1 + 3 * c)) for c in range(2)]
+        near_late = chain.tile([P, HALF], F32, name="near_late", align_bytes=64, offset=0)
+        near_last = [near_early[0][:], near_early[1][:], near_late[:, :P], near_late[:, P:]]
+        total_last = [chain.tile([P, P], F32, name=f"total_last{c}", align_bytes=64, offset=BLOCK_BYTES * (2 + c % 2)) for c in range(BLOCKS)]
+        root_late = chain.tile([P, PACK, HALF], F32, name="root_late", align_bytes=64, offset=BLOCK_BYTES * 4)
+        root = [root_early[:, :, :P], root_early[:, :, P:], root_late[:, :, :P], root_late[:, :, P:]]
+
+        def finish_last(c):
+            fetch_p2(total_last[c][:], LAST, c * P, P, near_last[c])
+            take_root(root[c][:, LAST, :], total_last[c][:])
+
+        z_in = [keep.tile([P, P * PACK], BF16, name=f"z_in{c}", align_bytes=64) for c in range(BLOCKS)]
+        z_words = [keep.tile([P, P], U32, name=f"z_words{c}", align_bytes=64) for c in range(BLOCKS)]
+        z_scales = [keep.tile([P, P], U8, name=f"z_scales{c}", align_bytes=64) for c in range(BLOCKS)]
+
+        def by_fours(tiles):
+            return tiles.rearrange("p t (c i) -> p c t i", i=4)
+
+        def interleaved(values):
+            return values.rearrange("p (c i t) -> p c t i", i=4, t=PACK)
 
         def normalise(c, lo=0, n=P):
-            cols = slice(c * P + lo, c * P + lo + n)
             nc.vector.tensor_tensor(
-                z_in[c][:, lo * PACK : (lo + n) * PACK].rearrange("p (c i t) -> p c t i", i=4, t=PACK),
-                gained[:, :, cols].rearrange("p t (c i) -> p c t i", i=4),
-                root[c // 2][:, :, (c % 2) * P + lo : (c % 2) * P + lo + n].rearrange("p t (c i) -> p c t i", i=4),
+                interleaved(z_in[c][:, lo * PACK : (lo + n) * PACK]),
+                by_fours(gained[:, :, c * P + lo : c * P + lo + n]),
+                by_fours(root[c][:, :, lo : lo + n]),
                 ALU.mult,
             )
 
-        out_words = keep.tile([P, S], U32, name="out_words", align_bytes=64)
-        out_scales = keep.tile([P, S], U8, name="out_scales", align_bytes=64)
-        res_in = keep.tile([P, S * PACK], BF16, name="res_in", align_bytes=64)
-        res = [keep.tile([P, PACK, P], F32, name=f"res{c}") for c in range(4)]
-        out_rows = out_0.rearrange("(p t) j -> p t j", t=PACK)
-        out_w = out_1[0].rearrange("p n t -> p (n t)").bitcast(I32)
-        banks = {}
+        banks = [psum.tile([P, PACK, P], F32, name=f"out{c}", offset=BANK * c) for c in range(BLOCKS - 1)]
+        last_banks = [psum.tile([P, 2, P], F32, name=f"out_last{u}", offset=BANK * (BLOCKS - 1 + u)) for u in range(2)]
 
-        def second(c):
+        def second_product(c):
             nc.vector.quantize_mx(z_words[c][:].bitcast(FP8X4), z_scales[c][:], z_in[c][:])
-            if c < 3:
-                banks[c] = psum.tile([P, PACK, P], F32, name=f"out{c}", offset=BANK * c)
-                outs = [banks[c][:, t, :] for t in range(PACK)]
-            else:
-                banks[c] = [psum.tile([P, 2, P], F32, name=f"out{c}_{u}", offset=BANK * (c + u)) for u in range(2)]
-                outs = [banks[c][t // 2][:, t % 2, :] for t in range(PACK)]
             for t in range(PACK):
                 nc.tensor.matmul_mx(
-                    out=outs[t],
+                    out=banks[c][:, t, :] if c < BLOCKS - 1 else last_banks[t // 2][:, t % 2, :],
                     lhsT=w2w[:, 2 * t * P : 2 * (t + 1) * P].bitcast(FP4X4),
                     lhsT_scale=w2s[:, t * P : (t + 1) * P],
                     rhs=z_words[c][:].bitcast(FP8X4),
@@ -227,116 +245,73 @@ def tile_picked_lrn8_relu_po_kernel(tc, x_words, x_scales, w1_words, w1_scales, 
                     stop=True,
                 )
 
-        def rounded(c):
-            return res_in[:, c * P * PACK : (c + 1) * P * PACK]
+        res = [keep.tile([P, PACK, P], F32, name=f"res{c}") for c in range(BLOCKS)]
+        rounded = keep.tile([P, S * PACK], BF16, name="rounded", align_bytes=64)
+        out_words = keep.tile([P, S], U32, name="out_words", align_bytes=64)
+        out_scales = keep.tile([P, S], U8, name="out_scales", align_bytes=64)
+        out_rows = out_0.rearrange("(p t) j -> p t j", t=PACK)
+        out_codes = out_1[0].rearrange("p n t -> p (n t)").bitcast(I32)
+
+        def store_block(c):
+            nc.sync.dma_start(out_rows[:, :, c * P : (c + 1) * P], res[c][:])
 
         def empty(c):
             nc.scalar.copy(res[c][:], banks[c][:])
-            nc.sync.dma_start(out_rows[:, :, c * P : (c + 1) * P], res[c][:])
+            store_block(c)
 
-        def round_pair(copy, u):
-            copy(
-                rounded(3).rearrange("p (j u e) -> p u j e", u=2, e=2)[:, u],
-                banks[3][u][:].rearrange("p e j -> p j e"),
+        def round_on_vector(c, n=P):
+            nc.vector.tensor_copy(interleaved(rounded[:, c * P * PACK : (c * P + n) * PACK]), by_fours(res[c][:, :, :n]))
+
+        def round_on_scalar(c, source, lo=0):
+            nc.scalar.copy(
+                rounded[:, (c * P + lo) * PACK : (c + 1) * P * PACK].rearrange("p (j t) -> p j t", t=PACK),
+                source[:, :, lo:].rearrange("p t j -> p j t"),
             )
 
-        def empty_pair(copy, u):
-            copy(res[3][:, 2 * u : 2 * u + 2, :], banks[3][u][:])
+        def quantise_result(lo, n):
+            nc.vector.quantize_mx(out_words[:, lo : lo + n].bitcast(FP8X4), out_scales[:, lo : lo + n], rounded[:, lo * PACK : (lo + n) * PACK])
 
-        def round_scalar(c):
-            nc.scalar.copy(rounded(c).rearrange("p (j t) -> p j t", t=PACK), banks[c][:].rearrange("p t j -> p j t"))
+        def store_words(queue, lo):
+            queue.dma_start(out_codes[:, lo : lo + HALF], out_words[:, lo : lo + HALF].bitcast(I32))
 
-        def round_bank(c):
-            nc.vector.tensor_copy(rounded(c).rearrange("p (j t) -> p j t", t=PACK), banks[c][:].rearrange("p t j -> p j t"))
-
-        def round_copy(c, n=P):
-            nc.vector.tensor_copy(
-                rounded(c)[:, : n * PACK].rearrange("p (c i t) -> p c t i", i=4, t=PACK),
-                res[c][:, :, :n].rearrange("p t (c i) -> p c t i", i=4),
-            )
-
-        def round_rest(c, lo):
-            nc.scalar.copy(rounded(c)[:, lo * PACK :].rearrange("p (j t) -> p j t", t=PACK), res[c][:, :, lo:].rearrange("p t j -> p j t"))
-
-        def planes(lo, n):
-            nc.vector.quantize_mx(out_words[:, lo : lo + n].bitcast(FP8X4), out_scales[:, lo : lo + n], res_in[:, lo * PACK : (lo + n) * PACK])
-
-        def store_words(queue, lo, n):
-            queue.dma_start(out_w[:, lo : lo + n], out_words[:, lo : lo + n].bitcast(I32))
-
-        for t in range(last):
-            for lo in (0, HALF):
-                fetch1(near[t][:, lo : lo + HALF], t, lo, HALF)
-            for lo in (0, HALF):
-                fetch2(total[:, t, lo : lo + HALF], t, lo, HALF, near[t][:, lo : lo + HALF])
-        for t in range(PACK):
-            gain(t, 0, S if t < 2 else HALF)
-        take_root(root_a[:, 0:2, :], total[:, 0:2, :HALF], bias[:])
-        take_root(root_a[:, 2, :], total[:, 2, :HALF])
-
-        partial = {}
-        sums = {}
-
-        def begin(c):
-            partial[c] = roots.tile([P, P], F32, name=f"partial{c}", align_bytes=64, offset=[512, 2048][c])[:]
-            fetch1(partial[c], last, c * P, P)
-
-        def begin_late():
-            both = roots.tile([P, HALF], F32, name="partial_late", align_bytes=64, offset=0)
-            partial[2] = both[:, :P]
-            partial[3] = both[:, P:]
-            fetch1(both[:], last, HALF, HALF)
-
-        def finish(c):
-            sums[c] = roots.tile([P, P], F32, name=f"sums{c}", align_bytes=64, offset=1024 + 512 * (c % 2))
-            fetch2(sums[c][:], last, c * P, P, partial[c])
-
-        def last_root(c):
-            take_root(root[c // 2][:, last, (c % 2) * P : (c % 2 + 1) * P], sums[c][:])
-
-        root_b = roots.tile([P, PACK, HALF], F32, name="root_b", align_bytes=64, offset=2048)
-        root = [root_a, root_b]
-        begin(0)
-        begin(1)
-        finish(0)
-        last_root(0)
-        finish(1)
-        last_root(1)
-        take_root(root_b[:, 0:last, :], total[:, :, HALF:])
+        for c in range(2):
+            fetch_p1(near_last[c], LAST, c * P, P)
+        for c in range(2):
+            finish_last(c)
+        take_root(root_late[:, 0:LAST, :], total[:, :, HALF:])
         for t in range(2, PACK):
             gain(t, HALF, HALF)
-        begin_late()
+        fetch_p1(near_late[:], LAST, HALF, HALF)
+
         normalise(0)
-        finish(2)
-        last_root(2)
-        second(0)
+        finish_last(2)
+        second_product(0)
         normalise(1)
-        finish(3)
-        last_root(3)
-        second(1)
+        finish_last(3)
+        second_product(1)
         empty(0)
-        round_scalar(0)
+        round_on_scalar(0, banks[0])
         normalise(2)
         normalise(3, 0, P // 2)
-        second(2)
+        second_product(2)
         normalise(3, P // 2, P // 2)
-        planes(0, P)
-        second(3)
+        quantise_result(0, P)
+        second_product(3)
+
         empty(1)
         empty(2)
-        round_copy(1)
-        empty_pair(nc.vector.tensor_copy, 0)
-        empty_pair(nc.scalar.copy, 1)
-        nc.sync.dma_start(out_rows[:, :, 3 * P :], res[3][:])
-        round_copy(2)
-        round_copy(3, P // 2)
-        round_rest(3, P // 2)
-        planes(P, P)
-        store_words(nc.sync, 0, HALF)
-        planes(HALF, P)
-        planes(3 * P, P)
-        store_words(nc.scalar, HALF, HALF)
-
-        for q in range(4):
+        round_on_vector(1)
+        nc.vector.tensor_copy(res[3][:, 0:2, :], last_banks[0][:])
+        nc.scalar.copy(res[3][:, 2:4, :], last_banks[1][:])
+        store_block(3)
+        round_on_vector(2)
+        round_on_vector(3, P // 2)
+        round_on_scalar(3, res[3], P // 2)
+        quantise_result(P, P)
+        store_words(nc.sync, 0)
+        quantise_result(2 * P, P)
+        quantise_result(3 * P, P)
+        store_words(nc.scalar, HALF)
+        for q in range(QUADRANTS):
             queue = nc.sync if q % 2 == 0 else nc.scalar
             queue.dma_start(out_2[0, 4 * q : 4 * q + 4, :].bitcast(I32), out_scales[32 * q : 32 * q + 4, :].bitcast(I32))

@@ -49,6 +49,7 @@ def tile_picked_lrn8_relu_po_kernel(tc, x_words, x_scales, w1_words, w1_scales, 
         later = ctx.enter_context(tc.tile_pool(name="later", bufs=1))
         spent = ctx.enter_context(tc.tile_pool(name="spent", bufs=1))
         chain = ctx.enter_context(tc.tile_pool(name="chain", bufs=1))
+        behind = ctx.enter_context(tc.tile_pool(name="behind", bufs=1))
         psum = ctx.enter_context(tc.psum_pool(name="psum", bufs=1))
 
         offs_sb = keep.tile([P, S // 16], U16, name="offs_sb")
@@ -56,13 +57,13 @@ def tile_picked_lrn8_relu_po_kernel(tc, x_words, x_scales, w1_words, w1_scales, 
         p2_sb = keep.tile([P, S // 16], U16, name="p2_sb")
 
         xs_raw = keep.tile([P, T], U8, name="xs_raw", align_bytes=64)
-        xs_got = keep.tile([P, S], U8, name="xs_got", align_bytes=64)
+        xs_got = behind.tile([P, S], U8, name="xs_got", align_bytes=64, offset=0)
         w1s_raw = keep.tile([P, H], U8, name="w1s_raw", align_bytes=64)
         w2s_raw = keep.tile([P, N], U8, name="w2s_raw", align_bytes=64)
         w2s_flat = keep.tile([P, N], U8, name="w2s_flat", align_bytes=64)
         w2s = keep.tile([P, N], U8, name="w2s", align_bytes=64)
         joined = keep.tile([P, ROWS], U8, name="joined", align_bytes=64)
-        w2w_raw = keep.tile([P, 2 * N], U8, name="w2w_raw", align_bytes=64)
+        w2w_raw = behind.tile([P, 2 * N], U8, name="w2w_raw", align_bytes=64, offset=0)
         w2w = keep.tile([P, 2 * N], U8, name="w2w", align_bytes=64)
         xw_raw = [
             later.tile([P, T], U32, name="xw_raw0", align_bytes=64, offset=0),
@@ -93,7 +94,6 @@ def tile_picked_lrn8_relu_po_kernel(tc, x_words, x_scales, w1_words, w1_scales, 
         )
         for g in range(PASSES):
             nc.sync.dma_start(xw_raw[g][:].bitcast(I32), x_words[g].rearrange("p n t -> p (n t)").bitcast(I32))
-        nc.sync.dma_start(w2w_raw[:].bitcast(I32), w2_words[0].bitcast(I32))
         nc.sync.dma_start(p1_sb[:], p1)
         nc.sync.dma_start(p2_sb[:], p2)
         nc.scalar.activation(bias[:], ones[:], ACT.Abs_reciprocal_sqrt)
@@ -102,10 +102,11 @@ def tile_picked_lrn8_relu_po_kernel(tc, x_words, x_scales, w1_words, w1_scales, 
         deal_scales(nc, joined[:, S:], w1s_raw[:])
         nc.vector.tensor_copy(joined[:, :S].bitcast(I32), xs_got[:].bitcast(I32))
         for q in range(QUADRANTS):
-            nc.scalar.dma_start(
+            nc.sync.dma_start(
                 scales1[32 * q : 32 * q + 4, :].bitcast(I32).rearrange("r (g c) -> r g c", g=PASSES),
                 joined[8 * q : 8 * q + 8, :].bitcast(I32),
             )
+        nc.sync.dma_start(w2w_raw[:].bitcast(I32), w2_words[0].bitcast(I32))
         deal_words(nc, w1w[:], w1w_raw[:])
         nc.vector.tensor_copy(xw[0][:], xw_raw[0][:].indirect(offs_sb[:]))
         deal_scales(nc, w2s_flat[:], w2s_raw[:])
@@ -157,7 +158,7 @@ def tile_picked_lrn8_relu_po_kernel(tc, x_words, x_scales, w1_words, w1_scales, 
         nc.vector.tensor_tensor(own[0][:, HALF:], y[0][:, HALF:], y[0][:, HALF:], ALU.mult)
 
         for h in range(2):
-            acc = psum.tile([P, HALF], F32, name=f"acc1_{h}", offset=BANK * (BLOCKS + h))
+            acc = psum.tile([P, HALF], F32, name=f"acc1_{h}", offset=BANK * h)
             for lo in (0, P):
                 first_product(acc[:, lo : lo + P], 1, h * HALF + lo, P, [1, 0])
             nc.scalar.activation(y[1][:, h * HALF : (h + 1) * HALF], acc[:], ACT.Relu)

@@ -162,16 +162,18 @@ def tile_picked_lrn8_relu_po_kernel(tc, x_words, x_scales, w1_words, w1_scales, 
             for lo in (0, P):
                 first_product(acc[:, lo : lo + P], 1, h * HALF + lo, P, [1, 0])
             nc.scalar.activation(y[1][:, h * HALF : (h + 1) * HALF], acc[:], ACT.Relu)
-            square(own if h == 0 else sq, 1, 0, HALF)
-        square(own, 1, HALF, HALF)
-        square(sq, 1, HALF, HALF)
+        for out in (sq, own):
+            for lo in (0, HALF):
+                square(out, 1, lo, HALF)
         for t in range(2, PACK):
             acc = psum.tile([P, S], F32, name=f"acc{t}", offset=BANK * (BLOCKS + t))
             first_product(acc[:], t, 0, S, [1, 0])
             nc.scalar.activation(y[t][:], acc[:], ACT.Relu)
-        for t in range(2, PACK):
-            square(own, t, 0, S)
-            square(sq, t, 0, S)
+        square(sq, 2, 0, S)
+        square(sq, LAST, 0, S)
+        nc.sync.dma_start(own[LAST][:], sq[LAST][:])
+        for lo in (0, HALF):
+            square(own, 2, lo, HALF)
 
         def fetch_p1(out, t, lo, n):
             nc.vector.tensor_tensor(out, sq[t][:].indirect(entries(p1_sb, lo, n)), own[t][:, lo : lo + n], ALU.add)

@@ -88,6 +88,8 @@ def tile_picked_lrn8_relu_po_kernel(tc, x_words, x_scales, w1_words, w1_scales, 
         nc.scalar.dma_start(xs_raw[0:32, :].bitcast(I32), x_scales.bitcast(I32).rearrange("g r c -> r g c"))
         nc.scalar.dma_start(w1s_raw[0:32, :].bitcast(I32), w1_scales.bitcast(I32).rearrange("g r c -> r g c"))
         nc.scalar.dma_start(w2s_raw[0:16, :].bitcast(I32), w2_scales[0].bitcast(I32))
+        gn_sb = keep.tile([P, PACK], F32, name="gn_sb")
+        nc.scalar.dma_start(gn_sb[:], gn.rearrange("(p t) o -> p (t o)", t=PACK))
         nc.sync.dma_start(
             w1w_raw[:].bitcast(I32).rearrange("p (g c) -> p g c", g=PASSES),
             w1_words.bitcast(I32).rearrange("g p c -> p g c"),
@@ -118,8 +120,6 @@ def tile_picked_lrn8_relu_po_kernel(tc, x_words, x_scales, w1_words, w1_scales, 
             nc.vector.tensor_copy(xw[1][:, lo : lo + HALF], xw_raw[1][:].indirect(entries(offs_sb, lo, HALF)))
         deal_words(nc, w2w[:], w2w_raw[:])
 
-        gn_sb = later.tile([P, PACK], F32, name="gn_sb", align_bytes=64, offset=0)
-        nc.sync.dma_start(gn_sb[:], gn.rearrange("(p t) o -> p (t o)", t=PACK))
         for q in range(QUADRANTS):
             nc.sync.dma_start(w2s[32 * q : 32 * q + 4, :].bitcast(I32), w2s_flat[4 * q : 4 * q + 4, :].bitcast(I32))
 
@@ -136,12 +136,18 @@ def tile_picked_lrn8_relu_po_kernel(tc, x_words, x_scales, w1_words, w1_scales, 
                     stop=(g == passes[-1]),
                 )
 
-        y = [keep.tile([P, S], F32, name=f"y{t}") for t in range(PACK)]
-        sq = [keep.tile([P, S], F32, name=f"sq{t}") for t in range(PACK)]
-        own = [keep.tile([P, S], F32, name=f"own{t}") for t in range(PACK)]
+        window = [keep.tile([P, 2 * S], F32, name=f"window{t}") for t in range(PACK)]
+        sq = [w[:, :S] for w in window]
+        y = [w[:, S:] for w in window]
+        own = keep.tile([P, S], F32, name="own")
+        near = [keep.tile([P, S], F32, name=f"near{t}") for t in range(PACK)]
+        partial = [keep.tile([P, S], F32, name=f"partial{t}") for t in range(PACK)]
+        total = keep.tile([P, PACK, S], F32, name="total")
+        gained = keep.tile([P, PACK, S], F32, name="gained")
+        root = keep.tile([P, PACK, S], F32, name="root")
 
-        def square(out, t, lo, n):
-            nc.scalar.activation(out[t][:, lo : lo + n], y[t][:, lo : lo + n], ACT.Square)
+        def square(t, lo, n):
+            nc.scalar.activation(sq[t][:, lo : lo + n], y[t][:, lo : lo + n], ACT.Square)
 
         for c in range(BLOCKS):
             columns = slice(c * P, (c + 1) * P)
@@ -150,69 +156,60 @@ def tile_picked_lrn8_relu_po_kernel(tc, x_words, x_scales, w1_words, w1_scales, 
             if c * P < HALF:
                 nc.scalar.activation(y[0][:, columns], acc[:], ACT.Relu)
                 if (c + 1) * P == HALF:
-                    square(sq, 0, 0, HALF)
+                    square(0, 0, HALF)
             else:
                 nc.vector.tensor_scalar_max(y[0][:, columns], acc[:], 0.0)
-                square(sq, 0, c * P, P)
-        nc.vector.tensor_copy(own[0][:, :HALF], sq[0][:, :HALF])
-        nc.vector.tensor_tensor(own[0][:, HALF:], y[0][:, HALF:], y[0][:, HALF:], ALU.mult)
+                square(0, c * P, P)
+        nc.vector.tensor_copy(own[:, :HALF], sq[0][:, :HALF])
+        nc.vector.tensor_tensor(own[:, HALF:], y[0][:, HALF:], y[0][:, HALF:], ALU.mult)
+
+        def fetch_p2(t):
+            for lo in (0, HALF):
+                nc.vector.tensor_tensor(total[:, t, lo : lo + HALF], window[t][:].indirect(entries(p2_sb, lo, HALF)), partial[t][:, lo : lo + HALF], ALU.add)
+
+        def gain(t):
+            nc.vector.tensor_scalar(gained[:, t, :], y[t], gn_sb[:, t : t + 1], None, ALU.mult)
+
+        for lo in (0, HALF):
+            nc.vector.tensor_tensor(partial[0][:, lo : lo + HALF], window[0][:].indirect(entries(p1_sb, lo, HALF)), own[:, lo : lo + HALF], ALU.add)
+        fetch_p2(0)
+        gain(0)
 
         for h in range(2):
             acc = psum.tile([P, HALF], F32, name=f"acc1_{h}", offset=BANK * h)
             for lo in (0, P):
                 first_product(acc[:, lo : lo + P], 1, h * HALF + lo, P, [1, 0])
             nc.scalar.activation(y[1][:, h * HALF : (h + 1) * HALF], acc[:], ACT.Relu)
-        for out in (sq, own):
-            for lo in (0, HALF):
-                square(out, 1, lo, HALF)
-        for t in range(2, PACK):
+        for lo in (0, HALF):
+            square(1, lo, HALF)
+        gain(1)
+
+        def project(t):
             acc = psum.tile([P, S], F32, name=f"acc{t}", offset=BANK * (BLOCKS + t))
             first_product(acc[:], t, 0, S, [1, 0])
-            nc.scalar.activation(y[t][:], acc[:], ACT.Relu)
-        square(sq, 2, 0, S)
-        square(sq, LAST, 0, S)
-        nc.sync.dma_start(own[LAST][:], sq[LAST][:])
-        for lo in (0, HALF):
-            square(own, 2, lo, HALF)
+            nc.scalar.activation(y[t], acc[:], ACT.Relu)
+            gain(t)
 
-        def fetch_p1(out, t, lo, n):
-            nc.vector.tensor_tensor(out, sq[t][:].indirect(entries(p1_sb, lo, n)), own[t][:, lo : lo + n], ALU.add)
-
-        def fetch_p2(out, t, lo, n, so_far):
-            nc.vector.tensor_tensor(out, sq[t][:].indirect(entries(p2_sb, lo, n)), so_far, ALU.add)
-
-        near = [keep.tile([P, S], F32, name=f"near{t}") for t in range(LAST)]
-        total = keep.tile([P, LAST, S], F32, name="total")
-        for t in range(LAST):
+        def look_up(t):
+            nc.scalar.activation(near[t][:], window[t][:].indirect(p1_sb[:]), ACT.Copy)
             for lo in (0, HALF):
-                fetch_p1(near[t][:, lo : lo + HALF], t, lo, HALF)
-            for lo in (0, HALF):
-                fetch_p2(total[:, t, lo : lo + HALF], t, lo, HALF, near[t][:, lo : lo + HALF])
+                nc.vector.tensor_tensor(partial[t][:, lo : lo + HALF], near[t][:, lo : lo + HALF], sq[t][:, lo : lo + HALF], ALU.add)
+            fetch_p2(t)
 
-        gained = spent.tile([P, PACK, S], F32, name="gained", align_bytes=64, offset=0)
-        root_early = spent.tile([P, PACK, HALF], F32, name="root_early", align_bytes=64, offset=2048 * 4)
+        def take_root(tiles, lo, one=1.0):
+            nc.scalar.activation(root[:, tiles, lo : lo + HALF], total[:, tiles, lo : lo + HALF], ACT.Abs_reciprocal_sqrt, bias=one, scale=0.5)
 
-        def gain(t, lo, n):
-            nc.scalar.activation(gained[:, t, lo : lo + n], y[t][:, lo : lo + n], ACT.Copy, scale=gn_sb[:, t : t + 1])
-
-        def take_root(out, sums, one=1.0):
-            nc.scalar.activation(out, sums, ACT.Abs_reciprocal_sqrt, bias=one, scale=0.5)
-
-        for t in range(PACK):
-            gain(t, 0, S if t < 2 else HALF)
-        take_root(root_early[:, 0:2, :], total[:, 0:2, :HALF], bias[:])
-        take_root(root_early[:, 2, :], total[:, 2, :HALF])
-
-        near_early = [chain.tile([P, P], F32, name=f"near_early{c}", align_bytes=64, offset=BLOCK_BYTES * (1 + 3 * c)) for c in range(2)]
-        near_late = chain.tile([P, HALF], F32, name="near_late", align_bytes=64, offset=0)
-        near_last = [near_early[0][:], near_early[1][:], near_late[:, :P], near_late[:, P:]]
-        total_last = [chain.tile([P, P], F32, name=f"total_last{c}", align_bytes=64, offset=BLOCK_BYTES * (2 + c % 2)) for c in range(BLOCKS)]
-        root_late = chain.tile([P, PACK, HALF], F32, name="root_late", align_bytes=64, offset=BLOCK_BYTES * 4)
-        root = [root_early[:, :, :P], root_early[:, :, P:], root_late[:, :, :P], root_late[:, :, P:]]
-
-        def finish_last(c):
-            fetch_p2(total_last[c][:], LAST, c * P, P, near_last[c])
-            take_root(root[c][:, LAST, :], total_last[c][:])
+        project(2)
+        look_up(1)
+        square(2, 0, S)
+        project(3)
+        look_up(2)
+        square(3, 0, S)
+        look_up(3)
+        take_root(slice(0, 3), 0, bias[:])
+        take_root(3, 0)
+        take_root(slice(0, 3), HALF)
+        take_root(3, HALF)
 
         z_in = [keep.tile([P, P * PACK], BF16, name=f"z_in{c}", align_bytes=64) for c in range(BLOCKS)]
         z_words = [keep.tile([P, P], U32, name=f"z_words{c}", align_bytes=64) for c in range(BLOCKS)]
@@ -224,11 +221,11 @@ def tile_picked_lrn8_relu_po_kernel(tc, x_words, x_scales, w1_words, w1_scales, 
         def interleaved(values):
             return values.rearrange("p (c i t) -> p c t i", i=4, t=PACK)
 
-        def normalise(c, lo=0, n=P):
+        def normalise(c):
             nc.vector.tensor_tensor(
-                interleaved(z_in[c][:, lo * PACK : (lo + n) * PACK]),
-                by_fours(gained[:, :, c * P + lo : c * P + lo + n]),
-                by_fours(root[c][:, :, lo : lo + n]),
+                interleaved(z_in[c][:]),
+                by_fours(gained[:, :, c * P : (c + 1) * P]),
+                by_fours(root[:, :, c * P : (c + 1) * P]),
                 ALU.mult,
             )
 
@@ -277,41 +274,25 @@ def tile_picked_lrn8_relu_po_kernel(tc, x_words, x_scales, w1_words, w1_scales, 
         def store_words(queue, lo):
             queue.dma_start(out_codes[:, lo : lo + HALF], out_words[:, lo : lo + HALF].bitcast(I32))
 
-        for c in range(2):
-            fetch_p1(near_last[c], LAST, c * P, P)
-        for c in range(2):
-            finish_last(c)
-        take_root(root_late[:, 0:LAST, :], total[:, :, HALF:])
-        for t in range(2, PACK):
-            gain(t, HALF, HALF)
-        fetch_p1(near_late[:], LAST, HALF, HALF)
-
-        normalise(0)
-        finish_last(2)
-        second_product(0)
-        normalise(1)
-        finish_last(3)
-        second_product(1)
+        for h in range(2):
+            normalise(2 * h)
+            normalise(2 * h + 1)
+            second_product(2 * h)
+            second_product(2 * h + 1)
         empty(0)
-        round_on_scalar(0, banks[0])
-        normalise(2)
-        normalise(3, 0, P // 2)
-        second_product(2)
-        normalise(3, P // 2, P // 2)
-        quantise_result(0, P)
-        second_product(3)
-
         empty(1)
         empty(2)
+        round_on_vector(0)
         round_on_vector(1)
+        quantise_result(0, P)
         nc.vector.tensor_copy(res[3][:, 0:2, :], last_banks[0][:])
         nc.scalar.copy(res[3][:, 2:4, :], last_banks[1][:])
         store_block(3)
+        quantise_result(P, P)
+        store_words(nc.sync, 0)
         round_on_vector(2)
         round_on_vector(3, P // 2)
         round_on_scalar(3, res[3], P // 2)
-        quantise_result(P, P)
-        store_words(nc.sync, 0)
         quantise_result(2 * P, P)
         quantise_result(3 * P, P)
         store_words(nc.scalar, HALF)

@@ -25,7 +25,7 @@ LAST = PACK - 1
 BANK = 2048
 QUADRANTS = 4
 ROWS = S + H
-BLOCK_BYTES = 4 * P
+LARGE = 2.0**126
 
 
 def deal_words(nc, dealt, raw):
@@ -69,7 +69,10 @@ def tile_picked_lrn8_relu_po_kernel(tc, x_words, x_scales, w1_words, w1_scales, 
             later.tile([P, T], U32, name="xw_raw0", align_bytes=64, offset=0),
             keep.tile([P, T], U32, name="xw_raw1", align_bytes=64),
         ]
-        xw = [spent.tile([P, S], U32, name=f"xw{g}", align_bytes=64, offset=2048 * g) for g in range(PASSES)]
+        xw = [
+            spent.tile([P, S], U32, name="xw0", align_bytes=64, offset=0),
+            later.tile([P, S], U32, name="xw1", align_bytes=64, offset=0),
+        ]
         w1w_raw = spent.tile([P, PASSES * 2 * H], U8, name="w1w_raw", align_bytes=64, offset=2048 * 2)
         w1w = spent.tile([P, PASSES * 2 * H], U8, name="w1w", align_bytes=64, offset=2048 * 3)
         scales1 = spent.tile([P, PASSES * ROWS], U8, name="scales1", align_bytes=64, offset=2048 * 4)
@@ -111,6 +114,13 @@ def tile_picked_lrn8_relu_po_kernel(tc, x_words, x_scales, w1_words, w1_scales, 
         nc.sync.dma_start(w2w_raw[:].bitcast(I32), w2_words[0].bitcast(I32))
         deal_words(nc, w1w[:], w1w_raw[:])
         nc.vector.tensor_copy(xw[0][:], xw_raw[0][:].indirect(offs_sb[:]))
+        total = keep.tile([P, LAST, S], F32, name="total", align_bytes=64)
+        inverse_raw = later.tile([P, PACK], F32, name="inverse_raw", align_bytes=64, offset=0)
+        inverse_last = keep.tile([P, 1], F32, name="inverse_last")
+        inverse = [total[:, 0, S - LAST + t : S - LAST + t + 1] for t in range(LAST)] + [inverse_last[:]]
+        nc.vector.reciprocal(inverse_raw[:], gn_sb[:])
+        nc.vector.tensor_scalar(total[:, 0, S - LAST :], inverse_raw[:, :LAST], LARGE, -LARGE, ALU.min, ALU.max)
+        nc.vector.tensor_scalar(inverse_last[:], inverse_raw[:, LAST:], LARGE, -LARGE, ALU.min, ALU.max)
         deal_scales(nc, w2s_flat[:], w2s_raw[:])
 
         def entries(lists, lo, n):
@@ -136,80 +146,91 @@ def tile_picked_lrn8_relu_po_kernel(tc, x_words, x_scales, w1_words, w1_scales, 
                     stop=(g == passes[-1]),
                 )
 
-        window = [keep.tile([P, 2 * S], F32, name=f"window{t}") for t in range(PACK)]
-        sq = [w[:, :S] for w in window]
-        y = [w[:, S:] for w in window]
-        own = keep.tile([P, S], F32, name="own")
-        near = [keep.tile([P, S], F32, name=f"near{t}") for t in range(PACK)]
-        partial = [keep.tile([P, S], F32, name=f"partial{t}") for t in range(PACK)]
-        total = keep.tile([P, PACK, S], F32, name="total")
-        gained = keep.tile([P, PACK, S], F32, name="gained")
-        root = keep.tile([P, PACK, S], F32, name="root")
+        gained = keep.tile([P, PACK, S], F32, name="gained", align_bytes=64)
+        sq = [keep.tile([P, S], F32, name=f"sq{t}", align_bytes=64) for t in range(PACK)]
+        own = keep.tile([P, HALF], F32, name="own", align_bytes=64)
+        near = [[chain.tile([P, HALF], F32, name=f"near{t}_{h}", align_bytes=64, offset=4 * HALF * ((4, 5, 0, 6), (7, 8, 9, 10))[h][t]) for h in range(2)] for t in range(PACK)]
+        root_early = chain.tile([P, PACK, HALF], F32, name="root_early", align_bytes=64, offset=0)
+        partial = keep.tile([P, LAST, S], F32, name="partial", align_bytes=64)
+        last = keep.tile([P, HALF + PACK * HALF], F32, name="last", align_bytes=64)
+        partial_last = [last[:, P : P + HALF], last[:, :HALF]]
+        root_late = last[:, HALF:].rearrange("p (t j) -> p t j", t=PACK)
+        total_last = keep.tile([P, HALF], F32, name="total_last", align_bytes=64)
+        root = [root_early[:, :, :P], root_early[:, :, P:], root_late[:, :, :P], root_late[:, :, P:]]
+
+        def gain(t, acc, lo, n):
+            nc.vector.tensor_scalar(gained[:, t, lo : lo + n], acc, 0.0, gn_sb[:, t : t + 1], ALU.max, ALU.mult)
 
         def square(t, lo, n):
-            nc.scalar.activation(sq[t][:, lo : lo + n], y[t][:, lo : lo + n], ACT.Square)
+            nc.scalar.activation(sq[t][:, lo : lo + n], gained[:, t, lo : lo + n], ACT.Square, scale=inverse[t])
+
+        def fetch_p1(t, h):
+            nc.scalar.activation(near[t][h][:], sq[t][:].indirect(entries(p1_sb, h * HALF, HALF)), ACT.Copy)
+
+        def partial_of(t, h):
+            return partial[:, t, h * HALF : (h + 1) * HALF] if t < LAST else partial_last[h]
+
+        def add_own(t, h):
+            nc.vector.tensor_tensor(partial_of(t, h), near[t][h][:], sq[t][:, h * HALF : (h + 1) * HALF], ALU.add)
+
+        def fetch_p2(out, t, lo, n, so_far):
+            nc.vector.tensor_tensor(out, sq[t][:].indirect(entries(p2_sb, lo, n)), so_far, ALU.add)
+
+        def finish(t, h):
+            fetch_p2(total[:, t, h * HALF : (h + 1) * HALF], t, h * HALF, HALF, partial_of(t, h))
+
+        def take_root(out, sums, one=1.0):
+            nc.scalar.activation(out, sums, ACT.Abs_reciprocal_sqrt, bias=one, scale=0.5)
+
+        def finish_last(c):
+            sums = total_last[:, c % 2 * P : (c % 2 + 1) * P]
+            fetch_p2(sums, LAST, c * P, P, partial_last[c // 2][:, c % 2 * P : (c % 2 + 1) * P])
+            take_root(root[c][:, LAST, :], sums)
 
         for c in range(BLOCKS):
-            columns = slice(c * P, (c + 1) * P)
             acc = psum.tile([P, P], F32, name=f"acc0_{c}", offset=BANK * c)
             first_product(acc[:], 0, c * P, P, [0, 1])
-            if c * P < HALF:
-                nc.scalar.activation(y[0][:, columns], acc[:], ACT.Relu)
-                if (c + 1) * P == HALF:
-                    square(0, 0, HALF)
-            else:
-                nc.vector.tensor_scalar_max(y[0][:, columns], acc[:], 0.0)
-                square(0, c * P, P)
-        nc.vector.tensor_copy(own[:, :HALF], sq[0][:, :HALF])
-        nc.vector.tensor_tensor(own[:, HALF:], y[0][:, HALF:], y[0][:, HALF:], ALU.mult)
-
-        def fetch_p2(t):
-            for lo in (0, HALF):
-                nc.vector.tensor_tensor(total[:, t, lo : lo + HALF], window[t][:].indirect(entries(p2_sb, lo, HALF)), partial[t][:, lo : lo + HALF], ALU.add)
-
-        def gain(t):
-            nc.vector.tensor_scalar(gained[:, t, :], y[t], gn_sb[:, t : t + 1], None, ALU.mult)
-
-        for lo in (0, HALF):
-            nc.vector.tensor_tensor(partial[0][:, lo : lo + HALF], window[0][:].indirect(entries(p1_sb, lo, HALF)), own[:, lo : lo + HALF], ALU.add)
-        fetch_p2(0)
-        gain(0)
-
+            gain(0, acc[:], c * P, P)
+            square(0, c * P, P)
+        nc.vector.tensor_copy(own[:], sq[0][:, :HALF])
+        halves = [psum.tile([P, HALF], F32, name=f"acc1_{h}", offset=BANK * h) for h in range(2)]
         for h in range(2):
-            acc = psum.tile([P, HALF], F32, name=f"acc1_{h}", offset=BANK * h)
-            for lo in (0, P):
-                first_product(acc[:, lo : lo + P], 1, h * HALF + lo, P, [1, 0])
-            nc.scalar.activation(y[1][:, h * HALF : (h + 1) * HALF], acc[:], ACT.Relu)
-        for lo in (0, HALF):
-            square(1, lo, HALF)
-        gain(1)
-
-        def project(t):
-            acc = psum.tile([P, S], F32, name=f"acc{t}", offset=BANK * (BLOCKS + t))
-            first_product(acc[:], t, 0, S, [1, 0])
-            nc.scalar.activation(y[t], acc[:], ACT.Relu)
-            gain(t)
-
-        def look_up(t):
-            nc.scalar.activation(near[t][:], window[t][:].indirect(p1_sb[:]), ACT.Copy)
-            for lo in (0, HALF):
-                nc.vector.tensor_tensor(partial[t][:, lo : lo + HALF], near[t][:, lo : lo + HALF], sq[t][:, lo : lo + HALF], ALU.add)
-            fetch_p2(t)
-
-        def take_root(tiles, lo, one=1.0):
-            nc.scalar.activation(root[:, tiles, lo : lo + HALF], total[:, tiles, lo : lo + HALF], ACT.Abs_reciprocal_sqrt, bias=one, scale=0.5)
-
-        project(2)
-        look_up(1)
+            first_product(halves[h][:], 1, h * HALF, HALF, [1, 0])
+        wholes = {t: psum.tile([P, S], F32, name=f"acc{t}", offset=BANK * (BLOCKS + t)) for t in (2, 3)}
+        for t in (2, 3):
+            first_product(wholes[t][:], t, 0, S, [1, 0])
+        gain(1, halves[0][:], 0, HALF)
+        fetch_p1(0, 0)
+        fetch_p2(partial[:, 0, :HALF], 0, 0, HALF, own[:])
+        gain(1, halves[1][:], HALF, HALF)
+        fetch_p1(0, 1)
+        nc.vector.tensor_tensor(total[:, 0, :HALF], partial[:, 0, :HALF], near[0][0][:], ALU.add)
+        square(1, 0, S)
+        gain(2, wholes[2][:], 0, S)
+        add_own(0, 1)
+        gain(3, wholes[3][:], 0, S)
         square(2, 0, S)
-        project(3)
-        look_up(2)
+        finish(0, 1)
+        for h in range(2):
+            fetch_p1(1, h)
+            add_own(1, h)
         square(3, 0, S)
-        look_up(3)
-        take_root(slice(0, 3), 0, bias[:])
-        take_root(3, 0)
-        take_root(slice(0, 3), HALF)
-        take_root(3, HALF)
+        for h in range(2):
+            finish(1, h)
+        for h in range(2):
+            fetch_p1(2, h)
+            add_own(2, h)
+        fetch_p1(3, 0)
+        finish(2, 0)
+        take_root(root_early[:, 0:2, :], total[:, 0:2, :HALF], bias[:])
+        add_own(3, 0)
+        fetch_p1(3, 1)
+        finish(2, 1)
+        take_root(root_early[:, 2, :], total[:, 2, :HALF])
+        for c in range(2):
+            finish_last(c)
+        add_own(3, 1)
+        take_root(root_late[:, 0:LAST, :], total[:, :, HALF:])
 
         z_in = [keep.tile([P, P * PACK], BF16, name=f"z_in{c}", align_bytes=64) for c in range(BLOCKS)]
         z_words = [keep.tile([P, P], U32, name=f"z_words{c}", align_bytes=64) for c in range(BLOCKS)]
@@ -221,11 +242,11 @@ def tile_picked_lrn8_relu_po_kernel(tc, x_words, x_scales, w1_words, w1_scales, 
         def interleaved(values):
             return values.rearrange("p (c i t) -> p c t i", i=4, t=PACK)
 
-        def normalise(c):
+        def normalise(c, lo=0, n=P):
             nc.vector.tensor_tensor(
-                interleaved(z_in[c][:]),
-                by_fours(gained[:, :, c * P : (c + 1) * P]),
-                by_fours(root[:, :, c * P : (c + 1) * P]),
+                interleaved(z_in[c][:, lo * PACK : (lo + n) * PACK]),
+                by_fours(gained[:, :, c * P + lo : c * P + lo + n]),
+                by_fours(root[c][:, :, lo : lo + n]),
                 ALU.mult,
             )
 
@@ -274,25 +295,32 @@ def tile_picked_lrn8_relu_po_kernel(tc, x_words, x_scales, w1_words, w1_scales, 
         def store_words(queue, lo):
             queue.dma_start(out_codes[:, lo : lo + HALF], out_words[:, lo : lo + HALF].bitcast(I32))
 
-        for h in range(2):
-            normalise(2 * h)
-            normalise(2 * h + 1)
-            second_product(2 * h)
-            second_product(2 * h + 1)
+        normalise(0)
+        finish_last(2)
+        second_product(0)
+        normalise(1)
+        finish_last(3)
+        second_product(1)
         empty(0)
+        round_on_scalar(0, banks[0])
+        normalise(2)
+        normalise(3, 0, P // 2)
+        second_product(2)
+        normalise(3, P // 2, P // 2)
+        quantise_result(0, P)
+        second_product(3)
+
         empty(1)
         empty(2)
-        round_on_vector(0)
         round_on_vector(1)
-        quantise_result(0, P)
         nc.vector.tensor_copy(res[3][:, 0:2, :], last_banks[0][:])
         nc.scalar.copy(res[3][:, 2:4, :], last_banks[1][:])
         store_block(3)
-        quantise_result(P, P)
-        store_words(nc.sync, 0)
         round_on_vector(2)
         round_on_vector(3, P // 2)
         round_on_scalar(3, res[3], P // 2)
+        quantise_result(P, P)
+        store_words(nc.sync, 0)
         quantise_result(2 * P, P)
         quantise_result(3 * P, P)
         store_words(nc.scalar, HALF)

@@ -182,10 +182,15 @@ def tile_picked_lrn8_relu_po_kernel(tc, x_words, x_scales, w1_words, w1_scales, 
         def take_root(out, sums, one=1.0):
             nc.scalar.activation(out, sums, ACT.Abs_reciprocal_sqrt, bias=one, scale=0.5)
 
+        far_late = keep.tile([P, HALF], F32, name="far_late", align_bytes=64)
+
         def finish_last(c):
-            sums = total_last[:, c % 2 * P : (c % 2 + 1) * P]
-            fetch_p2(sums, LAST, c * P, P, partial_last[c // 2][:, c % 2 * P : (c % 2 + 1) * P])
-            take_root(root[c][:, LAST, :], sums)
+            columns = slice(c % 2 * P, (c % 2 + 1) * P)
+            if c < 2:
+                fetch_p2(total_last[:, columns], LAST, c * P, P, partial_last[0][:, columns])
+            else:
+                nc.vector.tensor_tensor(total_last[:, columns], partial_last[1][:, columns], far_late[:, columns], ALU.add)
+            take_root(root[c][:, LAST, :], total_last[:, columns])
 
         for c in range(BLOCKS):
             acc = psum.tile([P, P], F32, name=f"acc0_{c}", offset=BANK * c)
@@ -225,6 +230,7 @@ def tile_picked_lrn8_relu_po_kernel(tc, x_words, x_scales, w1_words, w1_scales, 
         take_root(root_early[:, 0:2, :], total[:, 0:2, :HALF], bias[:])
         add_own(3, 0)
         fetch_p1(3, 1)
+        nc.scalar.activation(far_late[:], sq[LAST][:].indirect(entries(p2_sb, HALF, HALF)), ACT.Copy)
         finish(2, 1)
         take_root(root_early[:, 2, :], total[:, 2, :HALF])
         for c in range(2):
@@ -236,17 +242,17 @@ def tile_picked_lrn8_relu_po_kernel(tc, x_words, x_scales, w1_words, w1_scales, 
         z_words = [keep.tile([P, P], U32, name=f"z_words{c}", align_bytes=64) for c in range(BLOCKS)]
         z_scales = [keep.tile([P, P], U8, name=f"z_scales{c}", align_bytes=64) for c in range(BLOCKS)]
 
-        def by_fours(tiles):
-            return tiles.rearrange("p t (c i) -> p c t i", i=4)
+        def by_fours(tiles, run=4):
+            return tiles.rearrange("p t (c i) -> p c t i", i=run)
 
-        def interleaved(values):
-            return values.rearrange("p (c i t) -> p c t i", i=4, t=PACK)
+        def interleaved(values, run=4):
+            return values.rearrange("p (c i t) -> p c t i", i=run, t=PACK)
 
         def normalise(c, lo=0, n=P):
             nc.vector.tensor_tensor(
-                interleaved(z_in[c][:, lo * PACK : (lo + n) * PACK]),
-                by_fours(gained[:, :, c * P + lo : c * P + lo + n]),
-                by_fours(root[c][:, :, lo : lo + n]),
+                interleaved(z_in[c][:, lo * PACK : (lo + n) * PACK], 2),
+                by_fours(gained[:, :, c * P + lo : c * P + lo + n], 2),
+                by_fours(root[c][:, :, lo : lo + n], 2),
                 ALU.mult,
             )
 
@@ -307,8 +313,8 @@ def tile_picked_lrn8_relu_po_kernel(tc, x_words, x_scales, w1_words, w1_scales, 
         normalise(3, 0, P // 2)
         second_product(2)
         normalise(3, P // 2, P // 2)
-        quantise_result(0, P)
         second_product(3)
+        quantise_result(0, P)
 
         empty(1)
         empty(2)

@@ -126,8 +126,8 @@ def tile_picked_lrn8_relu_po_kernel(tc, x_words, x_scales, w1_words, w1_scales, 
         def entries(lists, lo, n):
             return lists[:, lo // 16 : (lo + n) // 16]
 
-        for lo in (0, HALF):
-            nc.vector.tensor_copy(xw[1][:, lo : lo + HALF], xw_raw[1][:].indirect(entries(offs_sb, lo, HALF)))
+        for lo in range(0, S, P):
+            nc.vector.tensor_copy(xw[1][:, lo : lo + P], xw_raw[1][:].indirect(entries(offs_sb, lo, P)))
         deal_words(nc, w2w[:], w2w_raw[:])
 
         for q in range(QUADRANTS):

from contextlib import ExitStack

import concourse.mybir as mybir

K, T, S, N, H = 1024, 2048, 512, 512, 512
FLOPS = 2 * K * H * S + 2 * H * N * S

F32 = mybir.dt.float32
BF16 = mybir.dt.bfloat16
I32 = mybir.dt.int32
U32 = mybir.dt.uint32
U16 = mybir.dt.uint16
U8 = mybir.dt.uint8
FP8X4 = mybir.dt.float8_e4m3fn_x4
FP4X4 = mybir.dt.float4_e2m1fn_x4
ACT = mybir.ActivationFunctionType
ALU = mybir.AluOpType

P = 128
PACK = 4
PASSES = K // 512
BLOCKS = S // P
HALF = S // 2
LAST = PACK - 1
BANK = 2048
QUADRANTS = 4
ROWS = S + H
LARGE = 2.0**126


def deal_words(nc, dealt, raw):
    nc.vector.tensor_copy(
        out=dealt.bitcast(U16).rearrange("p (t c m) -> p c t m", t=PACK, m=8),
        in_=raw.bitcast(U16).rearrange("p (c m t) -> p c t m", t=PACK, m=8),
    )


def deal_scales(nc, dealt, raw):
    nc.vector.tensor_copy(
        out=dealt.rearrange("p (t c m) -> p c t m", t=PACK, m=16),
        in_=raw.rearrange("p (c m t) -> p c t m", t=PACK, m=16),
    )


def tile_picked_lrn8_relu_po_kernel(tc, x_words, x_scales, w1_words, w1_scales, gn, w2_words, w2_scales, offs, p1, p2, out_0, out_1, out_2):
    nc = tc.nc
    with ExitStack() as ctx:
        keep = ctx.enter_context(tc.tile_pool(name="keep", bufs=1))
        later = ctx.enter_context(tc.tile_pool(name="later", bufs=1))
        spent = ctx.enter_context(tc.tile_pool(name="spent", bufs=1))
        chain = ctx.enter_context(tc.tile_pool(name="chain", bufs=1))
        behind = ctx.enter_context(tc.tile_pool(name="behind", bufs=1))
        psum = ctx.enter_context(tc.psum_pool(name="psum", bufs=1))

        offs_sb = keep.tile([P, S // 16], U16, name="offs_sb")
        p1_sb = keep.tile([P, S // 16], U16, name="p1_sb")
        p2_sb = keep.tile([P, S // 16], U16, name="p2_sb")

        xs_raw = keep.tile([P, T], U8, name="xs_raw", align_bytes=64)
        xs_got = behind.tile([P, S], U8, name="xs_got", align_bytes=64, offset=0)
        w1s_raw = keep.tile([P, H], U8, name="w1s_raw", align_bytes=64)
        w2s_raw = keep.tile([P, N], U8, name="w2s_raw", align_bytes=64)
        w2s_flat = keep.tile([P, N], U8, name="w2s_flat", align_bytes=64)
        w2s = keep.tile([P, N], U8, name="w2s", align_bytes=64)
        joined = keep.tile([P, ROWS], U8, name="joined", align_bytes=64)
        w2w_raw = behind.tile([P, 2 * N], U8, name="w2w_raw", align_bytes=64, offset=0)
        w2w = keep.tile([P, 2 * N], U8, name="w2w", align_bytes=64)
        xw_raw = [
            later.tile([P, T], U32, name="xw_raw0", align_bytes=64, offset=0),
            keep.tile([P, T], U32, name="xw_raw1", align_bytes=64),
        ]
        xw = [
            spent.tile([P, S], U32, name="xw0", align_bytes=64, offset=0),
            later.tile([P, S], U32, name="xw1", align_bytes=64, offset=0),
        ]
        w1w_raw = spent.tile([P, PASSES * 2 * H], U8, name="w1w_raw", align_bytes=64, offset=2048 * 2)
        w1w = spent.tile([P, PASSES * 2 * H], U8, name="w1w", align_bytes=64, offset=2048 * 3)
        scales1 = spent.tile([P, PASSES * ROWS], U8, name="scales1", align_bytes=64, offset=2048 * 4)
        ones = keep.tile([P, 1], F32, name="ones")
        bias = keep.tile([P, 1], F32, name="bias")

        nc.vector.memset(w2s_raw[:].bitcast(I32), 0)
        nc.vector.memset(ones[:], 1.0)
        for raw in (xs_raw, w1s_raw):
            nc.vector.memset(raw[32:64, :].bitcast(I32), 0)
            nc.vector.memset(raw[64:128, :].bitcast(I32), 0)
        nc.vector.memset(scales1[:].bitcast(I32), 0)
        nc.vector.memset(w2s[:].bitcast(I32), 0)

        nc.sync.dma_start(offs_sb[:], offs)
        nc.scalar.dma_start(xs_raw[0:32, :].bitcast(I32), x_scales.bitcast(I32).rearrange("g r c -> r g c"))
        nc.scalar.dma_start(w1s_raw[0:32, :].bitcast(I32), w1_scales.bitcast(I32).rearrange("g r c -> r g c"))
        nc.scalar.dma_start(w2s_raw[0:16, :].bitcast(I32), w2_scales[0].bitcast(I32))
        gn_sb = keep.tile([P, PACK], F32, name="gn_sb")
        nc.scalar.dma_start(gn_sb[:], gn.rearrange("(p t) o -> p (t o)", t=PACK))
        nc.sync.dma_start(
            w1w_raw[:].bitcast(I32).rearrange("p (g c) -> p g c", g=PASSES),
            w1_words.bitcast(I32).rearrange("g p c -> p g c"),
        )
        for g in range(PASSES):
            nc.sync.dma_start(xw_raw[g][:].bitcast(I32), x_words[g].rearrange("p n t -> p (n t)").bitcast(I32))
        nc.sync.dma_start(p1_sb[:], p1)
        nc.sync.dma_start(p2_sb[:], p2)
        nc.scalar.activation(bias[:], ones[:], ACT.Abs_reciprocal_sqrt)

        nc.vector.tensor_copy(xs_got[:], xs_raw[:].indirect(offs_sb[:]))
        deal_scales(nc, joined[:, S:], w1s_raw[:])
        nc.vector.tensor_copy(joined[:, :S].bitcast(I32), xs_got[:].bitcast(I32))
        for q in range(QUADRANTS):
            nc.sync.dma_start(
                scales1[32 * q : 32 * q + 4, :].bitcast(I32).rearrange("r (g c) -> r g c", g=PASSES),
                joined[8 * q : 8 * q + 8, :].bitcast(I32),
            )
        nc.sync.dma_start(w2w_raw[:].bitcast(I32), w2_words[0].bitcast(I32))
        deal_words(nc, w1w[:], w1w_raw[:])
        nc.vector.tensor_copy(xw[0][:], xw_raw[0][:].indirect(offs_sb[:]))
        total = keep.tile([P, LAST, S], F32, name="total", align_bytes=64)
        inverse_raw = later.tile([P, PACK], F32, name="inverse_raw", align_bytes=64, offset=0)
        inverse_last = keep.tile([P, 1], F32, name="inverse_last")
        inverse = [total[:, 0, S - LAST + t : S - LAST + t + 1] for t in range(LAST)] + [inverse_last[:]]
        nc.vector.reciprocal(inverse_raw[:], gn_sb[:])
        nc.vector.tensor_scalar(total[:, 0, S - LAST :], inverse_raw[:, :LAST], LARGE, -LARGE, ALU.min, ALU.max)
        nc.vector.tensor_scalar(inverse_last[:], inverse_raw[:, LAST:], LARGE, -LARGE, ALU.min, ALU.max)
        deal_scales(nc, w2s_flat[:], w2s_raw[:])

        def entries(lists, lo, n):
            return lists[:, lo // 16 : (lo + n) // 16]

        for lo in range(0, S, P):
            nc.vector.tensor_copy(xw[1][:, lo : lo + P], xw_raw[1][:].indirect(entries(offs_sb, lo, P)))
        deal_words(nc, w2w[:], w2w_raw[:])

        for q in range(QUADRANTS):
            nc.sync.dma_start(w2s[32 * q : 32 * q + 4, :].bitcast(I32), w2s_flat[4 * q : 4 * q + 4, :].bitcast(I32))

        def first_product(acc, t, lo, n, passes):
            for g in passes:
                column = (t * PASSES + g) * P
                nc.tensor.matmul_mx(
                    out=acc,
                    lhsT=w1w[:, 2 * column : 2 * column + 2 * P].bitcast(FP4X4),
                    lhsT_scale=scales1[:, g * ROWS + S + t * P : g * ROWS + S + (t + 1) * P],
                    rhs=xw[g][:, lo : lo + n].bitcast(FP8X4),
                    rhs_scale=scales1[:, g * ROWS + lo : g * ROWS + lo + n],
                    start=(g == passes[0]),
                    stop=(g == passes[-1]),
                )

        gained = keep.tile([P, PACK, S], F32, name="gained", align_bytes=64)
        sq = [keep.tile([P, S], F32, name=f"sq{t}", align_bytes=64) for t in range(PACK)]
        own = keep.tile([P, HALF], F32, name="own", align_bytes=64)
        near = [[chain.tile([P, HALF], F32, name=f"near{t}_{h}", align_bytes=64, offset=4 * HALF * ((4, 5, 0, 6), (7, 8, 9, 10))[h][t]) for h in range(2)] for t in range(PACK)]
        root_early = chain.tile([P, PACK, HALF], F32, name="root_early", align_bytes=64, offset=0)
        partial = keep.tile([P, LAST, S], F32, name="partial", align_bytes=64)
        last = keep.tile([P, HALF + PACK * HALF], F32, name="last", align_bytes=64)
        partial_last = [last[:, P : P + HALF], last[:, :HALF]]
        root_late = last[:, HALF:].rearrange("p (t j) -> p t j", t=PACK)
        total_last = keep.tile([P, HALF], F32, name="total_last", align_bytes=64)
        root = [root_early[:, :, :P], root_early[:, :, P:], root_late[:, :, :P], root_late[:, :, P:]]

        def gain(t, acc, lo, n):
            nc.vector.tensor_scalar(gained[:, t, lo : lo + n], acc, 0.0, gn_sb[:, t : t + 1], ALU.max, ALU.mult)

        def square(t, lo, n):
            nc.scalar.activation(sq[t][:, lo : lo + n], gained[:, t, lo : lo + n], ACT.Square, scale=inverse[t])

        def fetch_p1(t, h):
            nc.scalar.activation(near[t][h][:], sq[t][:].indirect(entries(p1_sb, h * HALF, HALF)), ACT.Copy)

        def partial_of(t, h):
            return partial[:, t, h * HALF : (h + 1) * HALF] if t < LAST else partial_last[h]

        def add_own(t, h):
            nc.vector.tensor_tensor(partial_of(t, h), near[t][h][:], sq[t][:, h * HALF : (h + 1) * HALF], ALU.add)

        def fetch_p2(out, t, lo, n, so_far):
            nc.vector.tensor_tensor(out, sq[t][:].indirect(entries(p2_sb, lo, n)), so_far, ALU.add)

        def finish(t, h):
            fetch_p2(total[:, t, h * HALF : (h + 1) * HALF], t, h * HALF, HALF, partial_of(t, h))

        def take_root(out, sums, one=1.0):
            nc.scalar.activation(out, sums, ACT.Abs_reciprocal_sqrt, bias=one, scale=0.5)

        far_late = keep.tile([P, HALF], F32, name="far_late", align_bytes=64)

        def finish_last(c):
            columns = slice(c % 2 * P, (c % 2 + 1) * P)
            if c < 2:
                fetch_p2(total_last[:, columns], LAST, c * P, P, partial_last[0][:, columns])
            else:
                nc.vector.tensor_tensor(total_last[:, columns], partial_last[1][:, columns], far_late[:, columns], ALU.add)
            take_root(root[c][:, LAST, :], total_last[:, columns])

        for c in range(BLOCKS):
            acc = psum.tile([P, P], F32, name=f"acc0_{c}", offset=BANK * c)
            first_product(acc[:], 0, c * P, P, [0, 1])
            gain(0, acc[:], c * P, P)
            square(0, c * P, P)
        nc.vector.tensor_copy(own[:], sq[0][:, :HALF])
        halves = [psum.tile([P, HALF], F32, name=f"acc1_{h}", offset=BANK * h) for h in range(2)]
        for h in range(2):
            first_product(halves[h][:], 1, h * HALF, HALF, [1, 0])
        wholes = {t: psum.tile([P, S], F32, name=f"acc{t}", offset=BANK * (BLOCKS + t)) for t in (2, 3)}
        for t in (2, 3):
            first_product(wholes[t][:], t, 0, S, [1, 0])
        gain(1, halves[0][:], 0, HALF)
        fetch_p1(0, 0)
        fetch_p2(partial[:, 0, :HALF], 0, 0, HALF, own[:])
        gain(1, halves[1][:], HALF, HALF)
        fetch_p1(0, 1)
        nc.vector.tensor_tensor(total[:, 0, :HALF], partial[:, 0, :HALF], near[0][0][:], ALU.add)
        square(1, 0, S)
        gain(2, wholes[2][:], 0, S)
        add_own(0, 1)
        gain(3, wholes[3][:], 0, S)
        square(2, 0, S)
        finish(0, 1)
        for h in range(2):
            fetch_p1(1, h)
            add_own(1, h)
        square(3, 0, S)
        for h in range(2):
            finish(1, h)
        for h in range(2):
            fetch_p1(2, h)
            add_own(2, h)
        fetch_p1(3, 0)
        finish(2, 0)
        take_root(root_early[:, 0:2, :], total[:, 0:2, :HALF], bias[:])
        add_own(3, 0)
        fetch_p1(3, 1)
        nc.scalar.activation(far_late[:], sq[LAST][:].indirect(entries(p2_sb, HALF, HALF)), ACT.Copy)
        finish(2, 1)
        take_root(root_early[:, 2, :], total[:, 2, :HALF])
        for c in range(2):
            finish_last(c)
        add_own(3, 1)
        take_root(root_late[:, 0:LAST, :], total[:, :, HALF:])

        z_in = [keep.tile([P, P * PACK], BF16, name=f"z_in{c}", align_bytes=64) for c in range(BLOCKS)]
        z_words = [keep.tile([P, P], U32, name=f"z_words{c}", align_bytes=64) for c in range(BLOCKS)]
        z_scales = [keep.tile([P, P], U8, name=f"z_scales{c}", align_bytes=64) for c in range(BLOCKS)]

        def by_fours(tiles, run=4):
            return tiles.rearrange("p t (c i) -> p c t i", i=run)

        def interleaved(values, run=4):
            return values.rearrange("p (c i t) -> p c t i", i=run, t=PACK)

        def normalise(c, lo=0, n=P):
            nc.vector.tensor_tensor(
                interleaved(z_in[c][:, lo * PACK : (lo + n) * PACK], 2),
                by_fours(gained[:, :, c * P + lo : c * P + lo + n], 2),
                by_fours(root[c][:, :, lo : lo + n], 2),
                ALU.mult,
            )

        banks = [psum.tile([P, PACK, P], F32, name=f"out{c}", offset=BANK * c) for c in range(BLOCKS - 1)]
        last_banks = [psum.tile([P, 2, P], F32, name=f"out_last{u}", offset=BANK * (BLOCKS - 1 + u)) for u in range(2)]

        def second_product(c):
            nc.vector.quantize_mx(z_words[c][:].bitcast(FP8X4), z_scales[c][:], z_in[c][:])
            for t in range(PACK):
                nc.tensor.matmul_mx(
                    out=banks[c][:, t, :] if c < BLOCKS - 1 else last_banks[t // 2][:, t % 2, :],
                    lhsT=w2w[:, 2 * t * P : 2 * (t + 1) * P].bitcast(FP4X4),
                    lhsT_scale=w2s[:, t * P : (t + 1) * P],
                    rhs=z_words[c][:].bitcast(FP8X4),
                    rhs_scale=z_scales[c][:],
                    start=True,
                    stop=True,
                )

        res = [keep.tile([P, PACK, P], F32, name=f"res{c}") for c in range(BLOCKS)]
        rounded = keep.tile([P, S * PACK], BF16, name="rounded", align_bytes=64)
        out_words = keep.tile([P, S], U32, name="out_words", align_bytes=64)
        out_scales = keep.tile([P, S], U8, name="out_scales", align_bytes=64)
        out_rows = out_0.rearrange("(p t) j -> p t j", t=PACK)
        out_codes = out_1[0].rearrange("p n t -> p (n t)").bitcast(I32)

        def store_block(c):
            nc.sync.dma_start(out_rows[:, :, c * P : (c + 1) * P], res[c][:])

        def empty(c):
            nc.scalar.copy(res[c][:], banks[c][:])
            store_block(c)

        def round_on_vector(c, n=P):
            nc.vector.tensor_copy(interleaved(rounded[:, c * P * PACK : (c * P + n) * PACK]), by_fours(res[c][:, :, :n]))

        def round_on_scalar(c, source, lo=0):
            nc.scalar.copy(
                rounded[:, (c * P + lo) * PACK : (c + 1) * P * PACK].rearrange("p (j t) -> p j t", t=PACK),
                source[:, :, lo:].rearrange("p t j -> p j t"),
            )

        def quantise_result(lo, n):
            nc.vector.quantize_mx(out_words[:, lo : lo + n].bitcast(FP8X4), out_scales[:, lo : lo + n], rounded[:, lo * PACK : (lo + n) * PACK])

        def store_words(queue, lo):
            queue.dma_start(out_codes[:, lo : lo + HALF], out_words[:, lo : lo + HALF].bitcast(I32))

        normalise(0)
        finish_last(2)
        second_product(0)
        normalise(1)
        finish_last(3)
        second_product(1)
        empty(0)
        round_on_scalar(0, banks[0])
        normalise(2)
        normalise(3, 0, P // 2)
        second_product(2)
        normalise(3, P // 2, P // 2)
        second_product(3)
        quantise_result(0, P)

        empty(1)
        empty(2)
        round_on_vector(1)
        nc.vector.tensor_copy(res[3][:, 0:2, :], last_banks[0][:])
        nc.scalar.copy(res[3][:, 2:4, :], last_banks[1][:])
        store_block(3)
        round_on_vector(2)
        round_on_vector(3, P // 2)
        round_on_scalar(3, res[3], P // 2)
        quantise_result(P, P)
        store_words(nc.sync, 0)
        quantise_result(2 * P, P)
        quantise_result(3 * P, P)
        store_words(nc.scalar, HALF)
        for q in range(QUADRANTS):
            queue = nc.sync if q % 2 == 0 else nc.scalar
            queue.dma_start(out_2[0, 4 * q : 4 * q + 4, :].bitcast(I32), out_scales[32 * q : 32 * q + 4, :].bitcast(I32))
